import numpy as np
import ml_dtypes


def mxq(x, axis, fmt="e4m3"):
    dtype, down = {"e4m3": (ml_dtypes.float8_e4m3fn, 7), "e5m2": (ml_dtypes.float8_e5m2, 14)}[fmt]
    v = np.moveaxis(np.asarray(x, np.float32).astype(ml_dtypes.bfloat16).astype(np.float64), axis, -1)
    blocks = v.reshape(v.shape[:-1] + (-1, 32))
    amax = np.abs(blocks).max(-1, keepdims=True)
    byte = np.maximum(np.where(amax > 0, np.frexp(amax)[1] - 1 + 127, 0) - down, 1)
    scale = np.exp2(byte - 127.0)
    codes = (blocks / scale).astype(np.float32).astype(dtype).astype(np.float64)
    return np.moveaxis((codes * scale).reshape(v.shape), -1, axis)


WIDE = False


def mx_kscale(k):
    if not WIDE:
        return np.ones(k)
    levels = np.array([10, -10, 5, -5, 0])
    if k % 512:
        return np.exp2(np.random.permutation(np.resize(levels, k // 32))).repeat(32)
    a = np.empty((k // 512, 16))
    for p in range(k // 512):
        a[p, :8] = np.random.permutation(np.resize(levels, 8))
        for g in range(8):
            far = levels[np.abs(levels - a[p, g]) >= 10]
            a[p, g + 8] = far[np.random.randint(len(far))]
    return np.exp2(a.ravel()).repeat(32)


def f64(x):
    return np.asarray(x).astype(np.float64)


def striped(idx):
    return np.tile(idx.reshape(-1, 16).T, (8, 1)).astype(np.uint16)


def unstriped(offs):
    return offs[:16].T.reshape(-1).astype(np.int64)


E2M1 = np.array([0.0, 0.5, 1.0, 1.5, 2.0, 3.0, 4.0, 6.0, -0.0, -0.5, -1.0, -1.5, -2.0, -3.0, -4.0, -6.0])


def pack_weight(w, fmt):
    k, n = w.shape
    w = f64(np.asarray(w, np.float32).astype(ml_dtypes.bfloat16)).reshape(k // 32, 32, n)
    amax = np.abs(w).max(1)
    if fmt == "e4m3":
        byte = np.frexp(amax)[1] - 1 + 127 - 7
    else:
        mant, ex = np.frexp(amax / 6.0)
        byte = np.where(mant > 0.5, ex, ex - 1) + 127
    byte = np.clip(np.where(amax > 0, byte, 1), 1, 254)
    scaled = (w * np.exp2(127.0 - byte)[:, None, :]).reshape(k, n).astype(np.float32)
    by_word = np.ascontiguousarray(scaled.reshape(k // 512, 128, 4, n).transpose(0, 1, 3, 2))
    if fmt == "e4m3":
        words = by_word.astype(ml_dtypes.float8_e4m3fn).view(np.uint8)
    else:
        c = by_word.astype(ml_dtypes.float4_e2m1fn).view(np.uint8) & 0xF
        words = (c[..., 0::2] | (c[..., 1::2] << 4)).reshape(k // 512, 128, 2 * n)
    return np.ascontiguousarray(words), np.ascontiguousarray(byte.astype(np.uint8).reshape(k // 512, 16, n))


def unpack_weight(words, scales, fmt):
    g, _, n = scales.shape
    words = np.ascontiguousarray(words).reshape(g, 128, n, -1)
    if fmt == "e4m3":
        vals = words.view(ml_dtypes.float8_e4m3fn).astype(np.float64)
    else:
        nib = np.empty((g, 128, n, 4), np.uint8)
        nib[..., 0::2] = words & 0xF
        nib[..., 1::2] = words >> 4
        vals = E2M1[nib]
    vals = vals * np.repeat(np.exp2(scales.astype(np.float64) - 127.0), 8, axis=1)[..., None]
    return vals.transpose(0, 1, 3, 2).reshape(g * 512, n)


def gelu(v):
    return 0.5 * v * (1.0 + np.tanh(np.sqrt(2.0 / np.pi) * (v + 0.044715 * v**3)))


T, S, P, P2, K, H, N = 2048, 1024, 512, 256, 1024, 1536, 768


def setup_inputs():
    n = np.random.standard_normal
    s = mx_kscale(K)[:, None]
    u = mx_kscale(H)[:, None]
    tab_words, tab_scales = pack_weight(n((K, T)) * s, "e4m3")
    w4_words, w4_scales = pack_weight(n((K, H)) / np.sqrt(K) / s * u.T, "e2m1")
    return {
        "tab_words": tab_words,
        "tab_scales": tab_scales,
        "offs": striped(np.random.permutation(T)[:S]),
        "pos1": striped(np.random.permutation(S)[:P]),
        "pos2": striped(np.random.permutation(S)[:P]),
        "pos3": striped(np.random.permutation(P)[:P2]),
        "pos4": striped(np.random.permutation(P)[:P2]),
        "w4_words": w4_words,
        "w4_scales": w4_scales,
        "coef": (np.random.uniform(0.04, 0.12, H) / u[:, 0] ** 2).astype(np.float32),
        "w2": (n((H, N)) / np.sqrt(H) / u).astype(np.float32),
    }


def reference(tab_words, tab_scales, offs, pos1, pos2, pos3, pos4, w4_words, w4_scales, coef, w2):
    v = unpack_weight(tab_words, tab_scales, "e4m3")[:, unstriped(offs)]
    w4 = unpack_weight(w4_words, w4_scales, "e2m1")
    h = w4.T @ v
    x = h[:, unstriped(pos1)] + h[:, unstriped(pos2)]
    z = x + f64(coef)[:, None] * x ** 3
    y = mxq(f64(w2), 0, "e4m3").T @ mxq(z, 0, "e4m3")
    return np.minimum(y[:, unstriped(pos3)], y[:, unstriped(pos4)])

@@ -1,0 +1,224 @@
+from contextlib import ExitStack
+
+import concourse.mybir as mybir
+from concourse.masks import make_identity
+
+T, S, P1, P2, K, H, N = 2048, 1024, 512, 256, 1024, 1536, 768
+FLOPS = 2 * K * H * S + 2 * H * N * P1
+
+F32 = mybir.dt.float32
+BF16 = mybir.dt.bfloat16
+I32 = mybir.dt.int32
+U32 = mybir.dt.uint32
+U16 = mybir.dt.uint16
+U8 = mybir.dt.uint8
+FP8X4 = mybir.dt.float8_e4m3fn_x4
+FP4X4 = mybir.dt.float4_e2m1fn_x4
+ACT = mybir.ActivationFunctionType
+ALU = mybir.AluOpType
+
+P = 128
+PACK = 4
+K_PASS = P * PACK
+A_PASSES = K // K_PASS
+G_PASSES = H // K_PASS
+BANK = 512
+HALVES = S // BANK
+N_TILES = N // P
+BANKS = 8
+W2_CUTS = (0, 256, N)
+CAST_COLS = 256
+
+
+def tile_list_claim_charting_kernel(
+    tc, tab_words, tab_scales, offs, pos1, pos2, pos3, pos4, w4_words, w4_scales, coef, w2, out
+):
+    nc = tc.nc
+    with ExitStack() as ctx:
+        keep = ctx.enter_context(tc.tile_pool(name="keep", bufs=1))
+        ring = ctx.enter_context(tc.tile_pool(name="ring", bufs=2))
+        psum = ctx.enter_context(tc.psum_pool(name="psum", bufs=1))
+
+        def load_list(src, name):
+            tile = keep.tile(list(src.shape), U16, name=name)
+            nc.sync.dma_start(tile[:], src)
+            return tile
+
+        tab_plane = keep.tile([P, T], U8, align_bytes=64)
+        nc.vector.memset(tab_plane[:].bitcast(I32), 0)
+        v_plane1 = keep.tile([P, S], U8, align_bytes=64)
+        nc.vector.memset(v_plane1[:].bitcast(I32), 0)
+        w4_plane_raw = keep.tile([P, A_PASSES * H], U8, align_bytes=64)
+        nc.gpsimd.memset(w4_plane_raw[:].bitcast(I32), 0)
+
+        offs_t = load_list(offs, "offs_t")
+        for q in range(4):
+            nc.sync.dma_start(
+                tab_plane[32 * q : 32 * q + 4 * A_PASSES, :].bitcast(I32),
+                tab_scales[:, 4 * q : 4 * q + 4, :].bitcast(I32),
+            )
+        tab_w = [keep.tile([P, T], I32, name=f"tab_w{a}", align_bytes=64) for a in range(A_PASSES)]
+        w4_raw = [keep.tile([P, A_PASSES, K_PASS // 2], I32, name=f"w4_raw{g}") for g in range(G_PASSES)]
+
+        def load_tab(a):
+            nc.sync.dma_start(tab_w[a][:], tab_words[a].rearrange("p t i -> p (t i)").bitcast(I32))
+
+        def load_w4(g):
+            cols = slice(2 * K_PASS * g, 2 * K_PASS * (g + 1))
+            nc.sync.dma_start(w4_raw[g][:], w4_words[:, :, cols].rearrange("a p c -> p a c").bitcast(I32))
+
+        load_tab(0)
+        load_w4(0)
+        load_tab(1)
+        for q in range(4):
+            nc.gpsimd.dma_start(
+                w4_plane_raw[32 * q : 32 * q + 4, :].bitcast(I32).rearrange("r (a c) -> r a c", a=A_PASSES),
+                w4_scales[:, 4 * q : 4 * q + 4, :].bitcast(I32).rearrange("a r c -> r a c"),
+            )
+        pos1_t = load_list(pos1, "pos1_t")
+        pos2_t = load_list(pos2, "pos2_t")
+        for g in range(1, G_PASSES):
+            load_w4(g)
+        coef_rows = keep.tile([P, G_PASSES * P], F32)
+        nc.gpsimd.memset(coef_rows[:], 0.0)
+        nc.gpsimd.dma_start(
+            coef_rows[0:PACK, :].rearrange("t (b i) -> t b i", i=8),
+            coef.rearrange("(b t i) -> t b i", t=PACK, i=8),
+        )
+        ident = keep.tile([P, P], F32)
+        make_identity(nc, ident[:])
+        coef_turned = psum.tile([P, G_PASSES, P], F32, tag=f"bank{BANKS - 1}")
+        for g in range(G_PASSES):
+            nc.tensor.transpose(coef_turned[:, g, :], coef_rows[:, g * P : (g + 1) * P], ident[:])
+        coef_t = keep.tile([P, G_PASSES, PACK], F32)
+        nc.scalar.activation(coef_t[:], coef_turned[:, :, 0:PACK], ACT.Copy)
+
+        v_plane0 = keep.tile([P, S], U8, align_bytes=64)
+        nc.vector.tensor_copy(v_plane0[:], tab_plane[:].indirect(offs_t[:]))
+        for q in range(4):
+            nc.scalar.dma_start(
+                v_plane1[32 * q : 32 * q + 4, :].bitcast(I32),
+                v_plane0[32 * q + 4 : 32 * q + 8, :].bitcast(I32),
+            )
+        v_planes = [v_plane0, v_plane1]
+
+        w2_raw = [keep.tile([P, PACK, N], F32, name=f"w2_raw{g}") for g in range(G_PASSES)]
+        for g in range(G_PASSES):
+            rows = w2[K_PASS * g : K_PASS * (g + 1), :].rearrange("(q t i) n -> t q i n", t=PACK, i=8)
+            for t in range(PACK):
+                nc.sync.dma_start(w2_raw[g][:, t, :], rows[t])
+        pos3_t = load_list(pos3, "pos3_t")
+        pos4_t = load_list(pos4, "pos4_t")
+
+        v_w = {}
+
+        def gather_words(a, half):
+            v_w[a, half] = keep.tile([P, BANK], U32, name=f"v_w{a}_{half}", align_bytes=64)
+            cols = slice(half * BANK // 16, (half + 1) * BANK // 16)
+            nc.vector.tensor_copy(v_w[a, half][:], tab_w[a][:].bitcast(U32).indirect(offs_t[:, cols]))
+
+        w4_codes, w4_planes = {}, {}
+
+        def order_w4(g):
+            w4_codes[g] = keep.tile([P, A_PASSES * K_PASS * 2], U8, name=f"w4_codes{g}", align_bytes=64)
+            nc.vector.tensor_copy(
+                w4_codes[g][:].bitcast(I32).rearrange("p (a t q w) -> p a t q w", a=A_PASSES, t=PACK, w=4),
+                w4_raw[g][:].rearrange("p a (q t w) -> p a t q w", t=PACK, w=4),
+            )
+            w4_planes[g] = keep.tile([P, A_PASSES * K_PASS], U8, name=f"w4_plane{g}", align_bytes=64)
+            nc.vector.tensor_copy(
+                w4_planes[g][:].bitcast(I32).rearrange("p (a t q w) -> p a t q w", a=A_PASSES, t=PACK, w=2),
+                w4_plane_raw[:].bitcast(I32).rearrange("p (a g q t w) -> p g a t q w", a=A_PASSES, g=G_PASSES, t=PACK, w=2)[:, g],
+            )
+
+        for half in range(HALVES):
+            gather_words(0, half)
+        order_w4(0)
+        for half in range(HALVES):
+            gather_words(1, half)
+        for g in range(1, G_PASSES):
+            order_w4(g)
+
+        h = {}
+        for j in range(G_PASSES * PACK):
+            g, t = divmod(j, PACK)
+            h[j] = ring.tile([P, S], F32, name=f"h{j}", tag="rows", bufs=G_PASSES * PACK)
+            for half in range(HALVES):
+                bank = psum.tile([P, BANK], F32, name=f"hb{j}_{half}", tag=f"bank{(HALVES * j + half) % BANKS}")
+                for a in range(A_PASSES):
+                    col = (a * PACK + t) * P
+                    nc.tensor.matmul_mx(
+                        out=bank[:],
+                        lhsT=w4_codes[g][:, 2 * col : 2 * (col + P)].bitcast(FP4X4),
+                        lhsT_scale=w4_planes[g][:, col : col + P],
+                        rhs=v_w[a, half][:].bitcast(FP8X4),
+                        rhs_scale=v_planes[a][:, half * BANK : (half + 1) * BANK],
+                        start=(a == 0),
+                        stop=(a == A_PASSES - 1),
+                    )
+                nc.scalar.activation(h[j][:, half * BANK : (half + 1) * BANK], bank[:], ACT.Copy)
+
+        acc = [psum.tile([P, P1], F32, name=f"acc{n}", tag=f"bank{n}") for n in range(N_TILES)]
+
+        def quantise_w2(g, c0, c1):
+            width = c1 - c0
+            woven = ring.tile([P, width, PACK], BF16, name=f"w2_woven{g}_{c0}", tag=f"w2_woven{c0}", align_bytes=64)
+            for c in range(0, width, CAST_COLS):
+                nc.scalar.copy(
+                    woven[:, c : c + CAST_COLS, :].rearrange("p (c i) t -> p c t i", i=4),
+                    w2_raw[g][:, :, c0 + c : c0 + c + CAST_COLS].rearrange("p t (c i) -> p c t i", i=4),
+                )
+            codes = keep.tile([P, width], U32, name=f"w2_codes{g}_{c0}", align_bytes=64)
+            plane = keep.tile([P, width], U8, name=f"w2_plane{g}_{c0}", align_bytes=64)
+            nc.vector.quantize_mx(out=codes[:].bitcast(FP8X4), scales=plane[:], in_=woven[:].rearrange("p c t -> p (c t)"))
+            return codes, plane
+
+        for g in range(G_PASSES):
+            x = keep.tile([P, PACK, P1], F32, name=f"x{g}")
+            u = ring.tile([P, PACK, P1], F32, name=f"u{g}", tag="u")
+            for t in range(PACK):
+                j = g * PACK + t
+                first = ring.tile([P, P1], F32, name=f"first{j}", tag="first", bufs=4)
+                nc.vector.tensor_copy(first[:], h[j][:].indirect(pos1_t[:]))
+                nc.vector.tensor_tensor(x[:, t, :], h[j][:].indirect(pos2_t[:]), first[:], ALU.add)
+                sq = ring.tile([P, P1], F32, name=f"sq{j}", tag="sq")
+                nc.scalar.activation(sq[:], x[:, t, :], ACT.Square)
+                nc.scalar.activation(u[:, t, :], sq[:], ACT.Identity, bias=1.0, scale=coef_t[:, g, t : t + 1])
+            z = ring.tile([P, P1, PACK], BF16, name=f"z{g}", tag="z", align_bytes=64)
+            z_codes = keep.tile([P, P1], U32, name=f"z_codes{g}", align_bytes=64)
+            z_plane = keep.tile([P, P1], U8, name=f"z_plane{g}", align_bytes=64)
+            halves = [slice(0, P1 // 2), slice(P1 // 2, P1)]
+            for m in halves:
+                nc.vector.tensor_tensor(
+                    z[:, m, :].rearrange("p (c i) t -> p c t i", i=4),
+                    u[:, :, m].rearrange("p t (c i) -> p c t i", i=4),
+                    x[:, :, m].rearrange("p t (c i) -> p c t i", i=4),
+                    ALU.mult,
+                )
+            for m in halves:
+                nc.vector.quantize_mx(
+                    out=z_codes[:, m].bitcast(FP8X4), scales=z_plane[:, m], in_=z[:, m, :].rearrange("p c t -> p (c t)")
+                )
+            for c0, c1 in zip(W2_CUTS[:-1], W2_CUTS[1:]):
+                codes, plane = quantise_w2(g, c0, c1)
+                for n in range(c0 // P, c1 // P):
+                    cols = slice(n * P - c0, (n + 1) * P - c0)
+                    nc.tensor.matmul_mx(
+                        out=acc[n][:],
+                        lhsT=codes[:, cols].bitcast(FP8X4),
+                        lhsT_scale=plane[:, cols],
+                        rhs=z_codes[:].bitcast(FP8X4),
+                        rhs_scale=z_plane[:],
+                        start=(g == 0),
+                        stop=(g == G_PASSES - 1),
+                    )
+
+        for n in range(N_TILES):
+            y = ring.tile([P, P1], F32, name=f"y{n}", tag="rows", bufs=G_PASSES * PACK)
+            nc.scalar.activation(y[:], acc[n][:], ACT.Copy)
+            rivals = ring.tile([P, 2, P2], F32, name=f"rivals{n}", tag="first", bufs=4)
+            nc.vector.tensor_copy(rivals[:, 0, :], y[:].indirect(pos3_t[:]))
+            nc.vector.tensor_copy(rivals[:, 1, :], y[:].indirect(pos4_t[:]))
+            least = keep.tile([P, P2], F32, name=f"least{n}")
+            nc.vector.tensor_tensor(least[:], rivals[:, 0, :], rivals[:, 1, :], ALU.min)
+            nc.sync.dma_start(out[n * P : (n + 1) * P, :], least[:])

@@ -28,6 +28,7 @@ N_TILES = N // P
 BANKS = 8
 W2_CUTS = (0, 256, N)
 CAST_COLS = 256
+LAST_PIECE = 64
 
 
 def tile_list_claim_charting_kernel(
@@ -44,41 +45,51 @@ def tile_list_claim_charting_kernel(
             nc.sync.dma_start(tile[:], src)
             return tile
 
+        rows0 = P - A_PASSES * 16
         tab_plane = keep.tile([P, T], U8, align_bytes=64)
-        nc.vector.memset(tab_plane[:].bitcast(I32), 0)
-        v_plane1 = keep.tile([P, S], U8, align_bytes=64)
-        nc.vector.memset(v_plane1[:].bitcast(I32), 0)
+        nc.vector.memset(tab_plane[0:rows0, :].bitcast(I32), 0)
+        v_planes = keep.tile([P, A_PASSES * S], U8, align_bytes=64)
+        nc.vector.memset(v_planes[:].bitcast(I32), 0)
         w4_plane_raw = keep.tile([P, A_PASSES * H], U8, align_bytes=64)
         nc.gpsimd.memset(w4_plane_raw[:].bitcast(I32), 0)
 
         offs_t = load_list(offs, "offs_t")
-        for q in range(4):
-            nc.sync.dma_start(
-                tab_plane[32 * q : 32 * q + 4 * A_PASSES, :].bitcast(I32),
-                tab_scales[:, 4 * q : 4 * q + 4, :].bitcast(I32),
-            )
-        tab_w = [keep.tile([P, T], I32, name=f"tab_w{a}", align_bytes=64) for a in range(A_PASSES)]
-        w4_raw = [keep.tile([P, A_PASSES, K_PASS // 2], I32, name=f"w4_raw{g}") for g in range(G_PASSES)]
+        nc.sync.dma_start(tab_plane[rows0:P, :].bitcast(I32), tab_scales.rearrange("a q t -> (a q) t").bitcast(I32))
+        tab_w = [keep.tile([P, T], I32, name=f"tab_w{a}", tag=f"stage{a}", align_bytes=64) for a in range(A_PASSES)]
 
         def load_tab(a):
             nc.sync.dma_start(tab_w[a][:], tab_words[a].rearrange("p t i -> p (t i)").bitcast(I32))
 
-        def load_w4(g):
-            cols = slice(2 * K_PASS * g, 2 * K_PASS * (g + 1))
-            nc.sync.dma_start(w4_raw[g][:], w4_words[:, :, cols].rearrange("a p c -> p a c").bitcast(I32))
+        def load_w4(g0, g1, **place):
+            raw = keep.tile([P, A_PASSES, (g1 - g0) * K_PASS // 2], I32, name=f"w4_raw{g0}", align_bytes=64, **place)
+            cols = slice(2 * K_PASS * g0, 2 * K_PASS * g1)
+            nc.sync.dma_start(raw[:], w4_words[:, :, cols].rearrange("a p c -> p a c").bitcast(I32))
+            return [raw[:, :, (g - g0) * K_PASS // 2 : (g - g0 + 1) * K_PASS // 2] for g in range(g0, g1)]
 
         load_tab(0)
-        load_w4(0)
+        pos1_t = load_list(pos1, "pos1_t")
+        pos2_t = load_list(pos2, "pos2_t")
+        pos3_t = load_list(pos3, "pos3_t")
+        pos4_t = load_list(pos4, "pos4_t")
+        w4_raw = load_w4(0, 1)
         load_tab(1)
         for q in range(4):
             nc.gpsimd.dma_start(
                 w4_plane_raw[32 * q : 32 * q + 4, :].bitcast(I32).rearrange("r (a c) -> r a c", a=A_PASSES),
                 w4_scales[:, 4 * q : 4 * q + 4, :].bitcast(I32).rearrange("a r c -> r a c"),
             )
-        pos1_t = load_list(pos1, "pos1_t")
-        pos2_t = load_list(pos2, "pos2_t")
-        for g in range(1, G_PASSES):
-            load_w4(g)
+
+        v_rows = keep.tile([P, S], U8, align_bytes=64)
+        nc.vector.tensor_copy(v_rows[:], tab_plane[:].indirect(offs_t[:]))
+        for q in range(4):
+            queue = nc.gpsimd if q == 3 else nc.scalar
+            for a in range(A_PASSES):
+                row = rows0 + 16 * a + 4 * q
+                queue.dma_start(
+                    v_planes[32 * q : 32 * q + 4, a * S : (a + 1) * S].bitcast(I32),
+                    v_rows[row : row + 4, :].bitcast(I32),
+                )
+
         coef_rows = keep.tile([P, G_PASSES * P], F32)
         nc.gpsimd.memset(coef_rows[:], 0.0)
         nc.gpsimd.dma_start(
@@ -87,28 +98,14 @@ def tile_list_claim_charting_kernel(
         )
         ident = keep.tile([P, P], F32)
         make_identity(nc, ident[:])
-        coef_turned = psum.tile([P, G_PASSES, P], F32, tag=f"bank{BANKS - 1}")
-        for g in range(G_PASSES):
-            nc.tensor.transpose(coef_turned[:, g, :], coef_rows[:, g * P : (g + 1) * P], ident[:])
-        coef_t = keep.tile([P, G_PASSES, PACK], F32)
-        nc.scalar.activation(coef_t[:], coef_turned[:, :, 0:PACK], ACT.Copy)
 
-        v_plane0 = keep.tile([P, S], U8, align_bytes=64)
-        nc.vector.tensor_copy(v_plane0[:], tab_plane[:].indirect(offs_t[:]))
-        for q in range(4):
-            nc.scalar.dma_start(
-                v_plane1[32 * q : 32 * q + 4, :].bitcast(I32),
-                v_plane0[32 * q + 4 : 32 * q + 8, :].bitcast(I32),
-            )
-        v_planes = [v_plane0, v_plane1]
+        w2_raw = {}
 
-        w2_raw = [keep.tile([P, PACK, N], F32, name=f"w2_raw{g}") for g in range(G_PASSES)]
-        for g in range(G_PASSES):
+        def load_w2(g):
+            w2_raw[g] = keep.tile([P, PACK, N], F32, name=f"w2_raw{g}", tag=f"stage{(g + 1) % 2}", align_bytes=64)
             rows = w2[K_PASS * g : K_PASS * (g + 1), :].rearrange("(q t i) n -> t q i n", t=PACK, i=8)
             for t in range(PACK):
                 nc.sync.dma_start(w2_raw[g][:, t, :], rows[t])
-        pos3_t = load_list(pos3, "pos3_t")
-        pos4_t = load_list(pos4, "pos4_t")
 
         v_w = {}
 
@@ -123,7 +120,7 @@ def tile_list_claim_charting_kernel(
             w4_codes[g] = keep.tile([P, A_PASSES * K_PASS * 2], U8, name=f"w4_codes{g}", align_bytes=64)
             nc.vector.tensor_copy(
                 w4_codes[g][:].bitcast(I32).rearrange("p (a t q w) -> p a t q w", a=A_PASSES, t=PACK, w=4),
-                w4_raw[g][:].rearrange("p a (q t w) -> p a t q w", t=PACK, w=4),
+                w4_raw[g].rearrange("p a (q t w) -> p a t q w", t=PACK, w=4),
             )
             w4_planes[g] = keep.tile([P, A_PASSES * K_PASS], U8, name=f"w4_plane{g}", align_bytes=64)
             nc.vector.tensor_copy(
@@ -133,36 +130,60 @@ def tile_list_claim_charting_kernel(
 
         for half in range(HALVES):
             gather_words(0, half)
+        w4_raw.extend(load_w4(1, G_PASSES, tag="stage0"))
         order_w4(0)
         for half in range(HALVES):
             gather_words(1, half)
+        load_w2(0)
         for g in range(1, G_PASSES):
             order_w4(g)
+        load_w2(1)
 
         h = {}
-        for j in range(G_PASSES * PACK):
+        banks = {}
+
+        def multiply_first(j, half):
             g, t = divmod(j, PACK)
-            h[j] = ring.tile([P, S], F32, name=f"h{j}", tag="rows", bufs=G_PASSES * PACK)
-            for half in range(HALVES):
-                bank = psum.tile([P, BANK], F32, name=f"hb{j}_{half}", tag=f"bank{(HALVES * j + half) % BANKS}")
-                for a in range(A_PASSES):
-                    col = (a * PACK + t) * P
-                    nc.tensor.matmul_mx(
-                        out=bank[:],
-                        lhsT=w4_codes[g][:, 2 * col : 2 * (col + P)].bitcast(FP4X4),
-                        lhsT_scale=w4_planes[g][:, col : col + P],
-                        rhs=v_w[a, half][:].bitcast(FP8X4),
-                        rhs_scale=v_planes[a][:, half * BANK : (half + 1) * BANK],
-                        start=(a == 0),
-                        stop=(a == A_PASSES - 1),
-                    )
-                nc.scalar.activation(h[j][:, half * BANK : (half + 1) * BANK], bank[:], ACT.Copy)
+            banks[j, half] = psum.tile([P, BANK], F32, name=f"hb{j}_{half}", tag=f"bank{len(banks) % BANKS}")
+            for a in range(A_PASSES):
+                col = (a * PACK + t) * P
+                nc.tensor.matmul_mx(
+                    out=banks[j, half][:],
+                    lhsT=w4_codes[g][:, 2 * col : 2 * (col + P)].bitcast(FP4X4),
+                    lhsT_scale=w4_planes[g][:, col : col + P],
+                    rhs=v_w[a, half][:].bitcast(FP8X4),
+                    rhs_scale=v_planes[:, a * S + half * BANK : a * S + (half + 1) * BANK],
+                    start=(a == 0),
+                    stop=(a == A_PASSES - 1),
+                )
+
+        def empty_first(j, c0, c1):
+            half = c0 // BANK
+            nc.scalar.activation(h[j][:, c0:c1], banks[j, half][:, c0 - half * BANK : c1 - half * BANK], ACT.Copy)
+
+        last = G_PASSES * PACK - 1
+        batches = [[0]] + [[j, j + 1] for j in range(1, last, 2)] + [[last]]
+        for batch in batches:
+            cuts = (0, BANK, S) if len(batch) == 1 else (0, BANK, S - LAST_PIECE, S)
+            for j in batch:
+                h[j] = ring.tile([P, S], F32, name=f"h{j}", tag="rows", bufs=G_PASSES * PACK)
+            for c0, c1 in zip(cuts[:-1], cuts[1:]):
+                for j in batch:
+                    if c0 % BANK == 0:
+                        multiply_first(j, c0 // BANK)
+                    empty_first(j, c0, c1)
+
+        coef_turned = psum.tile([P, G_PASSES, P], F32, tag=f"bank{BANKS - 1}")
+        for g in range(G_PASSES):
+            nc.tensor.transpose(coef_turned[:, g, :], coef_rows[:, g * P : (g + 1) * P], ident[:])
+        coef_t = keep.tile([P, G_PASSES, PACK], F32)
+        nc.scalar.activation(coef_t[:], coef_turned[:, :, 0:PACK], ACT.Copy)
 
         acc = [psum.tile([P, P1], F32, name=f"acc{n}", tag=f"bank{n}") for n in range(N_TILES)]
 
         def quantise_w2(g, c0, c1):
             width = c1 - c0
-            woven = ring.tile([P, width, PACK], BF16, name=f"w2_woven{g}_{c0}", tag=f"w2_woven{c0}", align_bytes=64)
+            woven = ring.tile([P, width, PACK], BF16, name=f"w2_woven{g}_{c0}", tag=f"w2_woven{c0}", bufs=G_PASSES, align_bytes=64)
             for c in range(0, width, CAST_COLS):
                 nc.scalar.copy(
                     woven[:, c : c + CAST_COLS, :].rearrange("p (c i) t -> p c t i", i=4),
@@ -175,7 +196,7 @@ def tile_list_claim_charting_kernel(
 
         for g in range(G_PASSES):
             x = keep.tile([P, PACK, P1], F32, name=f"x{g}")
-            u = ring.tile([P, PACK, P1], F32, name=f"u{g}", tag="u")
+            u = ring.tile([P, PACK, P1], F32, name=f"u{g}", tag="u", bufs=G_PASSES)
             for t in range(PACK):
                 j = g * PACK + t
                 first = ring.tile([P, P1], F32, name=f"first{j}", tag="first", bufs=4)
@@ -212,6 +233,8 @@ def tile_list_claim_charting_kernel(
                         start=(g == 0),
                         stop=(g == G_PASSES - 1),
                     )
+            if g + 2 < G_PASSES:
+                load_w2(g + 2)
 
         for n in range(N_TILES):
             y = ring.tile([P, P1], F32, name=f"y{n}", tag="rows", bufs=G_PASSES * PACK)

@@ -46,10 +46,11 @@ def tile_list_claim_charting_kernel(
             return tile
 
         rows0 = P - A_PASSES * 16
-        tab_plane = keep.tile([P, T], U8, align_bytes=64)
+        tab_plane = keep.tile([P, T], U8, tag="early", align_bytes=64)
         nc.vector.memset(tab_plane[0:rows0, :].bitcast(I32), 0)
-        v_planes = keep.tile([P, A_PASSES * S], U8, align_bytes=64)
-        nc.vector.memset(v_planes[:].bitcast(I32), 0)
+        v_planes = [keep.tile([P, S], U8, name=f"v_plane{a}", align_bytes=64) for a in range(A_PASSES)]
+        for plane in v_planes:
+            nc.vector.memset(plane[:].bitcast(I32), 0)
         w4_plane_raw = keep.tile([P, A_PASSES * H], U8, align_bytes=64)
         nc.gpsimd.memset(w4_plane_raw[:].bitcast(I32), 0)
 
@@ -79,24 +80,24 @@ def tile_list_claim_charting_kernel(
                 w4_scales[:, 4 * q : 4 * q + 4, :].bitcast(I32).rearrange("a r c -> r a c"),
             )
 
-        v_rows = keep.tile([P, S], U8, align_bytes=64)
+        v_rows = keep.tile([P, S], U8, tag="rows_then_identity", align_bytes=64)
         nc.vector.tensor_copy(v_rows[:], tab_plane[:].indirect(offs_t[:]))
-        for q in range(4):
-            queue = nc.gpsimd if q == 3 else nc.scalar
-            for a in range(A_PASSES):
+        for a in range(A_PASSES):
+            for q in range(4):
+                queue = nc.gpsimd if (q, a) == (3, A_PASSES - 1) else nc.sync
                 row = rows0 + 16 * a + 4 * q
                 queue.dma_start(
-                    v_planes[32 * q : 32 * q + 4, a * S : (a + 1) * S].bitcast(I32),
+                    v_planes[a][32 * q : 32 * q + 4, :].bitcast(I32),
                     v_rows[row : row + 4, :].bitcast(I32),
                 )
 
-        coef_rows = keep.tile([P, G_PASSES * P], F32)
+        coef_rows = keep.tile([P, G_PASSES * P], F32, tag="early", align_bytes=64)
         nc.gpsimd.memset(coef_rows[:], 0.0)
         nc.gpsimd.dma_start(
             coef_rows[0:PACK, :].rearrange("t (b i) -> t b i", i=8),
             coef.rearrange("(b t i) -> t b i", t=PACK, i=8),
         )
-        ident = keep.tile([P, P], F32)
+        ident = keep.tile([P, P], F32, tag="rows_then_identity", align_bytes=64)
         make_identity(nc, ident[:])
 
         w2_raw = {}
@@ -152,7 +153,7 @@ def tile_list_claim_charting_kernel(
                     lhsT=w4_codes[g][:, 2 * col : 2 * (col + P)].bitcast(FP4X4),
                     lhsT_scale=w4_planes[g][:, col : col + P],
                     rhs=v_w[a, half][:].bitcast(FP8X4),
-                    rhs_scale=v_planes[:, a * S + half * BANK : a * S + (half + 1) * BANK],
+                    rhs_scale=v_planes[a][:, half * BANK : (half + 1) * BANK],
                     start=(a == 0),
                     stop=(a == A_PASSES - 1),
                 )
@@ -161,9 +162,15 @@ def tile_list_claim_charting_kernel(
             half = c0 // BANK
             nc.scalar.activation(h[j][:, c0:c1], banks[j, half][:, c0 - half * BANK : c1 - half * BANK], ACT.Copy)
 
-        last = G_PASSES * PACK - 1
-        batches = [[0]] + [[j, j + 1] for j in range(1, last, 2)] + [[last]]
-        for batch in batches:
+        coef_t = keep.tile([P, G_PASSES, PACK], F32)
+
+        def turn_coef():
+            banks["coef"] = psum.tile([P, G_PASSES, P], F32, name="coef_turned", tag=f"bank{len(banks) % BANKS}")
+            for g in range(G_PASSES):
+                nc.tensor.transpose(banks["coef"][:, g, :], coef_rows[:, g * P : (g + 1) * P], ident[:])
+            nc.scalar.activation(coef_t[:], banks["coef"][:, :, 0:PACK], ACT.Copy)
+
+        def first_product(batch):
             cuts = (0, BANK, S) if len(batch) == 1 else (0, BANK, S - LAST_PIECE, S)
             for j in batch:
                 h[j] = ring.tile([P, S], F32, name=f"h{j}", tag="rows", bufs=G_PASSES * PACK)
@@ -173,73 +180,109 @@ def tile_list_claim_charting_kernel(
                         multiply_first(j, c0 // BANK)
                     empty_first(j, c0, c1)
 
-        coef_turned = psum.tile([P, G_PASSES, P], F32, tag=f"bank{BANKS - 1}")
-        for g in range(G_PASSES):
-            nc.tensor.transpose(coef_turned[:, g, :], coef_rows[:, g * P : (g + 1) * P], ident[:])
-        coef_t = keep.tile([P, G_PASSES, PACK], F32)
-        nc.scalar.activation(coef_t[:], coef_turned[:, :, 0:PACK], ACT.Copy)
+        x = [keep.tile([P, PACK, P1], F32, name=f"x{g}") for g in range(G_PASSES)]
+        u = [keep.tile([P, PACK, P1], F32, name=f"u{g}") for g in range(G_PASSES)]
 
-        acc = [psum.tile([P, P1], F32, name=f"acc{n}", tag=f"bank{n}") for n in range(N_TILES)]
+        def pair_up(batch):
+            first = {}
+            for j in batch:
+                place = dict(tag=f"turn{j}", bufs=1) if j % 2 == 0 else dict(tag="first", bufs=4)
+                first[j] = ring.tile([P, P1], F32, name=f"first{j}", align_bytes=64, **place)
+                nc.vector.tensor_copy(first[j][:], h[j][:].indirect(pos1_t[:]))
+            for j in batch:
+                g, t = divmod(j, PACK)
+                nc.vector.tensor_tensor(x[g][:, t, :], h[j][:].indirect(pos2_t[:]), first[j][:], ALU.add)
 
-        def quantise_w2(g, c0, c1):
+        def factor(j):
+            g, t = divmod(j, PACK)
+            sq = ring.tile([P, P1], F32, name=f"sq{j}", tag="sq")
+            nc.scalar.activation(sq[:], x[g][:, t, :], ACT.Square)
+            nc.scalar.activation(u[g][:, t, :], sq[:], ACT.Identity, bias=1.0, scale=coef_t[:, g, t : t + 1])
+
+        def woven(view):
+            return view.rearrange("p (c i) t -> p c t i", i=4)
+
+        def planar(view):
+            return view.rearrange("p t (c i) -> p c t i", i=4)
+
+        w2_parts = {g: [] for g in range(G_PASSES)}
+
+        def quantise_w2(g, c0, c1, after=None):
             width = c1 - c0
-            woven = ring.tile([P, width, PACK], BF16, name=f"w2_woven{g}_{c0}", tag=f"w2_woven{c0}", bufs=G_PASSES, align_bytes=64)
-            for c in range(0, width, CAST_COLS):
-                nc.scalar.copy(
-                    woven[:, c : c + CAST_COLS, :].rearrange("p (c i) t -> p c t i", i=4),
-                    w2_raw[g][:, :, c0 + c : c0 + c + CAST_COLS].rearrange("p t (c i) -> p c t i", i=4),
-                )
+            if after is None:
+                rounded = keep.tile([P, width, PACK], BF16, name=f"w2_woven{g}_{c0}", align_bytes=64)
+                for c in range(0, width, CAST_COLS):
+                    nc.scalar.copy(
+                        woven(rounded[:, c : c + CAST_COLS, :]), planar(w2_raw[g][:, :, c0 + c : c0 + c + CAST_COLS])
+                    )
+            else:
+                rounded = ring.tile([P, width, PACK], BF16, name=f"w2_woven{g}_{c0}", tag=f"turn{after}", bufs=1, align_bytes=64)
+                nc.gpsimd.tensor_scalar(woven(rounded[:]), planar(w2_raw[g][:, :, c0:c1]), 1.0, 0.0, ALU.mult, ALU.add)
             codes = keep.tile([P, width], U32, name=f"w2_codes{g}_{c0}", align_bytes=64)
             plane = keep.tile([P, width], U8, name=f"w2_plane{g}_{c0}", align_bytes=64)
-            nc.vector.quantize_mx(out=codes[:].bitcast(FP8X4), scales=plane[:], in_=woven[:].rearrange("p c t -> p (c t)"))
-            return codes, plane
+            nc.vector.quantize_mx(out=codes[:].bitcast(FP8X4), scales=plane[:], in_=rounded[:].rearrange("p c t -> p (c t)"))
+            w2_parts[g].append((c0, c1, codes, plane))
 
-        for g in range(G_PASSES):
-            x = keep.tile([P, PACK, P1], F32, name=f"x{g}")
-            u = ring.tile([P, PACK, P1], F32, name=f"u{g}", tag="u", bufs=G_PASSES)
-            for t in range(PACK):
-                j = g * PACK + t
-                first = ring.tile([P, P1], F32, name=f"first{j}", tag="first", bufs=4)
-                nc.vector.tensor_copy(first[:], h[j][:].indirect(pos1_t[:]))
-                nc.vector.tensor_tensor(x[:, t, :], h[j][:].indirect(pos2_t[:]), first[:], ALU.add)
-                sq = ring.tile([P, P1], F32, name=f"sq{j}", tag="sq")
-                nc.scalar.activation(sq[:], x[:, t, :], ACT.Square)
-                nc.scalar.activation(u[:, t, :], sq[:], ACT.Identity, bias=1.0, scale=coef_t[:, g, t : t + 1])
-            z = ring.tile([P, P1, PACK], BF16, name=f"z{g}", tag="z", align_bytes=64)
-            z_codes = keep.tile([P, P1], U32, name=f"z_codes{g}", align_bytes=64)
-            z_plane = keep.tile([P, P1], U8, name=f"z_plane{g}", align_bytes=64)
-            halves = [slice(0, P1 // 2), slice(P1 // 2, P1)]
-            for m in halves:
-                nc.vector.tensor_tensor(
-                    z[:, m, :].rearrange("p (c i) t -> p c t i", i=4),
-                    u[:, :, m].rearrange("p t (c i) -> p c t i", i=4),
-                    x[:, :, m].rearrange("p t (c i) -> p c t i", i=4),
-                    ALU.mult,
-                )
-            for m in halves:
+        z_codes = [keep.tile([P, P1], U32, name=f"z_codes{g}", align_bytes=64) for g in range(G_PASSES)]
+        z_plane = [keep.tile([P, P1], U8, name=f"z_plane{g}", align_bytes=64) for g in range(G_PASSES)]
+
+        def quantise_z(g, afters=(None, None)):
+            z = {}
+            for half, after in enumerate(afters):
+                m = slice(half * P1 // 2, (half + 1) * P1 // 2)
+                place = dict(tag="z", bufs=4) if after is None else dict(tag=f"turn{after}", bufs=1)
+                z[half] = ring.tile([P, P1 // 2, PACK], BF16, name=f"z{g}_{half}", align_bytes=64, **place)
+                engine = nc.vector if after is None else nc.gpsimd
+                engine.tensor_tensor(woven(z[half][:]), planar(u[g][:, :, m]), planar(x[g][:, :, m]), ALU.mult)
+            for half in z:
+                m = slice(half * P1 // 2, (half + 1) * P1 // 2)
                 nc.vector.quantize_mx(
-                    out=z_codes[:, m].bitcast(FP8X4), scales=z_plane[:, m], in_=z[:, m, :].rearrange("p c t -> p (c t)")
+                    out=z_codes[g][:, m].bitcast(FP8X4), scales=z_plane[g][:, m], in_=z[half][:].rearrange("p c t -> p (c t)")
                 )
-            for c0, c1 in zip(W2_CUTS[:-1], W2_CUTS[1:]):
-                codes, plane = quantise_w2(g, c0, c1)
+
+        def second_product(g, acc):
+            for c0, c1, codes, plane in w2_parts[g]:
                 for n in range(c0 // P, c1 // P):
                     cols = slice(n * P - c0, (n + 1) * P - c0)
                     nc.tensor.matmul_mx(
                         out=acc[n][:],
                         lhsT=codes[:, cols].bitcast(FP8X4),
                         lhsT_scale=plane[:, cols],
-                        rhs=z_codes[:].bitcast(FP8X4),
-                        rhs_scale=z_plane[:],
+                        rhs=z_codes[g][:].bitcast(FP8X4),
+                        rhs_scale=z_plane[g][:],
                         start=(g == 0),
                         stop=(g == G_PASSES - 1),
                     )
-            if g + 2 < G_PASSES:
-                load_w2(g + 2)
+
+        last = G_PASSES * PACK - 1
+        batches = [[0]] + [[j, j + 1] for j in range(1, last, 2)] + [[last]]
+        factors_behind = {3: [0, 1, 2], 4: [3], 5: [4, 5, 6], 6: [7]}
+        for k, batch in enumerate(batches):
+            first_product(batch)
+            pair_up(batch)
+            if k < 3:
+                quantise_w2(0, k * CAST_COLS, (k + 1) * CAST_COLS, after=batch[-1])
+            if k == 2:
+                turn_coef()
+            for j in factors_behind.get(k, []):
+                factor(j)
+        load_w2(2)
+        acc = [psum.tile([P, P1], F32, name=f"acc{n}", tag=f"bank{n}") for n in range(N_TILES)]
+        quantise_z(0, afters=(6, 8))
+        second_product(0, acc)
+        for g in range(1, G_PASSES):
+            if g == G_PASSES - 1:
+                for t in range(PACK):
+                    factor(g * PACK + t)
+            quantise_z(g)
+            for c0, c1 in zip(W2_CUTS[:-1], W2_CUTS[1:]):
+                quantise_w2(g, c0, c1)
+            second_product(g, acc)
 
         for n in range(N_TILES):
             y = ring.tile([P, P1], F32, name=f"y{n}", tag="rows", bufs=G_PASSES * PACK)
             nc.scalar.activation(y[:], acc[n][:], ACT.Copy)
-            rivals = ring.tile([P, 2, P2], F32, name=f"rivals{n}", tag="first", bufs=4)
+            rivals = ring.tile([P, 2, P2], F32, name=f"rivals{n}", tag="first", bufs=4, align_bytes=64)
             nc.vector.tensor_copy(rivals[:, 0, :], y[:].indirect(pos3_t[:]))
             nc.vector.tensor_copy(rivals[:, 1, :], y[:].indirect(pos4_t[:]))
             least = keep.tile([P, P2], F32, name=f"least{n}")

@@ -186,8 +186,7 @@ def tile_list_claim_charting_kernel(
         def pair_up(batch):
             first = {}
             for j in batch:
-                place = dict(tag=f"turn{j}", bufs=1) if j % 2 == 0 else dict(tag="first", bufs=4)
-                first[j] = ring.tile([P, P1], F32, name=f"first{j}", align_bytes=64, **place)
+                first[j] = ring.tile([P, P1], F32, name=f"first{j}", tag="first", bufs=4, align_bytes=64)
                 nc.vector.tensor_copy(first[j][:], h[j][:].indirect(pos1_t[:]))
             for j in batch:
                 g, t = divmod(j, PACK)
@@ -207,17 +206,12 @@ def tile_list_claim_charting_kernel(
 
         w2_parts = {g: [] for g in range(G_PASSES)}
 
-        def quantise_w2(g, c0, c1, after=None):
+        def quantise_w2(g, c0, c1):
             width = c1 - c0
-            if after is None:
-                rounded = keep.tile([P, width, PACK], BF16, name=f"w2_woven{g}_{c0}", align_bytes=64)
-                for c in range(0, width, CAST_COLS):
-                    nc.scalar.copy(
-                        woven(rounded[:, c : c + CAST_COLS, :]), planar(w2_raw[g][:, :, c0 + c : c0 + c + CAST_COLS])
-                    )
-            else:
-                rounded = ring.tile([P, width, PACK], BF16, name=f"w2_woven{g}_{c0}", tag=f"turn{after}", bufs=1, align_bytes=64)
-                nc.gpsimd.tensor_scalar(woven(rounded[:]), planar(w2_raw[g][:, :, c0:c1]), 1.0, 0.0, ALU.mult, ALU.add)
+            rounded = keep.tile([P, width, PACK], BF16, name=f"w2_woven{g}_{c0}", align_bytes=64)
+            for c in range(0, width, CAST_COLS):
+                copy = nc.vector.tensor_copy if (g, c0 + c) == (G_PASSES - 1, N - CAST_COLS) else nc.scalar.copy
+                copy(woven(rounded[:, c : c + CAST_COLS, :]), planar(w2_raw[g][:, :, c0 + c : c0 + c + CAST_COLS]))
             codes = keep.tile([P, width], U32, name=f"w2_codes{g}_{c0}", align_bytes=64)
             plane = keep.tile([P, width], U8, name=f"w2_plane{g}_{c0}", align_bytes=64)
             nc.vector.quantize_mx(out=codes[:].bitcast(FP8X4), scales=plane[:], in_=rounded[:].rearrange("p c t -> p (c t)"))
@@ -226,18 +220,14 @@ def tile_list_claim_charting_kernel(
         z_codes = [keep.tile([P, P1], U32, name=f"z_codes{g}", align_bytes=64) for g in range(G_PASSES)]
         z_plane = [keep.tile([P, P1], U8, name=f"z_plane{g}", align_bytes=64) for g in range(G_PASSES)]
 
-        def quantise_z(g, afters=(None, None)):
-            z = {}
-            for half, after in enumerate(afters):
-                m = slice(half * P1 // 2, (half + 1) * P1 // 2)
-                place = dict(tag="z", bufs=4) if after is None else dict(tag=f"turn{after}", bufs=1)
-                z[half] = ring.tile([P, P1 // 2, PACK], BF16, name=f"z{g}_{half}", align_bytes=64, **place)
-                engine = nc.vector if after is None else nc.gpsimd
-                engine.tensor_tensor(woven(z[half][:]), planar(u[g][:, :, m]), planar(x[g][:, :, m]), ALU.mult)
-            for half in z:
-                m = slice(half * P1 // 2, (half + 1) * P1 // 2)
+        def quantise_z(g):
+            z = ring.tile([P, P1, PACK], BF16, name=f"z{g}", tag="z", bufs=G_PASSES, align_bytes=64)
+            halves = [slice(0, P1 // 2), slice(P1 // 2, P1)]
+            for m in halves:
+                nc.vector.tensor_tensor(woven(z[:, m, :]), planar(u[g][:, :, m]), planar(x[g][:, :, m]), ALU.mult)
+            for m in halves:
                 nc.vector.quantize_mx(
-                    out=z_codes[g][:, m].bitcast(FP8X4), scales=z_plane[g][:, m], in_=z[half][:].rearrange("p c t -> p (c t)")
+                    out=z_codes[g][:, m].bitcast(FP8X4), scales=z_plane[g][:, m], in_=z[:, m, :].rearrange("p c t -> p (c t)")
                 )
 
         def second_product(g, acc):
@@ -256,28 +246,29 @@ def tile_list_claim_charting_kernel(
 
         last = G_PASSES * PACK - 1
         batches = [[0]] + [[j, j + 1] for j in range(1, last, 2)] + [[last]]
-        factors_behind = {3: [0, 1, 2], 4: [3], 5: [4, 5, 6], 6: [7]}
-        for k, batch in enumerate(batches):
+        for batch in batches:
             first_product(batch)
+        turn_coef()
+        for batch in batches:
             pair_up(batch)
-            if k < 3:
-                quantise_w2(0, k * CAST_COLS, (k + 1) * CAST_COLS, after=batch[-1])
-            if k == 2:
-                turn_coef()
-            for j in factors_behind.get(k, []):
-                factor(j)
-        load_w2(2)
         acc = [psum.tile([P, P1], F32, name=f"acc{n}", tag=f"bank{n}") for n in range(N_TILES)]
-        quantise_z(0, afters=(6, 8))
-        second_product(0, acc)
-        for g in range(1, G_PASSES):
-            if g == G_PASSES - 1:
-                for t in range(PACK):
-                    factor(g * PACK + t)
+        def make_z(g):
+            for t in range(PACK):
+                factor(g * PACK + t)
             quantise_z(g)
+
+        def finish_pass(g):
             for c0, c1 in zip(W2_CUTS[:-1], W2_CUTS[1:]):
                 quantise_w2(g, c0, c1)
             second_product(g, acc)
+
+        make_z(0)
+        make_z(1)
+        finish_pass(0)
+        load_w2(2)
+        make_z(2)
+        finish_pass(1)
+        finish_pass(2)
 
         for n in range(N_TILES):
             y = ring.tile([P, P1], F32, name=f"y{n}", tag="rows", bufs=G_PASSES * PACK)

@@ -22,13 +22,12 @@ PACK = 4
 K_PASS = P * PACK
 A_PASSES = K // K_PASS
 G_PASSES = H // K_PASS
+ROW_TILES = G_PASSES * PACK
 BANK = 512
 HALVES = S // BANK
 N_TILES = N // P
 BANKS = 8
-W2_CUTS = (0, 256, N)
-CAST_COLS = 256
-LAST_PIECE = 64
+EARLY = 256
 
 
 def tile_list_claim_charting_kernel(
@@ -40,29 +39,32 @@ def tile_list_claim_charting_kernel(
         ring = ctx.enter_context(tc.tile_pool(name="ring", bufs=2))
         psum = ctx.enter_context(tc.psum_pool(name="psum", bufs=1))
 
+        def tile(shape, dtype, name, tag=None):
+            return keep.tile(shape, dtype, name=name, tag=tag or name, align_bytes=64)
+
         def load_list(src, name):
-            tile = keep.tile(list(src.shape), U16, name=name)
-            nc.sync.dma_start(tile[:], src)
-            return tile
+            held = keep.tile(list(src.shape), U16, name=name)
+            nc.sync.dma_start(held[:], src)
+            return held
 
         rows0 = P - A_PASSES * 16
-        tab_plane = keep.tile([P, T], U8, tag="early", align_bytes=64)
+        tab_plane = tile([P, T], U8, "tab_plane", "early")
         nc.vector.memset(tab_plane[0:rows0, :].bitcast(I32), 0)
-        v_planes = [keep.tile([P, S], U8, name=f"v_plane{a}", align_bytes=64) for a in range(A_PASSES)]
+        v_planes = [tile([P, S], U8, f"v_plane{a}") for a in range(A_PASSES)]
         for plane in v_planes:
             nc.vector.memset(plane[:].bitcast(I32), 0)
-        w4_plane_raw = keep.tile([P, A_PASSES * H], U8, align_bytes=64)
+        w4_plane_raw = tile([P, A_PASSES * H], U8, "w4_plane_raw", "last_rounded")
         nc.gpsimd.memset(w4_plane_raw[:].bitcast(I32), 0)
 
         offs_t = load_list(offs, "offs_t")
         nc.sync.dma_start(tab_plane[rows0:P, :].bitcast(I32), tab_scales.rearrange("a q t -> (a q) t").bitcast(I32))
-        tab_w = [keep.tile([P, T], I32, name=f"tab_w{a}", tag=f"stage{a}", align_bytes=64) for a in range(A_PASSES)]
+        tab_w = [tile([P, T], I32, f"tab_w{a}", f"stage{a}") for a in range(A_PASSES)]
 
         def load_tab(a):
             nc.sync.dma_start(tab_w[a][:], tab_words[a].rearrange("p t i -> p (t i)").bitcast(I32))
 
-        def load_w4(g0, g1, **place):
-            raw = keep.tile([P, A_PASSES, (g1 - g0) * K_PASS // 2], I32, name=f"w4_raw{g0}", align_bytes=64, **place)
+        def load_w4(g0, g1, tag):
+            raw = tile([P, A_PASSES, (g1 - g0) * K_PASS // 2], I32, f"w4_raw{g0}", tag)
             cols = slice(2 * K_PASS * g0, 2 * K_PASS * g1)
             nc.sync.dma_start(raw[:], w4_words[:, :, cols].rearrange("a p c -> p a c").bitcast(I32))
             return [raw[:, :, (g - g0) * K_PASS // 2 : (g - g0 + 1) * K_PASS // 2] for g in range(g0, g1)]
@@ -72,7 +74,7 @@ def tile_list_claim_charting_kernel(
         pos2_t = load_list(pos2, "pos2_t")
         pos3_t = load_list(pos3, "pos3_t")
         pos4_t = load_list(pos4, "pos4_t")
-        w4_raw = load_w4(0, 1)
+        w4_raw = load_w4(0, 1, "w4_first")
         load_tab(1)
         for q in range(4):
             nc.gpsimd.dma_start(
@@ -80,7 +82,7 @@ def tile_list_claim_charting_kernel(
                 w4_scales[:, 4 * q : 4 * q + 4, :].bitcast(I32).rearrange("a r c -> r a c"),
             )
 
-        v_rows = keep.tile([P, S], U8, tag="rows_then_identity", align_bytes=64)
+        v_rows = tile([P, S], U8, "v_rows", "rows_then_identity")
         nc.vector.tensor_copy(v_rows[:], tab_plane[:].indirect(offs_t[:]))
         for a in range(A_PASSES):
             for q in range(4):
@@ -90,40 +92,41 @@ def tile_list_claim_charting_kernel(
                     v_planes[a][32 * q : 32 * q + 4, :].bitcast(I32),
                     v_rows[row : row + 4, :].bitcast(I32),
                 )
+        w4_raw.extend(load_w4(1, G_PASSES, "early"))
 
-        coef_rows = keep.tile([P, G_PASSES * P], F32, tag="early", align_bytes=64)
+        coef_rows = tile([P, G_PASSES * P], F32, "coef_rows")
         nc.gpsimd.memset(coef_rows[:], 0.0)
         nc.gpsimd.dma_start(
             coef_rows[0:PACK, :].rearrange("t (b i) -> t b i", i=8),
             coef.rearrange("(b t i) -> t b i", t=PACK, i=8),
         )
-        ident = keep.tile([P, P], F32, tag="rows_then_identity", align_bytes=64)
+        ident = tile([P, P], F32, "ident", "rows_then_identity")
         make_identity(nc, ident[:])
 
         w2_raw = {}
 
-        def load_w2(g):
-            w2_raw[g] = keep.tile([P, PACK, N], F32, name=f"w2_raw{g}", tag=f"stage{(g + 1) % 2}", align_bytes=64)
-            rows = w2[K_PASS * g : K_PASS * (g + 1), :].rearrange("(q t i) n -> t q i n", t=PACK, i=8)
+        def load_w2(g, c0, c1, tag):
+            w2_raw[g, c0] = tile([P, PACK, c1 - c0], F32, f"w2_raw{g}_{c0}", tag)
+            rows = w2[K_PASS * g : K_PASS * (g + 1), c0:c1].rearrange("(q t i) n -> t q i n", t=PACK, i=8)
             for t in range(PACK):
-                nc.sync.dma_start(w2_raw[g][:, t, :], rows[t])
+                nc.sync.dma_start(w2_raw[g, c0][:, t, :], rows[t])
 
         v_w = {}
 
         def gather_words(a, half):
-            v_w[a, half] = keep.tile([P, BANK], U32, name=f"v_w{a}_{half}", align_bytes=64)
+            v_w[a, half] = tile([P, BANK], U32, f"v_w{a}_{half}")
             cols = slice(half * BANK // 16, (half + 1) * BANK // 16)
             nc.vector.tensor_copy(v_w[a, half][:], tab_w[a][:].bitcast(U32).indirect(offs_t[:, cols]))
 
         w4_codes, w4_planes = {}, {}
 
         def order_w4(g):
-            w4_codes[g] = keep.tile([P, A_PASSES * K_PASS * 2], U8, name=f"w4_codes{g}", align_bytes=64)
+            w4_codes[g] = tile([P, A_PASSES * K_PASS * 2], U8, f"w4_codes{g}")
             nc.vector.tensor_copy(
                 w4_codes[g][:].bitcast(I32).rearrange("p (a t q w) -> p a t q w", a=A_PASSES, t=PACK, w=4),
                 w4_raw[g].rearrange("p a (q t w) -> p a t q w", t=PACK, w=4),
             )
-            w4_planes[g] = keep.tile([P, A_PASSES * K_PASS], U8, name=f"w4_plane{g}", align_bytes=64)
+            w4_planes[g] = tile([P, A_PASSES * K_PASS], U8, f"w4_plane{g}")
             nc.vector.tensor_copy(
                 w4_planes[g][:].bitcast(I32).rearrange("p (a t q w) -> p a t q w", a=A_PASSES, t=PACK, w=2),
                 w4_plane_raw[:].bitcast(I32).rearrange("p (a g q t w) -> p g a t q w", a=A_PASSES, g=G_PASSES, t=PACK, w=2)[:, g],
@@ -131,72 +134,49 @@ def tile_list_claim_charting_kernel(
 
         for half in range(HALVES):
             gather_words(0, half)
-        w4_raw.extend(load_w4(1, G_PASSES, tag="stage0"))
+        load_w2(0, 0, N, "stage0")
         order_w4(0)
         for half in range(HALVES):
             gather_words(1, half)
-        load_w2(0)
+        load_w2(1, 0, N, "stage1")
         for g in range(1, G_PASSES):
             order_w4(g)
-        load_w2(1)
+        load_w2(2, 0, EARLY, "last_rounded")
+        load_w2(2, EARLY, N, "early")
 
-        h = {}
-        banks = {}
+        h = []
+        banks = []
 
-        def multiply_first(j, half):
+        def next_bank(shape, name):
+            banks.append(psum.tile(shape, F32, name=name, tag=f"bank{len(banks) % BANKS}"))
+            return banks[-1]
+
+        first = [tile([P, PACK, P1], F32, f"first{g}") for g in range(G_PASSES)]
+        for j in range(ROW_TILES):
             g, t = divmod(j, PACK)
-            banks[j, half] = psum.tile([P, BANK], F32, name=f"hb{j}_{half}", tag=f"bank{len(banks) % BANKS}")
-            for a in range(A_PASSES):
-                col = (a * PACK + t) * P
-                nc.tensor.matmul_mx(
-                    out=banks[j, half][:],
-                    lhsT=w4_codes[g][:, 2 * col : 2 * (col + P)].bitcast(FP4X4),
-                    lhsT_scale=w4_planes[g][:, col : col + P],
-                    rhs=v_w[a, half][:].bitcast(FP8X4),
-                    rhs_scale=v_planes[a][:, half * BANK : (half + 1) * BANK],
-                    start=(a == 0),
-                    stop=(a == A_PASSES - 1),
-                )
+            h.append(tile([P, S], F32, f"h{j}"))
+            for half in range(HALVES):
+                cols = slice(half * BANK, (half + 1) * BANK)
+                bank = next_bank([P, BANK], f"hb{j}_{half}")
+                for a in range(A_PASSES):
+                    col = (a * PACK + t) * P
+                    nc.tensor.matmul_mx(
+                        out=bank[:],
+                        lhsT=w4_codes[g][:, 2 * col : 2 * (col + P)].bitcast(FP4X4),
+                        lhsT_scale=w4_planes[g][:, col : col + P],
+                        rhs=v_w[a, half][:].bitcast(FP8X4),
+                        rhs_scale=v_planes[a][:, cols],
+                        start=(a == 0),
+                        stop=(a == A_PASSES - 1),
+                    )
+                nc.scalar.activation(h[j][:, cols], bank[:], ACT.Copy)
+            nc.vector.tensor_copy(first[g][:, t, :], h[j][:].indirect(pos1_t[:]))
 
-        def empty_first(j, c0, c1):
-            half = c0 // BANK
-            nc.scalar.activation(h[j][:, c0:c1], banks[j, half][:, c0 - half * BANK : c1 - half * BANK], ACT.Copy)
-
-        coef_t = keep.tile([P, G_PASSES, PACK], F32)
-
-        def turn_coef():
-            banks["coef"] = psum.tile([P, G_PASSES, P], F32, name="coef_turned", tag=f"bank{len(banks) % BANKS}")
-            for g in range(G_PASSES):
-                nc.tensor.transpose(banks["coef"][:, g, :], coef_rows[:, g * P : (g + 1) * P], ident[:])
-            nc.scalar.activation(coef_t[:], banks["coef"][:, :, 0:PACK], ACT.Copy)
-
-        def first_product(batch):
-            cuts = (0, BANK, S) if len(batch) == 1 else (0, BANK, S - LAST_PIECE, S)
-            for j in batch:
-                h[j] = ring.tile([P, S], F32, name=f"h{j}", tag="rows", bufs=G_PASSES * PACK)
-            for c0, c1 in zip(cuts[:-1], cuts[1:]):
-                for j in batch:
-                    if c0 % BANK == 0:
-                        multiply_first(j, c0 // BANK)
-                    empty_first(j, c0, c1)
-
-        x = [keep.tile([P, PACK, P1], F32, name=f"x{g}") for g in range(G_PASSES)]
-        u = [keep.tile([P, PACK, P1], F32, name=f"u{g}") for g in range(G_PASSES)]
-
-        def pair_up(batch):
-            first = {}
-            for j in batch:
-                first[j] = ring.tile([P, P1], F32, name=f"first{j}", tag="first", bufs=4, align_bytes=64)
-                nc.vector.tensor_copy(first[j][:], h[j][:].indirect(pos1_t[:]))
-            for j in batch:
-                g, t = divmod(j, PACK)
-                nc.vector.tensor_tensor(x[g][:, t, :], h[j][:].indirect(pos2_t[:]), first[j][:], ALU.add)
-
-        def factor(j):
-            g, t = divmod(j, PACK)
-            sq = ring.tile([P, P1], F32, name=f"sq{j}", tag="sq")
-            nc.scalar.activation(sq[:], x[g][:, t, :], ACT.Square)
-            nc.scalar.activation(u[g][:, t, :], sq[:], ACT.Identity, bias=1.0, scale=coef_t[:, g, t : t + 1])
+        coef_t = tile([P, G_PASSES, PACK], F32, "coef_t")
+        turned = next_bank([P, G_PASSES, P], "coef_turned")
+        for g in range(G_PASSES):
+            nc.tensor.transpose(turned[:, g, :], coef_rows[:, g * P : (g + 1) * P], ident[:])
+        nc.scalar.activation(coef_t[:], turned[:, :, 0:PACK], ACT.Copy)
 
         def woven(view):
             return view.rearrange("p (c i) t -> p c t i", i=4)
@@ -204,78 +184,97 @@ def tile_list_claim_charting_kernel(
         def planar(view):
             return view.rearrange("p t (c i) -> p c t i", i=4)
 
-        w2_parts = {g: [] for g in range(G_PASSES)}
+        rounded = {}
+        for g in range(G_PASSES):
+            for c0, c1 in ((0, EARLY), (EARLY, N)):
+                rounded[g, c0] = tile([P, c1 - c0, PACK], BF16, f"w2_woven{g}_{c0}")
+                if (g, c0) in w2_raw and g == G_PASSES - 1:
+                    src = w2_raw[g, c0][:]
+                else:
+                    src = w2_raw[g, 0][:, :, c0:c1]
+                if (g, c0) != (G_PASSES - 1, EARLY):
+                    nc.gpsimd.tensor_scalar(rounded[g, c0][:], src.rearrange("p t c -> p c t"), 1.0, 0.0, ALU.mult, ALU.add)
 
-        def quantise_w2(g, c0, c1):
-            width = c1 - c0
-            rounded = keep.tile([P, width, PACK], BF16, name=f"w2_woven{g}_{c0}", align_bytes=64)
-            for c in range(0, width, CAST_COLS):
-                copy = nc.vector.tensor_copy if (g, c0 + c) == (G_PASSES - 1, N - CAST_COLS) else nc.scalar.copy
-                copy(woven(rounded[:, c : c + CAST_COLS, :]), planar(w2_raw[g][:, :, c0 + c : c0 + c + CAST_COLS]))
-            codes = keep.tile([P, width], U32, name=f"w2_codes{g}_{c0}", align_bytes=64)
-            plane = keep.tile([P, width], U8, name=f"w2_plane{g}_{c0}", align_bytes=64)
-            nc.vector.quantize_mx(out=codes[:].bitcast(FP8X4), scales=plane[:], in_=rounded[:].rearrange("p c t -> p (c t)"))
-            w2_parts[g].append((c0, c1, codes, plane))
+        x = tile([P, ROW_TILES, P1], F32, "x", "last_rounded")
+        for j in range(ROW_TILES):
+            g, t = divmod(j, PACK)
+            nc.vector.tensor_tensor(x[:, j, :], h[j][:].indirect(pos2_t[:]), first[g][:, t, :], ALU.add)
+        for j in range(ROW_TILES):
+            g, t = divmod(j, PACK)
+            sq = ring.tile([P, P1], F32, name=f"sq{j}", tag="sq")
+            nc.scalar.activation(sq[:], x[:, j, :], ACT.Square)
+            nc.scalar.activation(first[g][:, t, :], sq[:], ACT.Identity, bias=1.0, scale=coef_t[:, g, t : t + 1])
+        nc.scalar.copy(woven(rounded[G_PASSES - 1, EARLY][:]), planar(w2_raw[G_PASSES - 1, EARLY][:]))
 
-        z_codes = [keep.tile([P, P1], U32, name=f"z_codes{g}", align_bytes=64) for g in range(G_PASSES)]
-        z_plane = [keep.tile([P, P1], U8, name=f"z_plane{g}", align_bytes=64) for g in range(G_PASSES)]
+        w2_mx = {}
 
-        def quantise_z(g):
-            z = ring.tile([P, P1, PACK], BF16, name=f"z{g}", tag="z", bufs=G_PASSES, align_bytes=64)
+        def quantise_w2(g, c0, c1, codes):
+            plane = tile([P, c1 - c0], U8, f"w2_plane{g}_{c0}")
+            nc.vector.quantize_mx(out=codes.bitcast(FP8X4), scales=plane[:], in_=rounded[g, c0][:].rearrange("p c t -> p (c t)"))
+            for n in range(c0 // P, c1 // P):
+                cols = slice(n * P - c0, (n + 1) * P - c0)
+                w2_mx[g, n] = (codes[:, cols], plane[:, cols])
+
+        z_codes = [tile([P, P1], U32, f"z_codes{g}") for g in range(G_PASSES)]
+        z_plane = [tile([P, P1], U8, f"z_plane{g}") for g in range(G_PASSES)]
+
+        def make_z(g):
+            z = tile([P, P1, PACK], BF16, f"z{g}")
             halves = [slice(0, P1 // 2), slice(P1 // 2, P1)]
             for m in halves:
-                nc.vector.tensor_tensor(woven(z[:, m, :]), planar(u[g][:, :, m]), planar(x[g][:, :, m]), ALU.mult)
+                nc.vector.tensor_tensor(
+                    woven(z[:, m, :]), planar(first[g][:, :, m]), planar(x[:, PACK * g : PACK * (g + 1), m]), ALU.mult
+                )
             for m in halves:
                 nc.vector.quantize_mx(
                     out=z_codes[g][:, m].bitcast(FP8X4), scales=z_plane[g][:, m], in_=z[:, m, :].rearrange("p c t -> p (c t)")
                 )
 
-        def second_product(g, acc):
-            for c0, c1, codes, plane in w2_parts[g]:
-                for n in range(c0 // P, c1 // P):
-                    cols = slice(n * P - c0, (n + 1) * P - c0)
-                    nc.tensor.matmul_mx(
-                        out=acc[n][:],
-                        lhsT=codes[:, cols].bitcast(FP8X4),
-                        lhsT_scale=plane[:, cols],
-                        rhs=z_codes[g][:].bitcast(FP8X4),
-                        rhs_scale=z_plane[g][:],
-                        start=(g == 0),
-                        stop=(g == G_PASSES - 1),
-                    )
-
-        last = G_PASSES * PACK - 1
-        batches = [[0]] + [[j, j + 1] for j in range(1, last, 2)] + [[last]]
-        for batch in batches:
-            first_product(batch)
-        turn_coef()
-        for batch in batches:
-            pair_up(batch)
         acc = [psum.tile([P, P1], F32, name=f"acc{n}", tag=f"bank{n}") for n in range(N_TILES)]
-        def make_z(g):
-            for t in range(PACK):
-                factor(g * PACK + t)
-            quantise_z(g)
 
-        def finish_pass(g):
-            for c0, c1 in zip(W2_CUTS[:-1], W2_CUTS[1:]):
-                quantise_w2(g, c0, c1)
-            second_product(g, acc)
+        def second_product(g, n):
+            codes, plane = w2_mx[g, n]
+            nc.tensor.matmul_mx(
+                out=acc[n][:],
+                lhsT=codes.bitcast(FP8X4),
+                lhsT_scale=plane,
+                rhs=z_codes[g][:].bitcast(FP8X4),
+                rhs_scale=z_plane[g][:],
+                start=(g == 0),
+                stop=(g == G_PASSES - 1),
+            )
 
         make_z(0)
+        for g in range(G_PASSES):
+            quantise_w2(g, 0, EARLY, tile([P, EARLY], U32, f"w2_codes{g}", f"h{g}")[:])
+        quantise_w2(0, EARLY, N, tile([P, N - EARLY], U32, "w2_codes0_late", f"h{G_PASSES}")[:])
         make_z(1)
-        finish_pass(0)
-        load_w2(2)
         make_z(2)
-        finish_pass(1)
-        finish_pass(2)
-
+        late = tile([P, G_PASSES - 1, N - EARLY], U32, "w2_codes_late", f"first{G_PASSES - 1}")
+        for g in range(1, G_PASSES):
+            quantise_w2(g, EARLY, N, late[:, g - 1, :])
         for n in range(N_TILES):
-            y = ring.tile([P, P1], F32, name=f"y{n}", tag="rows", bufs=G_PASSES * PACK)
-            nc.scalar.activation(y[:], acc[n][:], ACT.Copy)
-            rivals = ring.tile([P, 2, P2], F32, name=f"rivals{n}", tag="first", bufs=4, align_bytes=64)
-            nc.vector.tensor_copy(rivals[:, 0, :], y[:].indirect(pos3_t[:]))
-            nc.vector.tensor_copy(rivals[:, 1, :], y[:].indirect(pos4_t[:]))
-            least = keep.tile([P, P2], F32, name=f"least{n}")
+            second_product(0, n)
+        for g in range(1, G_PASSES):
+            for n in range(EARLY // P):
+                second_product(g, n)
+        for n in range(EARLY // P, N_TILES):
+            for g in range(1, G_PASSES):
+                second_product(g, n)
+
+        def finish(n, rivals):
+            least = tile([P, P2], F32, f"least{n}")
             nc.vector.tensor_tensor(least[:], rivals[:, 0, :], rivals[:, 1, :], ALU.min)
             nc.sync.dma_start(out[n * P : (n + 1) * P, :], least[:])
+
+        waiting = None
+        for n in range(N_TILES):
+            y = tile([P, P1], F32, f"y{n}", f"h{PACK + n}")
+            nc.scalar.activation(y[:], acc[n][:], ACT.Copy)
+            rivals = ring.tile([P, 2, P2], F32, name=f"rivals{n}", tag="rivals", bufs=3, align_bytes=64)
+            nc.vector.tensor_copy(rivals[:, 0, :], y[:].indirect(pos3_t[:]))
+            if waiting:
+                finish(*waiting)
+            nc.vector.tensor_copy(rivals[:, 1, :], y[:].indirect(pos4_t[:]))
+            waiting = (n, rivals)
+        finish(*waiting)

@@ -1,7 +1,6 @@
 from contextlib import ExitStack
 
 import concourse.mybir as mybir
-from concourse.masks import make_identity
 
 T, S, P1, P2, K, H, N = 2048, 1024, 512, 256, 1024, 1536, 768
 FLOPS = 2 * K * H * S + 2 * H * N * P1
@@ -27,7 +26,8 @@ BANK = 512
 HALVES = S // BANK
 N_TILES = N // P
 BANKS = 8
-EARLY = 256
+PIECE = 256
+LAST_PIECE = 64
 
 
 def tile_list_claim_charting_kernel(
@@ -53,7 +53,7 @@ def tile_list_claim_charting_kernel(
         v_planes = [tile([P, S], U8, f"v_plane{a}") for a in range(A_PASSES)]
         for plane in v_planes:
             nc.vector.memset(plane[:].bitcast(I32), 0)
-        w4_plane_raw = tile([P, A_PASSES * H], U8, "w4_plane_raw", "last_rounded")
+        w4_plane_raw = tile([P, A_PASSES * H], U8, "w4_plane_raw")
         nc.gpsimd.memset(w4_plane_raw[:].bitcast(I32), 0)
 
         offs_t = load_list(offs, "offs_t")
@@ -86,30 +86,20 @@ def tile_list_claim_charting_kernel(
         nc.vector.tensor_copy(v_rows[:], tab_plane[:].indirect(offs_t[:]))
         for a in range(A_PASSES):
             for q in range(4):
-                queue = nc.gpsimd if (q, a) == (3, A_PASSES - 1) else nc.sync
                 row = rows0 + 16 * a + 4 * q
-                queue.dma_start(
+                nc.sync.dma_start(
                     v_planes[a][32 * q : 32 * q + 4, :].bitcast(I32),
                     v_rows[row : row + 4, :].bitcast(I32),
                 )
         w4_raw.extend(load_w4(1, G_PASSES, "early"))
 
-        coef_rows = tile([P, G_PASSES * P], F32, "coef_rows")
-        nc.gpsimd.memset(coef_rows[:], 0.0)
-        nc.gpsimd.dma_start(
-            coef_rows[0:PACK, :].rearrange("t (b i) -> t b i", i=8),
-            coef.rearrange("(b t i) -> t b i", t=PACK, i=8),
-        )
-        ident = tile([P, P], F32, "ident", "rows_then_identity")
-        make_identity(nc, ident[:])
-
         w2_raw = {}
 
-        def load_w2(g, c0, c1, tag):
-            w2_raw[g, c0] = tile([P, PACK, c1 - c0], F32, f"w2_raw{g}_{c0}", tag)
-            rows = w2[K_PASS * g : K_PASS * (g + 1), c0:c1].rearrange("(q t i) n -> t q i n", t=PACK, i=8)
+        def load_w2(g, tag):
+            w2_raw[g] = tile([P, PACK, N], F32, f"w2_raw{g}", tag)
+            rows = w2[K_PASS * g : K_PASS * (g + 1), :].rearrange("(q t i) n -> t q i n", t=PACK, i=8)
             for t in range(PACK):
-                nc.sync.dma_start(w2_raw[g, c0][:, t, :], rows[t])
+                nc.sync.dma_start(w2_raw[g][:, t, :], rows[t])
 
         v_w = {}
 
@@ -134,49 +124,63 @@ def tile_list_claim_charting_kernel(
 
         for half in range(HALVES):
             gather_words(0, half)
-        load_w2(0, 0, N, "stage0")
+        load_w2(0, "stage0")
         order_w4(0)
         for half in range(HALVES):
             gather_words(1, half)
-        load_w2(1, 0, N, "stage1")
+        load_w2(1, "stage1")
         for g in range(1, G_PASSES):
             order_w4(g)
-        load_w2(2, 0, EARLY, "last_rounded")
-        load_w2(2, EARLY, N, "early")
+        load_w2(2, "early")
+        coef_t = tile([P, ROW_TILES, 8], F32, "coef_t", "rows_then_identity")
+        coef_rows = coef.rearrange("(g q t i o) -> g t q i o", g=G_PASSES, t=PACK, i=8, o=1)
+        with nc.allow_non_contiguous_dma(reason="one coefficient for each partition and row tile"):
+            for j in range(ROW_TILES):
+                nc.sync.dma_start(coef_t[:, j, 0:1], coef_rows[j // PACK, j % PACK])
 
-        h = []
         banks = []
 
         def next_bank(shape, name):
             banks.append(psum.tile(shape, F32, name=name, tag=f"bank{len(banks) % BANKS}"))
             return banks[-1]
 
+        h = [tile([P, S], F32, f"h{j}") for j in range(ROW_TILES)]
         first = [tile([P, PACK, P1], F32, f"first{g}") for g in range(G_PASSES)]
+
+        def first_product(j, half):
+            g, t = divmod(j, PACK)
+            cols = slice(half * BANK, (half + 1) * BANK)
+            bank = next_bank([P, BANK], f"hb{j}_{half}")
+            for a in range(A_PASSES):
+                col = (a * PACK + t) * P
+                nc.tensor.matmul_mx(
+                    out=bank[:],
+                    lhsT=w4_codes[g][:, 2 * col : 2 * (col + P)].bitcast(FP4X4),
+                    lhsT_scale=w4_planes[g][:, col : col + P],
+                    rhs=v_w[a, half][:].bitcast(FP8X4),
+                    rhs_scale=v_planes[a][:, cols],
+                    start=(a == 0),
+                    stop=(a == A_PASSES - 1),
+                )
+            return bank
+
+        def empty(j, bank, c0, c1):
+            nc.scalar.activation(h[j][:, c0:c1], bank[:, c0 % BANK : (c1 - 1) % BANK + 1], ACT.Copy)
+
+        for batch in [[0], [1, 2], [3, 4]] + [[j] for j in range(5, ROW_TILES)]:
+            cut = S - LAST_PIECE if len(batch) > 1 else S
+            for j in batch:
+                empty(j, first_product(j, 0), 0, BANK)
+            second = {}
+            for j in batch:
+                second[j] = first_product(j, 1)
+                empty(j, second[j], BANK, cut)
+            if cut < S:
+                for j in batch:
+                    empty(j, second[j], cut, S)
         for j in range(ROW_TILES):
             g, t = divmod(j, PACK)
-            h.append(tile([P, S], F32, f"h{j}"))
-            for half in range(HALVES):
-                cols = slice(half * BANK, (half + 1) * BANK)
-                bank = next_bank([P, BANK], f"hb{j}_{half}")
-                for a in range(A_PASSES):
-                    col = (a * PACK + t) * P
-                    nc.tensor.matmul_mx(
-                        out=bank[:],
-                        lhsT=w4_codes[g][:, 2 * col : 2 * (col + P)].bitcast(FP4X4),
-                        lhsT_scale=w4_planes[g][:, col : col + P],
-                        rhs=v_w[a, half][:].bitcast(FP8X4),
-                        rhs_scale=v_planes[a][:, cols],
-                        start=(a == 0),
-                        stop=(a == A_PASSES - 1),
-                    )
-                nc.scalar.activation(h[j][:, cols], bank[:], ACT.Copy)
             nc.vector.tensor_copy(first[g][:, t, :], h[j][:].indirect(pos1_t[:]))
-
-        coef_t = tile([P, G_PASSES, PACK], F32, "coef_t")
-        turned = next_bank([P, G_PASSES, P], "coef_turned")
-        for g in range(G_PASSES):
-            nc.tensor.transpose(turned[:, g, :], coef_rows[:, g * P : (g + 1) * P], ident[:])
-        nc.scalar.activation(coef_t[:], turned[:, :, 0:PACK], ACT.Copy)
 
         def woven(view):
             return view.rearrange("p (c i) t -> p c t i", i=4)
@@ -184,83 +188,72 @@ def tile_list_claim_charting_kernel(
         def planar(view):
             return view.rearrange("p t (c i) -> p c t i", i=4)
 
-        rounded = {}
-        for g in range(G_PASSES):
-            for c0, c1 in ((0, EARLY), (EARLY, N)):
-                rounded[g, c0] = tile([P, c1 - c0, PACK], BF16, f"w2_woven{g}_{c0}")
-                if (g, c0) in w2_raw and g == G_PASSES - 1:
-                    src = w2_raw[g, c0][:]
-                else:
-                    src = w2_raw[g, 0][:, :, c0:c1]
-                if (g, c0) != (G_PASSES - 1, EARLY):
-                    nc.gpsimd.tensor_scalar(rounded[g, c0][:], src.rearrange("p t c -> p c t"), 1.0, 0.0, ALU.mult, ALU.add)
-
-        x = tile([P, ROW_TILES, P1], F32, "x", "last_rounded")
+        x = [tile([P, PACK, P1], F32, f"x{g}", f"v_w{g - 1}_1" if g else None) for g in range(G_PASSES)]
         for j in range(ROW_TILES):
             g, t = divmod(j, PACK)
-            nc.vector.tensor_tensor(x[:, j, :], h[j][:].indirect(pos2_t[:]), first[g][:, t, :], ALU.add)
-        for j in range(ROW_TILES):
+            nc.vector.tensor_tensor(x[g][:, t, :], h[j][:].indirect(pos2_t[:]), first[g][:, t, :], ALU.add)
+
+        def factor(j):
             g, t = divmod(j, PACK)
             sq = ring.tile([P, P1], F32, name=f"sq{j}", tag="sq")
-            nc.scalar.activation(sq[:], x[:, j, :], ACT.Square)
-            nc.scalar.activation(first[g][:, t, :], sq[:], ACT.Identity, bias=1.0, scale=coef_t[:, g, t : t + 1])
-        nc.scalar.copy(woven(rounded[G_PASSES - 1, EARLY][:]), planar(w2_raw[G_PASSES - 1, EARLY][:]))
+            nc.scalar.activation(sq[:], x[g][:, t, :], ACT.Square)
+            nc.scalar.activation(first[g][:, t, :], sq[:], ACT.Identity, bias=1.0, scale=coef_t[:, j, 0:1])
+
+        rounded = {}
+
+        def round_w2(g, c):
+            rounded[g, c] = tile([P, PIECE, PACK], BF16, f"w2_woven{g}_{c}")
+            nc.scalar.copy(woven(rounded[g, c][:]), planar(w2_raw[g][:, :, c * PIECE : (c + 1) * PIECE]))
+
+        pieces = [(g, c) for c in range(N // PIECE) for g in range(G_PASSES)]
+        for j in range(ROW_TILES):
+            factor(j)
+            if ROW_TILES - 4 <= j < ROW_TILES - 2:
+                round_w2(*pieces[len(rounded)])
+        for g, c in pieces[len(rounded) :]:
+            round_w2(g, c)
 
         w2_mx = {}
 
-        def quantise_w2(g, c0, c1, codes):
-            plane = tile([P, c1 - c0], U8, f"w2_plane{g}_{c0}")
-            nc.vector.quantize_mx(out=codes.bitcast(FP8X4), scales=plane[:], in_=rounded[g, c0][:].rearrange("p c t -> p (c t)"))
-            for n in range(c0 // P, c1 // P):
-                cols = slice(n * P - c0, (n + 1) * P - c0)
-                w2_mx[g, n] = (codes[:, cols], plane[:, cols])
+        def quantise_w2(g, c):
+            codes = tile([P, PIECE], U32, f"w2_codes{g}_{c}")
+            plane = tile([P, PIECE], U8, f"w2_plane{g}_{c}")
+            nc.vector.quantize_mx(out=codes[:].bitcast(FP8X4), scales=plane[:], in_=rounded[g, c][:].rearrange("p c t -> p (c t)"))
+            for n in range(PIECE // P):
+                cols = slice(n * P, (n + 1) * P)
+                w2_mx[g, c * PIECE // P + n] = (codes[:, cols], plane[:, cols])
 
         z_codes = [tile([P, P1], U32, f"z_codes{g}") for g in range(G_PASSES)]
         z_plane = [tile([P, P1], U8, f"z_plane{g}") for g in range(G_PASSES)]
 
         def make_z(g):
-            z = tile([P, P1, PACK], BF16, f"z{g}")
+            z = tile([P, P1, PACK], BF16, f"z{g}", f"h{g}")
             halves = [slice(0, P1 // 2), slice(P1 // 2, P1)]
             for m in halves:
-                nc.vector.tensor_tensor(
-                    woven(z[:, m, :]), planar(first[g][:, :, m]), planar(x[:, PACK * g : PACK * (g + 1), m]), ALU.mult
-                )
+                nc.vector.tensor_tensor(woven(z[:, m, :]), planar(first[g][:, :, m]), planar(x[g][:, :, m]), ALU.mult)
             for m in halves:
                 nc.vector.quantize_mx(
                     out=z_codes[g][:, m].bitcast(FP8X4), scales=z_plane[g][:, m], in_=z[:, m, :].rearrange("p c t -> p (c t)")
                 )
 
-        acc = [psum.tile([P, P1], F32, name=f"acc{n}", tag=f"bank{n}") for n in range(N_TILES)]
-
-        def second_product(g, n):
-            codes, plane = w2_mx[g, n]
-            nc.tensor.matmul_mx(
-                out=acc[n][:],
-                lhsT=codes.bitcast(FP8X4),
-                lhsT_scale=plane,
-                rhs=z_codes[g][:].bitcast(FP8X4),
-                rhs_scale=z_plane[g][:],
-                start=(g == 0),
-                stop=(g == G_PASSES - 1),
-            )
-
-        make_z(0)
         for g in range(G_PASSES):
-            quantise_w2(g, 0, EARLY, tile([P, EARLY], U32, f"w2_codes{g}", f"h{g}")[:])
-        quantise_w2(0, EARLY, N, tile([P, N - EARLY], U32, "w2_codes0_late", f"h{G_PASSES}")[:])
-        make_z(1)
-        make_z(2)
-        late = tile([P, G_PASSES - 1, N - EARLY], U32, "w2_codes_late", f"first{G_PASSES - 1}")
-        for g in range(1, G_PASSES):
-            quantise_w2(g, EARLY, N, late[:, g - 1, :])
+            make_z(g)
+        for g, c in pieces:
+            quantise_w2(g, c)
+
+        acc = [psum.tile([P, P1], F32, name=f"acc{n}", tag=f"bank{n}") for n in range(N_TILES)]
         for n in range(N_TILES):
-            second_product(0, n)
-        for g in range(1, G_PASSES):
-            for n in range(EARLY // P):
-                second_product(g, n)
-        for n in range(EARLY // P, N_TILES):
-            for g in range(1, G_PASSES):
-                second_product(g, n)
+            for g in range(G_PASSES):
+                codes, plane = w2_mx[g, n]
+                nc.tensor.matmul_mx(
+                    out=acc[n][:],
+                    lhsT=codes.bitcast(FP8X4),
+                    lhsT_scale=plane,
+                    rhs=z_codes[g][:].bitcast(FP8X4),
+                    rhs_scale=z_plane[g][:],
+                    start=(g == 0),
+                    stop=(g == G_PASSES - 1),
+                )
 
         def finish(n, rivals):
             least = tile([P, P2], F32, f"least{n}")

@@ -28,6 +28,7 @@ N_TILES = N // P
 BANKS = 8
 PIECE = 256
 LAST_PIECE = 64
+SHARE = 192
 
 
 def tile_list_claim_charting_kernel(
@@ -108,31 +109,30 @@ def tile_list_claim_charting_kernel(
             cols = slice(half * BANK // 16, (half + 1) * BANK // 16)
             nc.vector.tensor_copy(v_w[a, half][:], tab_w[a][:].bitcast(U32).indirect(offs_t[:, cols]))
 
-        w4_codes, w4_planes = {}, {}
+        w4_mx = {}
 
-        def order_w4(g):
-            w4_codes[g] = tile([P, A_PASSES * K_PASS * 2], U8, f"w4_codes{g}")
+        def order_w4(g, t0, t1, codes_tag=None, plane_tag=None):
+            n = t1 - t0
+            codes = tile([P, A_PASSES, n, 2 * P], U8, f"w4_codes{g}_{t0}", codes_tag)
             nc.vector.tensor_copy(
-                w4_codes[g][:].bitcast(I32).rearrange("p (a t q w) -> p a t q w", a=A_PASSES, t=PACK, w=4),
-                w4_raw[g].rearrange("p a (q t w) -> p a t q w", t=PACK, w=4),
+                codes[:].rearrange("p a t c -> p (a t c)").bitcast(I32).rearrange("p (a t q w) -> p a t q w", a=A_PASSES, t=n, w=4),
+                w4_raw[g].rearrange("p a (q t w) -> p a t q w", t=PACK, w=4)[:, :, t0:t1],
             )
-            w4_planes[g] = tile([P, A_PASSES * K_PASS], U8, f"w4_plane{g}")
+            plane = tile([P, A_PASSES, n, P], U8, f"w4_plane{g}_{t0}", plane_tag)
             nc.vector.tensor_copy(
-                w4_planes[g][:].bitcast(I32).rearrange("p (a t q w) -> p a t q w", a=A_PASSES, t=PACK, w=2),
-                w4_plane_raw[:].bitcast(I32).rearrange("p (a g q t w) -> p g a t q w", a=A_PASSES, g=G_PASSES, t=PACK, w=2)[:, g],
+                plane[:].rearrange("p a t c -> p (a t c)").bitcast(I32).rearrange("p (a t q w) -> p a t q w", a=A_PASSES, t=n, w=2),
+                w4_plane_raw[:].bitcast(I32).rearrange("p (a g q t w) -> p g a t q w", a=A_PASSES, g=G_PASSES, t=PACK, w=2)[:, g, :, t0:t1],
             )
+            for t in range(t0, t1):
+                w4_mx[g * PACK + t] = (codes[:, :, t - t0, :], plane[:, :, t - t0, :])
 
         for half in range(HALVES):
             gather_words(0, half)
-        load_w2(0, "stage0")
-        order_w4(0)
+        order_w4(0, 0, 1)
         for half in range(HALVES):
             gather_words(1, half)
-        load_w2(1, "stage1")
-        for g in range(1, G_PASSES):
-            order_w4(g)
-        load_w2(2, "early")
-        coef_t = tile([P, ROW_TILES, 8], F32, "coef_t", "rows_then_identity")
+        order_w4(0, 1, PACK, "rows_then_identity", "stage1")
+        coef_t = tile([P, ROW_TILES, 8], F32, "coef_t", "stage0")
         coef_rows = coef.rearrange("(g q t i o) -> g t q i o", g=G_PASSES, t=PACK, i=8, o=1)
         with nc.allow_non_contiguous_dma(reason="one coefficient for each partition and row tile"):
             for j in range(ROW_TILES):
@@ -145,18 +145,16 @@ def tile_list_claim_charting_kernel(
             return banks[-1]
 
         h = [tile([P, S], F32, f"h{j}") for j in range(ROW_TILES)]
-        first = [tile([P, PACK, P1], F32, f"first{g}") for g in range(G_PASSES)]
 
         def first_product(j, half):
-            g, t = divmod(j, PACK)
+            codes, plane = w4_mx[j]
             cols = slice(half * BANK, (half + 1) * BANK)
             bank = next_bank([P, BANK], f"hb{j}_{half}")
             for a in range(A_PASSES):
-                col = (a * PACK + t) * P
                 nc.tensor.matmul_mx(
                     out=bank[:],
-                    lhsT=w4_codes[g][:, 2 * col : 2 * (col + P)].bitcast(FP4X4),
-                    lhsT_scale=w4_planes[g][:, col : col + P],
+                    lhsT=codes[:, a, :].bitcast(FP4X4),
+                    lhsT_scale=plane[:, a, :],
                     rhs=v_w[a, half][:].bitcast(FP8X4),
                     rhs_scale=v_planes[a][:, cols],
                     start=(a == 0),
@@ -167,7 +165,7 @@ def tile_list_claim_charting_kernel(
         def empty(j, bank, c0, c1):
             nc.scalar.activation(h[j][:, c0:c1], bank[:, c0 % BANK : (c1 - 1) % BANK + 1], ACT.Copy)
 
-        for batch in [[0], [1, 2], [3, 4]] + [[j] for j in range(5, ROW_TILES)]:
+        def empty_tiles(batch):
             cut = S - LAST_PIECE if len(batch) > 1 else S
             for j in batch:
                 empty(j, first_product(j, 0), 0, BANK)
@@ -178,9 +176,6 @@ def tile_list_claim_charting_kernel(
             if cut < S:
                 for j in batch:
                     empty(j, second[j], cut, S)
-        for j in range(ROW_TILES):
-            g, t = divmod(j, PACK)
-            nc.vector.tensor_copy(first[g][:, t, :], h[j][:].indirect(pos1_t[:]))
 
         def woven(view):
             return view.rearrange("p (c i) t -> p c t i", i=4)
@@ -188,57 +183,133 @@ def tile_list_claim_charting_kernel(
         def planar(view):
             return view.rearrange("p t (c i) -> p c t i", i=4)
 
-        x = [tile([P, PACK, P1], F32, f"x{g}", f"v_w{g - 1}_1" if g else None) for g in range(G_PASSES)]
-        for j in range(ROW_TILES):
-            g, t = divmod(j, PACK)
-            nc.vector.tensor_tensor(x[g][:, t, :], h[j][:].indirect(pos2_t[:]), first[g][:, t, :], ALU.add)
+        picked, x, u = {}, {}, {}
 
-        def factor(j):
+        def pick(j, tag=None):
+            picked[j] = tile([P, P1], F32, f"picked{j}", tag)
+            nc.vector.tensor_copy(picked[j][:], h[j][:].indirect(pos1_t[:]))
+
+        def pair(j):
             g, t = divmod(j, PACK)
-            sq = ring.tile([P, P1], F32, name=f"sq{j}", tag="sq")
-            nc.scalar.activation(sq[:], x[g][:, t, :], ACT.Square)
-            nc.scalar.activation(first[g][:, t, :], sq[:], ACT.Identity, bias=1.0, scale=coef_t[:, j, 0:1])
+            if t == 0:
+                x[g] = tile([P, PACK, P1], F32, f"x{g}", ("x0", "x0", "u0")[g])
+            nc.vector.tensor_tensor(x[g][:, t, :], h[j][:].indirect(pos2_t[:]), picked[j][:], ALU.add)
+
+        squares = {}
+
+        def square(j, parts):
+            g, t = divmod(j, PACK)
+            squares[j] = ring.tile([P, P1], F32, name=f"sq{j}", tag="sq")
+            for m in parts:
+                nc.scalar.activation(squares[j][:, m], x[g][:, t, m], ACT.Square)
+
+        def scale_up(j, parts):
+            g, t = divmod(j, PACK)
+            if t == 0:
+                u[g] = tile([P, PACK, P1], F32, f"u{g}", ("u0", "u1", "v_w0_1")[g])
+            for m in parts:
+                nc.scalar.activation(u[g][:, t, m], squares[j][:, m], ACT.Identity, bias=1.0, scale=coef_t[:, j, 0:1])
+
+        def factor(j, between=None):
+            parts = [slice(0, P1)] if between else halves
+            square(j, parts)
+            if between:
+                between()
+            scale_up(j, parts)
+
+        def empty_half(j, half):
+            empty(j, first_product(j, half), half * BANK, (half + 1) * BANK)
 
         rounded = {}
+        pieces = [(g, c) for c in range(N // PIECE) for g in range(G_PASSES)]
 
         def round_w2(g, c):
             rounded[g, c] = tile([P, PIECE, PACK], BF16, f"w2_woven{g}_{c}")
             nc.scalar.copy(woven(rounded[g, c][:]), planar(w2_raw[g][:, :, c * PIECE : (c + 1) * PIECE]))
 
-        pieces = [(g, c) for c in range(N // PIECE) for g in range(G_PASSES)]
-        for j in range(ROW_TILES):
-            factor(j)
-            if ROW_TILES - 4 <= j < ROW_TILES - 2:
-                round_w2(*pieces[len(rounded)])
-        for g, c in pieces[len(rounded) :]:
-            round_w2(g, c)
-
         w2_mx = {}
 
-        def quantise_w2(g, c):
-            codes = tile([P, PIECE], U32, f"w2_codes{g}_{c}")
+        def quantise_w2(g, c, tag=None):
+            codes = tile([P, PIECE], U32, f"w2_codes{g}_{c}", tag)
             plane = tile([P, PIECE], U8, f"w2_plane{g}_{c}")
             nc.vector.quantize_mx(out=codes[:].bitcast(FP8X4), scales=plane[:], in_=rounded[g, c][:].rearrange("p c t -> p (c t)"))
             for n in range(PIECE // P):
                 cols = slice(n * P, (n + 1) * P)
                 w2_mx[g, c * PIECE // P + n] = (codes[:, cols], plane[:, cols])
 
+        z = [tile([P, P1, PACK], BF16, f"z{g}") for g in range(G_PASSES)]
         z_codes = [tile([P, P1], U32, f"z_codes{g}") for g in range(G_PASSES)]
         z_plane = [tile([P, P1], U8, f"z_plane{g}") for g in range(G_PASSES)]
+        halves = [slice(0, P1 // 2), slice(P1 // 2, P1)]
 
-        def make_z(g):
-            z = tile([P, P1, PACK], BF16, f"z{g}", f"h{g}")
-            halves = [slice(0, P1 // 2), slice(P1 // 2, P1)]
-            for m in halves:
-                nc.vector.tensor_tensor(woven(z[:, m, :]), planar(first[g][:, :, m]), planar(x[g][:, :, m]), ALU.mult)
+        def multiply_beside(g, m):
+            nc.gpsimd.tensor_tensor(
+                z[g][:, m, :], u[g][:, :, m].rearrange("p t c -> p c t"), x[g][:, :, m].rearrange("p t c -> p c t"), ALU.mult
+            )
+
+        def multiply(g, m):
+            nc.vector.tensor_tensor(woven(z[g][:, m, :]), planar(u[g][:, :, m]), planar(x[g][:, :, m]), ALU.mult)
+
+        def quantise_z(g):
             for m in halves:
                 nc.vector.quantize_mx(
-                    out=z_codes[g][:, m].bitcast(FP8X4), scales=z_plane[g][:, m], in_=z[:, m, :].rearrange("p c t -> p (c t)")
+                    out=z_codes[g][:, m].bitcast(FP8X4), scales=z_plane[g][:, m], in_=z[g][:, m, :].rearrange("p c t -> p (c t)")
                 )
 
-        for g in range(G_PASSES):
-            make_z(g)
-        for g, c in pieces:
+        empty_tiles([0])
+        order_w4(1, 0, PACK, "w4_codes0_0", "w4_plane0_0")
+        empty_tiles([1, 2])
+        empty_tiles([3])
+        pick(0)
+        pair(0)
+        pick(1)
+        pick(2)
+        pair(1)
+        pick(3)
+        order_w4(2, 0, PACK, "picked0", "h0")
+        pair(2)
+        pair(3)
+        load_w2(0, "early")
+        load_w2(1, "w4_plane_raw")
+        factor(0, lambda: empty_half(4, 0))
+        empty_half(4, 1)
+        empty_tiles([5])
+        factor(1, lambda: empty_half(6, 0))
+        empty_half(6, 1)
+        factor(2)
+        factor(3)
+        for j in range(7, ROW_TILES):
+            empty_tiles([j])
+        load_w2(2, "v_w0_0")
+        multiply_beside(0, slice(0, P1))
+        round_w2(*pieces[0])
+        for j, tag in zip(range(4, 10), ("picked2", "picked3", "h2", "h3", None, None)):
+            pick(j, tag)
+        pair(4)
+        quantise_z(0)
+        for j in range(5, 10):
+            pair(j)
+        for j in range(4, 10):
+            factor(j)
+        multiply_beside(1, slice(0, SHARE))
+        for j in range(10, ROW_TILES):
+            pick(j, f"h{j - 4}")
+        for j in range(10, ROW_TILES):
+            pair(j)
+        for g, c in pieces[1:G_PASSES]:
+            round_w2(g, c)
+        for j in range(10, ROW_TILES):
+            factor(j)
+        for g, c in pieces[G_PASSES:]:
+            round_w2(g, c)
+        multiply(1, slice(SHARE, P1))
+        for g, c in pieces[:G_PASSES]:
+            quantise_w2(g, c, ("picked11", "h10", "h11")[g])
+        quantise_z(1)
+        for m in halves:
+            multiply(2, m)
+        quantise_z(2)
+        for g, c in pieces[G_PASSES:]:
             quantise_w2(g, c)
 
         acc = [psum.tile([P, P1], F32, name=f"acc{n}", tag=f"bank{n}") for n in range(N_TILES)]
@@ -256,13 +327,13 @@ def tile_list_claim_charting_kernel(
                 )
 
         def finish(n, rivals):
-            least = tile([P, P2], F32, f"least{n}")
+            least = tile([P, P2], F32, f"least{n}", f"h{4 + n}")
             nc.vector.tensor_tensor(least[:], rivals[:, 0, :], rivals[:, 1, :], ALU.min)
             nc.sync.dma_start(out[n * P : (n + 1) * P, :], least[:])
 
         waiting = None
         for n in range(N_TILES):
-            y = tile([P, P1], F32, f"y{n}", f"h{PACK + n}")
+            y = tile([P, P1], F32, f"y{n}", f"picked{4 + n}")
             nc.scalar.activation(y[:], acc[n][:], ACT.Copy)
             rivals = ring.tile([P, 2, P2], F32, name=f"rivals{n}", tag="rivals", bufs=3, align_bytes=64)
             nc.vector.tensor_copy(rivals[:, 0, :], y[:].indirect(pos3_t[:]))

@@ -243,9 +243,7 @@ def tile_list_claim_charting_kernel(
         halves = [slice(0, P1 // 2), slice(P1 // 2, P1)]
 
         def multiply_beside(g, m):
-            nc.gpsimd.tensor_tensor(
-                z[g][:, m, :], u[g][:, :, m].rearrange("p t c -> p c t"), x[g][:, :, m].rearrange("p t c -> p c t"), ALU.mult
-            )
+            nc.gpsimd.tensor_tensor(woven(z[g][:, m, :]), planar(u[g][:, :, m]), planar(x[g][:, :, m]), ALU.mult)
 
         def multiply(g, m):
             nc.vector.tensor_tensor(woven(z[g][:, m, :]), planar(u[g][:, :, m]), planar(x[g][:, :, m]), ALU.mult)

@@ -27,8 +27,8 @@ HALVES = S // BANK
 N_TILES = N // P
 BANKS = 8
 PIECE = 256
-LAST_PIECE = 64
-SHARE = 192
+SHORT = 128
+SHARE = 384
 
 
 def tile_list_claim_charting_kernel(
@@ -96,18 +96,22 @@ def tile_list_claim_charting_kernel(
 
         w2_raw = {}
 
-        def load_w2(g, tag):
-            w2_raw[g] = tile([P, PACK, N], F32, f"w2_raw{g}", tag)
-            rows = w2[K_PASS * g : K_PASS * (g + 1), :].rearrange("(q t i) n -> t q i n", t=PACK, i=8)
+        def load_w2(g, c0, c1, tag):
+            raw = tile([P, PACK, (c1 - c0) * PIECE], F32, f"w2_raw{g}_{c0}", tag)
+            rows = w2[K_PASS * g : K_PASS * (g + 1), c0 * PIECE : c1 * PIECE].rearrange("(q t i) n -> t q i n", t=PACK, i=8)
             for t in range(PACK):
-                nc.sync.dma_start(w2_raw[g][:, t, :], rows[t])
+                nc.sync.dma_start(raw[:, t, :], rows[t])
+            for c in range(c0, c1):
+                w2_raw[g, c] = raw[:, :, (c - c0) * PIECE : (c - c0 + 1) * PIECE]
 
         v_w = {}
 
-        def gather_words(a, half):
-            v_w[a, half] = tile([P, BANK], U32, f"v_w{a}_{half}")
-            cols = slice(half * BANK // 16, (half + 1) * BANK // 16)
-            nc.vector.tensor_copy(v_w[a, half][:], tab_w[a][:].bitcast(U32).indirect(offs_t[:, cols]))
+        def gather_words(a, half0, half1):
+            words = tile([P, (half1 - half0) * BANK], U32, f"v_w{a}_{half0}")
+            cols = slice(half0 * BANK // 16, half1 * BANK // 16)
+            nc.vector.tensor_copy(words[:], tab_w[a][:].bitcast(U32).indirect(offs_t[:, cols]))
+            for half in range(half0, half1):
+                v_w[a, half] = words[:, (half - half0) * BANK : (half - half0 + 1) * BANK]
 
         w4_mx = {}
 
@@ -126,17 +130,19 @@ def tile_list_claim_charting_kernel(
             for t in range(t0, t1):
                 w4_mx[g * PACK + t] = (codes[:, :, t - t0, :], plane[:, :, t - t0, :])
 
-        for half in range(HALVES):
-            gather_words(0, half)
+        gather_words(0, 0, HALVES)
+        load_w2(0, 0, 2, "stage0")
         order_w4(0, 0, 1)
         for half in range(HALVES):
-            gather_words(1, half)
-        order_w4(0, 1, PACK, "rows_then_identity", "stage1")
-        coef_t = tile([P, ROW_TILES, 8], F32, "coef_t", "stage0")
+            gather_words(1, half, half + 1)
+        order_w4(0, 1, PACK, "rows_then_identity")
+        coef_t = tile([P, ROW_TILES, 8], F32, "coef_t", "stage1")
         coef_rows = coef.rearrange("(g q t i o) -> g t q i o", g=G_PASSES, t=PACK, i=8, o=1)
         with nc.allow_non_contiguous_dma(reason="one coefficient for each partition and row tile"):
             for j in range(ROW_TILES):
                 nc.sync.dma_start(coef_t[:, j, 0:1], coef_rows[j // PACK, j % PACK])
+
+        load_w2(0, 2, 3, "w4_first")
 
         banks = []
 
@@ -155,7 +161,7 @@ def tile_list_claim_charting_kernel(
                     out=bank[:],
                     lhsT=codes[:, a, :].bitcast(FP4X4),
                     lhsT_scale=plane[:, a, :],
-                    rhs=v_w[a, half][:].bitcast(FP8X4),
+                    rhs=v_w[a, half].bitcast(FP8X4),
                     rhs_scale=v_planes[a][:, cols],
                     start=(a == 0),
                     stop=(a == A_PASSES - 1),
@@ -165,17 +171,9 @@ def tile_list_claim_charting_kernel(
         def empty(j, bank, c0, c1):
             nc.scalar.activation(h[j][:, c0:c1], bank[:, c0 % BANK : (c1 - 1) % BANK + 1], ACT.Copy)
 
-        def empty_tiles(batch):
-            cut = S - LAST_PIECE if len(batch) > 1 else S
-            for j in batch:
-                empty(j, first_product(j, 0), 0, BANK)
-            second = {}
-            for j in batch:
-                second[j] = first_product(j, 1)
-                empty(j, second[j], BANK, cut)
-            if cut < S:
-                for j in batch:
-                    empty(j, second[j], cut, S)
+        def empty_tile(j):
+            for half in range(HALVES):
+                empty(j, first_product(j, half), half * BANK, (half + 1) * BANK)
 
         def woven(view):
             return view.rearrange("p (c i) t -> p c t i", i=4)
@@ -192,10 +190,12 @@ def tile_list_claim_charting_kernel(
         def pair(j):
             g, t = divmod(j, PACK)
             if t == 0:
-                x[g] = tile([P, PACK, P1], F32, f"x{g}", ("x0", "x0", "u0")[g])
+                x[g] = tile([P, PACK, P1], F32, f"x{g}", ("w4_codes0_0", "w4_codes0_0", "u0")[g])
             nc.vector.tensor_tensor(x[g][:, t, :], h[j][:].indirect(pos2_t[:]), picked[j][:], ALU.add)
 
         squares = {}
+        halves = [slice(0, P1 // 2), slice(P1 // 2, P1)]
+        whole = [slice(0, P1)]
 
         def square(j, parts):
             g, t = divmod(j, PACK)
@@ -206,12 +206,11 @@ def tile_list_claim_charting_kernel(
         def scale_up(j, parts):
             g, t = divmod(j, PACK)
             if t == 0:
-                u[g] = tile([P, PACK, P1], F32, f"u{g}", ("u0", "u1", "v_w0_1")[g])
+                u[g] = tile([P, PACK, P1], F32, f"u{g}", ("u0", "u1", "v_w0_0")[g])
             for m in parts:
                 nc.scalar.activation(u[g][:, t, m], squares[j][:, m], ACT.Identity, bias=1.0, scale=coef_t[:, j, 0:1])
 
-        def factor(j, between=None):
-            parts = [slice(0, P1)] if between else halves
+        def factor(j, between=None, parts=halves):
             square(j, parts)
             if between:
                 between()
@@ -225,7 +224,11 @@ def tile_list_claim_charting_kernel(
 
         def round_w2(g, c):
             rounded[g, c] = tile([P, PIECE, PACK], BF16, f"w2_woven{g}_{c}")
-            nc.scalar.copy(woven(rounded[g, c][:]), planar(w2_raw[g][:, :, c * PIECE : (c + 1) * PIECE]))
+            nc.scalar.copy(woven(rounded[g, c][:]), planar(w2_raw[g, c]))
+
+        def round_beside(g, c, tag=None):
+            rounded[g, c] = tile([P, PIECE, PACK], BF16, f"w2_woven{g}_{c}", tag)
+            nc.gpsimd.tensor_scalar(rounded[g, c][:], w2_raw[g, c].rearrange("p t c -> p c t"), 1.0, 0.0, ALU.mult, ALU.add)
 
         w2_mx = {}
 
@@ -240,7 +243,6 @@ def tile_list_claim_charting_kernel(
         z = [tile([P, P1, PACK], BF16, f"z{g}") for g in range(G_PASSES)]
         z_codes = [tile([P, P1], U32, f"z_codes{g}") for g in range(G_PASSES)]
         z_plane = [tile([P, P1], U8, f"z_plane{g}") for g in range(G_PASSES)]
-        halves = [slice(0, P1 // 2), slice(P1 // 2, P1)]
 
         def multiply_beside(g, m):
             nc.gpsimd.tensor_tensor(woven(z[g][:, m, :]), planar(u[g][:, :, m]), planar(x[g][:, :, m]), ALU.mult)
@@ -248,67 +250,67 @@ def tile_list_claim_charting_kernel(
         def multiply(g, m):
             nc.vector.tensor_tensor(woven(z[g][:, m, :]), planar(u[g][:, :, m]), planar(x[g][:, :, m]), ALU.mult)
 
-        def quantise_z(g):
-            for m in halves:
+        def quantise_z(g, parts):
+            for m in parts:
                 nc.vector.quantize_mx(
                     out=z_codes[g][:, m].bitcast(FP8X4), scales=z_plane[g][:, m], in_=z[g][:, m, :].rearrange("p c t -> p (c t)")
                 )
 
-        empty_tiles([0])
+        empty_tile(0)
         order_w4(1, 0, PACK, "w4_codes0_0", "w4_plane0_0")
-        empty_tiles([1, 2])
-        empty_tiles([3])
-        pick(0)
-        pair(0)
-        pick(1)
-        pick(2)
-        pair(1)
-        pick(3)
-        order_w4(2, 0, PACK, "picked0", "h0")
-        pair(2)
-        pair(3)
-        load_w2(0, "early")
-        load_w2(1, "w4_plane_raw")
-        factor(0, lambda: empty_half(4, 0))
-        empty_half(4, 1)
-        empty_tiles([5])
-        factor(1, lambda: empty_half(6, 0))
-        empty_half(6, 1)
+        for j in range(1, 6):
+            empty_tile(j)
+        round_beside(0, 0)
+        round_beside(0, 1)
+        for j in range(PACK):
+            pick(j)
+        for j in range(PACK):
+            pair(j)
+        order_w4(2, 0, PACK, "h0", "picked0")
+        load_w2(1, 0, 3, "early")
+        load_w2(2, 0, 3, "w4_plane_raw")
+        empty_half(6, 0)
+        factor(0, lambda: empty_half(6, 1), whole)
+        factor(1)
         factor(2)
-        factor(3)
-        for j in range(7, ROW_TILES):
-            empty_tiles([j])
-        load_w2(2, "v_w0_0")
+        bank = first_product(7, 0)
+        factor(3, lambda: empty(7, bank, 0, SHORT))
+        empty(7, bank, SHORT, BANK)
+        empty_half(7, 1)
+        for j in range(8, ROW_TILES):
+            empty_tile(j)
+        round_beside(0, 2, "h2")
         multiply_beside(0, slice(0, P1))
-        round_w2(*pieces[0])
-        for j, tag in zip(range(4, 10), ("picked2", "picked3", "h2", "h3", None, None)):
+        later = [piece for piece in pieces if piece[0]]
+        round_w2(*later[0])
+        for j, tag in zip(range(4, 9), ("picked2", "picked3", "picked1", "h1", "h3")):
             pick(j, tag)
         pair(4)
-        quantise_z(0)
-        for j in range(5, 10):
+        quantise_z(0, whole)
+        for j in range(5, 9):
             pair(j)
-        for j in range(4, 10):
+        for j in range(4, 9):
             factor(j)
         multiply_beside(1, slice(0, SHARE))
-        for j in range(10, ROW_TILES):
+        for j in range(9, ROW_TILES):
             pick(j, f"h{j - 4}")
-        for j in range(10, ROW_TILES):
+        for j in range(9, ROW_TILES):
             pair(j)
-        for g, c in pieces[1:G_PASSES]:
+        for g, c in later[1:4]:
             round_w2(g, c)
-        for j in range(10, ROW_TILES):
+        for j in range(9, ROW_TILES):
             factor(j)
-        for g, c in pieces[G_PASSES:]:
+        for g, c in later[4:]:
             round_w2(g, c)
         multiply(1, slice(SHARE, P1))
-        for g, c in pieces[:G_PASSES]:
-            quantise_w2(g, c, ("picked11", "h10", "h11")[g])
-        quantise_z(1)
+        for (g, c), tag in zip(pieces[:G_PASSES], ("h9", "h10", "h11")):
+            quantise_w2(g, c, tag)
+        quantise_z(1, halves)
         for m in halves:
             multiply(2, m)
-        quantise_z(2)
-        for g, c in pieces[G_PASSES:]:
-            quantise_w2(g, c)
+        quantise_z(2, halves)
+        for (g, c), tag in zip(pieces[G_PASSES:], ("u0", "u1", "v_w0_0", "z0", "z1", None)):
+            quantise_w2(g, c, tag)
 
         acc = [psum.tile([P, P1], F32, name=f"acc{n}", tag=f"bank{n}") for n in range(N_TILES)]
         for n in range(N_TILES):
@@ -325,13 +327,13 @@ def tile_list_claim_charting_kernel(
                 )
 
         def finish(n, rivals):
-            least = tile([P, P2], F32, f"least{n}", f"h{4 + n}")
+            least = tile([P, P2], F32, f"least{n}")
             nc.vector.tensor_tensor(least[:], rivals[:, 0, :], rivals[:, 1, :], ALU.min)
             nc.sync.dma_start(out[n * P : (n + 1) * P, :], least[:])
 
         waiting = None
         for n in range(N_TILES):
-            y = tile([P, P1], F32, f"y{n}", f"picked{4 + n}")
+            y = tile([P, P1], F32, f"y{n}", f"y{n}")
             nc.scalar.activation(y[:], acc[n][:], ACT.Copy)
             rivals = ring.tile([P, 2, P2], F32, name=f"rivals{n}", tag="rivals", bufs=3, align_bytes=64)
             nc.vector.tensor_copy(rivals[:, 0, :], y[:].indirect(pos3_t[:]))

@@ -28,7 +28,7 @@ N_TILES = N // P
 BANKS = 8
 PIECE = 256
 SHORT = 128
-SHARE = 384
+SHARE = 352
 
 
 def tile_list_claim_charting_kernel(
@@ -58,7 +58,7 @@ def tile_list_claim_charting_kernel(
         nc.gpsimd.memset(w4_plane_raw[:].bitcast(I32), 0)
 
         offs_t = load_list(offs, "offs_t")
-        nc.sync.dma_start(tab_plane[rows0:P, :].bitcast(I32), tab_scales.rearrange("a q t -> (a q) t").bitcast(I32))
+        nc.scalar.dma_start(tab_plane[rows0:P, :].bitcast(I32), tab_scales.rearrange("a q t -> (a q) t").bitcast(I32))
         tab_w = [tile([P, T], I32, f"tab_w{a}", f"stage{a}") for a in range(A_PASSES)]
 
         def load_tab(a):
@@ -131,18 +131,15 @@ def tile_list_claim_charting_kernel(
                 w4_mx[g * PACK + t] = (codes[:, :, t - t0, :], plane[:, :, t - t0, :])
 
         gather_words(0, 0, HALVES)
-        load_w2(0, 0, 2, "stage0")
         order_w4(0, 0, 1)
         for half in range(HALVES):
             gather_words(1, half, half + 1)
         order_w4(0, 1, PACK, "rows_then_identity")
-        coef_t = tile([P, ROW_TILES, 8], F32, "coef_t", "stage1")
+        coef_t = tile([P, ROW_TILES, 8], F32, "coef_t", "stage0")
         coef_rows = coef.rearrange("(g q t i o) -> g t q i o", g=G_PASSES, t=PACK, i=8, o=1)
         with nc.allow_non_contiguous_dma(reason="one coefficient for each partition and row tile"):
             for j in range(ROW_TILES):
                 nc.sync.dma_start(coef_t[:, j, 0:1], coef_rows[j // PACK, j % PACK])
-
-        load_w2(0, 2, 3, "w4_first")
 
         banks = []
 
@@ -184,14 +181,12 @@ def tile_list_claim_charting_kernel(
         picked, x, u = {}, {}, {}
 
         def pick(j, tag=None):
-            picked[j] = tile([P, P1], F32, f"picked{j}", tag)
-            nc.vector.tensor_copy(picked[j][:], h[j][:].indirect(pos1_t[:]))
+            picked[j] = x[2][:, 0, :] if j == 2 * PACK - 1 else tile([P, P1], F32, f"picked{j}", tag)[:]
+            nc.vector.tensor_copy(picked[j], h[j][:].indirect(pos1_t[:]))
 
         def pair(j):
             g, t = divmod(j, PACK)
-            if t == 0:
-                x[g] = tile([P, PACK, P1], F32, f"x{g}", ("w4_codes0_0", "w4_codes0_0", "u0")[g])
-            nc.vector.tensor_tensor(x[g][:, t, :], h[j][:].indirect(pos2_t[:]), picked[j][:], ALU.add)
+            nc.vector.tensor_tensor(x[g][:, t, :], h[j][:].indirect(pos2_t[:]), picked[j], ALU.add)
 
         squares = {}
         halves = [slice(0, P1 // 2), slice(P1 // 2, P1)]
@@ -226,10 +221,6 @@ def tile_list_claim_charting_kernel(
             rounded[g, c] = tile([P, PIECE, PACK], BF16, f"w2_woven{g}_{c}")
             nc.scalar.copy(woven(rounded[g, c][:]), planar(w2_raw[g, c]))
 
-        def round_beside(g, c, tag=None):
-            rounded[g, c] = tile([P, PIECE, PACK], BF16, f"w2_woven{g}_{c}", tag)
-            nc.gpsimd.tensor_scalar(rounded[g, c][:], w2_raw[g, c].rearrange("p t c -> p c t"), 1.0, 0.0, ALU.mult, ALU.add)
-
         w2_mx = {}
 
         def quantise_w2(g, c, tag=None):
@@ -260,60 +251,69 @@ def tile_list_claim_charting_kernel(
         order_w4(1, 0, PACK, "w4_codes0_0", "w4_plane0_0")
         for j in range(1, 6):
             empty_tile(j)
-        round_beside(0, 0)
-        round_beside(0, 1)
+        empty_half(6, 0)
+        late_bank = first_product(6, 1)
+        next_banks = [first_product(7, half) for half in range(HALVES)]
+        sums = tile([P, PACK + 1, P1], F32, "sums", "w4_codes0_0")
+        x[0] = sums[:, 1:, :]
+        x[1] = sums[:, :PACK, :]
+        x[2] = tile([P, PACK, P1], F32, "last_sums")[:]
         for j in range(PACK):
             pick(j)
-        for j in range(PACK):
-            pair(j)
+        pair(0)
+        pair(1)
+        pick(4)
+        pair(2)
+        pair(3)
         order_w4(2, 0, PACK, "h0", "picked0")
+        pair(4)
+        load_w2(0, 0, 3, "stage1")
         load_w2(1, 0, 3, "early")
         load_w2(2, 0, 3, "w4_plane_raw")
-        empty_half(6, 0)
-        factor(0, lambda: empty_half(6, 1), whole)
+        factor(0, lambda: empty(6, late_bank, BANK, S), whole)
         factor(1)
         factor(2)
-        bank = first_product(7, 0)
-        factor(3, lambda: empty(7, bank, 0, SHORT))
-        empty(7, bank, SHORT, BANK)
-        empty_half(7, 1)
-        for j in range(8, ROW_TILES):
+        factor(3, lambda: empty(7, next_banks[0], 0, SHORT))
+        empty(7, next_banks[0], SHORT, BANK)
+        empty(7, next_banks[1], BANK, S)
+        empty_tile(8)
+        factor(4)
+        for j in range(9, ROW_TILES):
             empty_tile(j)
-        round_beside(0, 2, "h2")
+        round_w2(*pieces[0])
         multiply_beside(0, slice(0, P1))
-        later = [piece for piece in pieces if piece[0]]
-        round_w2(*later[0])
-        for j, tag in zip(range(4, 9), ("picked2", "picked3", "picked1", "h1", "h3")):
-            pick(j, tag)
-        pair(4)
-        quantise_z(0, whole)
         for j in range(5, 9):
+            pick(j)
+        for j in range(5, 8):
             pair(j)
-        for j in range(4, 9):
+        quantise_z(0, whole)
+        pair(8)
+        for j in range(5, 9):
             factor(j)
         multiply_beside(1, slice(0, SHARE))
         for j in range(9, ROW_TILES):
             pick(j, f"h{j - 4}")
-        for j in range(9, ROW_TILES):
-            pair(j)
-        for g, c in later[1:4]:
+        for g, c in pieces[1:5]:
             round_w2(g, c)
         for j in range(9, ROW_TILES):
+            pair(j)
+        for j in range(9, ROW_TILES):
             factor(j)
-        for g, c in later[4:]:
+        for g, c in pieces[5:-1]:
             round_w2(g, c)
         multiply(1, slice(SHARE, P1))
         for (g, c), tag in zip(pieces[:G_PASSES], ("h9", "h10", "h11")):
             quantise_w2(g, c, tag)
-        quantise_z(1, halves)
+        quantise_z(1, whole)
         for m in halves:
             multiply(2, m)
         quantise_z(2, halves)
-        for (g, c), tag in zip(pieces[G_PASSES:], ("u0", "u1", "v_w0_0", "z0", "z1", None)):
+        for (g, c), tag in zip(pieces[G_PASSES:-1], ("v_w0_0", "last_sums", None, None, None)):
             quantise_w2(g, c, tag)
 
         acc = [psum.tile([P, P1], F32, name=f"acc{n}", tag=f"bank{n}") for n in range(N_TILES)]
-        for n in range(N_TILES):
+
+        def second_product(n):
             for g in range(G_PASSES):
                 codes, plane = w2_mx[g, n]
                 nc.tensor.matmul_mx(
@@ -326,19 +326,35 @@ def tile_list_claim_charting_kernel(
                     stop=(g == G_PASSES - 1),
                 )
 
-        def finish(n, rivals):
+        y, rivals = {}, {}
+
+        def empty_second(n):
+            second_product(n)
+            y[n] = tile([P, P1], F32, f"y{n}", f"y{n}")
+            nc.scalar.activation(y[n][:], acc[n][:], ACT.Copy)
+
+        def finish(n):
             least = tile([P, P2], F32, f"least{n}")
-            nc.vector.tensor_tensor(least[:], rivals[:, 0, :], rivals[:, 1, :], ALU.min)
+            nc.vector.tensor_tensor(least[:], rivals[n][:, 0, :], rivals[n][:, 1, :], ALU.min)
             nc.sync.dma_start(out[n * P : (n + 1) * P, :], least[:])
 
-        waiting = None
-        for n in range(N_TILES):
-            y = tile([P, P1], F32, f"y{n}", f"y{n}")
-            nc.scalar.activation(y[:], acc[n][:], ACT.Copy)
-            rivals = ring.tile([P, 2, P2], F32, name=f"rivals{n}", tag="rivals", bufs=3, align_bytes=64)
-            nc.vector.tensor_copy(rivals[:, 0, :], y[:].indirect(pos3_t[:]))
-            if waiting:
-                finish(*waiting)
-            nc.vector.tensor_copy(rivals[:, 1, :], y[:].indirect(pos4_t[:]))
-            waiting = (n, rivals)
-        finish(*waiting)
+        def pick_rivals(n):
+            rivals[n] = ring.tile([P, 2, P2], F32, name=f"rivals{n}", tag="rivals", bufs=3, align_bytes=64)
+            nc.vector.tensor_copy(rivals[n][:, 0, :], y[n][:].indirect(pos3_t[:]))
+            if n:
+                finish(n - 1)
+            nc.vector.tensor_copy(rivals[n][:, 1, :], y[n][:].indirect(pos4_t[:]))
+
+        empty_second(0)
+        empty_second(1)
+        round_w2(*pieces[-1])
+        empty_second(2)
+        empty_second(3)
+        pick_rivals(0)
+        pick_rivals(1)
+        quantise_w2(*pieces[-1], "y0")
+        empty_second(4)
+        empty_second(5)
+        for n in range(2, N_TILES):
+            pick_rivals(n)
+        finish(N_TILES - 1)

@@ -28,7 +28,7 @@ N_TILES = N // P
 BANKS = 8
 PIECE = 256
 SHORT = 128
-SHARE = 352
+SHARES = (256, 272)
 
 
 def tile_list_claim_charting_kernel(
@@ -71,11 +71,11 @@ def tile_list_claim_charting_kernel(
             return [raw[:, :, (g - g0) * K_PASS // 2 : (g - g0 + 1) * K_PASS // 2] for g in range(g0, g1)]
 
         load_tab(0)
+        w4_raw = load_w4(0, 1, "w4_first")
         pos1_t = load_list(pos1, "pos1_t")
         pos2_t = load_list(pos2, "pos2_t")
         pos3_t = load_list(pos3, "pos3_t")
         pos4_t = load_list(pos4, "pos4_t")
-        w4_raw = load_w4(0, 1, "w4_first")
         load_tab(1)
         for q in range(4):
             nc.gpsimd.dma_start(
@@ -106,36 +106,41 @@ def tile_list_claim_charting_kernel(
 
         v_w = {}
 
-        def gather_words(a, half0, half1):
+        def gather_words(a, half0, half1, step):
             words = tile([P, (half1 - half0) * BANK], U32, f"v_w{a}_{half0}")
-            cols = slice(half0 * BANK // 16, half1 * BANK // 16)
-            nc.vector.tensor_copy(words[:], tab_w[a][:].bitcast(U32).indirect(offs_t[:, cols]))
+            for c in range(0, (half1 - half0) * BANK, step):
+                cols = slice((half0 * BANK + c) // 16, (half0 * BANK + c + step) // 16)
+                nc.vector.tensor_copy(words[:, c : c + step], tab_w[a][:].bitcast(U32).indirect(offs_t[:, cols]))
             for half in range(half0, half1):
                 v_w[a, half] = words[:, (half - half0) * BANK : (half - half0 + 1) * BANK]
 
-        w4_mx = {}
+        w4_codes = {}
 
-        def order_w4(g, t0, t1, codes_tag=None, plane_tag=None):
+        def order_w4(engine, g, t0, t1, tag=None):
             n = t1 - t0
-            codes = tile([P, A_PASSES, n, 2 * P], U8, f"w4_codes{g}_{t0}", codes_tag)
-            nc.vector.tensor_copy(
+            codes = tile([P, A_PASSES, n, 2 * P], U8, f"w4_codes{g}_{t0}", tag)
+            engine.tensor_copy(
                 codes[:].rearrange("p a t c -> p (a t c)").bitcast(I32).rearrange("p (a t q w) -> p a t q w", a=A_PASSES, t=n, w=4),
                 w4_raw[g].rearrange("p a (q t w) -> p a t q w", t=PACK, w=4)[:, :, t0:t1],
             )
-            plane = tile([P, A_PASSES, n, P], U8, f"w4_plane{g}_{t0}", plane_tag)
-            nc.vector.tensor_copy(
-                plane[:].rearrange("p a t c -> p (a t c)").bitcast(I32).rearrange("p (a t q w) -> p a t q w", a=A_PASSES, t=n, w=2),
-                w4_plane_raw[:].bitcast(I32).rearrange("p (a g q t w) -> p g a t q w", a=A_PASSES, g=G_PASSES, t=PACK, w=2)[:, g, :, t0:t1],
-            )
             for t in range(t0, t1):
-                w4_mx[g * PACK + t] = (codes[:, :, t - t0, :], plane[:, :, t - t0, :])
+                w4_codes[g * PACK + t] = codes[:, :, t - t0, :]
 
-        gather_words(0, 0, HALVES)
-        order_w4(0, 0, 1)
-        for half in range(HALVES):
-            gather_words(1, half, half + 1)
-        order_w4(0, 1, PACK, "rows_then_identity")
-        coef_t = tile([P, ROW_TILES, 8], F32, "coef_t", "stage0")
+        gather_words(0, 0, HALVES, S)
+        load_w2(0, 0, 1, "stage0")
+        order_w4(nc.gpsimd, 0, 0, 1)
+        w4_planes = []
+        for g in range(G_PASSES):
+            w4_planes.append(tile([P, A_PASSES, PACK, P], U8, f"w4_plane{g}"))
+            nc.gpsimd.tensor_copy(
+                w4_planes[g][:].rearrange("p a t c -> p (a t c)").bitcast(I32).rearrange("p (a t q w) -> p a t q w", a=A_PASSES, t=PACK, w=2),
+                w4_plane_raw[:].bitcast(I32).rearrange("p (a g q t w) -> p g a t q w", a=A_PASSES, g=G_PASSES, t=PACK, w=2)[:, g],
+            )
+        load_w2(0, 1, 2, "w4_plane_raw")
+        gather_words(1, 0, 1, BANK)
+        gather_words(1, 1, 2, BANK // 2)
+        order_w4(nc.vector, 0, 1, PACK, "rows_then_identity")
+        coef_t = tile([P, ROW_TILES, 8], F32, "coef_t", "stage1")
         coef_rows = coef.rearrange("(g q t i o) -> g t q i o", g=G_PASSES, t=PACK, i=8, o=1)
         with nc.allow_non_contiguous_dma(reason="one coefficient for each partition and row tile"):
             for j in range(ROW_TILES):
@@ -150,7 +155,7 @@ def tile_list_claim_charting_kernel(
         h = [tile([P, S], F32, f"h{j}") for j in range(ROW_TILES)]
 
         def first_product(j, half):
-            codes, plane = w4_mx[j]
+            codes, plane = w4_codes[j], w4_planes[j // PACK][:, :, j % PACK, :]
             cols = slice(half * BANK, (half + 1) * BANK)
             bank = next_bank([P, BANK], f"hb{j}_{half}")
             for a in range(A_PASSES):
@@ -164,6 +169,22 @@ def tile_list_claim_charting_kernel(
                     stop=(a == A_PASSES - 1),
                 )
             return bank
+
+        def narrow_product(j, c0, c1):
+            codes, plane = w4_codes[j], w4_planes[j // PACK][:, :, j % PACK, :]
+            bank = next_bank([P, c1 - c0], f"hb{j}_{c0}")
+            for a in range(A_PASSES):
+                for c in range(c0, c1, P):
+                    nc.tensor.matmul_mx(
+                        out=bank[:, c - c0 : c - c0 + P],
+                        lhsT=codes[:, a, :].bitcast(FP4X4),
+                        lhsT_scale=plane[:, a, :],
+                        rhs=v_w[a, c // BANK][:, c % BANK : c % BANK + P].bitcast(FP8X4),
+                        rhs_scale=v_planes[a][:, c : c + P],
+                        start=(a == 0 and c == c0),
+                        stop=(a == A_PASSES - 1 and c + P == c1),
+                    )
+            nc.scalar.activation(h[j][:, c0:c1], bank[:], ACT.Copy)
 
         def empty(j, bank, c0, c1):
             nc.scalar.activation(h[j][:, c0:c1], bank[:, c0 % BANK : (c1 - 1) % BANK + 1], ACT.Copy)
@@ -191,22 +212,32 @@ def tile_list_claim_charting_kernel(
         squares = {}
         halves = [slice(0, P1 // 2), slice(P1 // 2, P1)]
         whole = [slice(0, P1)]
+        cuts = [[slice(0, share), slice(share, P1)] for share in SHARES] + [halves]
 
         def square(j, parts):
             g, t = divmod(j, PACK)
-            squares[j] = ring.tile([P, P1], F32, name=f"sq{j}", tag="sq")
+            if j in (2 * PACK - 1, ROW_TILES - 1):
+                squares[j] = tile([P, P1], F32, f"sq{j}")
+            else:
+                squares[j] = ring.tile([P, P1], F32, name=f"sq{j}", tag="sq")
             for m in parts:
                 nc.scalar.activation(squares[j][:, m], x[g][:, t, m], ACT.Square)
 
         def scale_up(j, parts):
             g, t = divmod(j, PACK)
-            if t == 0:
-                u[g] = tile([P, PACK, P1], F32, f"u{g}", ("u0", "u1", "v_w0_0")[g])
+            if t == 0 and g == 0:
+                for m in parts:
+                    u[g, m.start] = tile([P, PACK, m.stop - m.start], F32, f"u{g}_{m.start}")[:]
+            elif t == 0:
+                whole_u = tile([P, PACK, P1], F32, f"u{g}", ("u1", "v_w0_0")[g - 1])
+                for m in parts:
+                    u[g, m.start] = whole_u[:, :, m]
             for m in parts:
-                nc.scalar.activation(u[g][:, t, m], squares[j][:, m], ACT.Identity, bias=1.0, scale=coef_t[:, j, 0:1])
+                nc.scalar.activation(u[g, m.start][:, t, :], squares[j][:, m], ACT.Identity, bias=1.0, scale=coef_t[:, j, 0:1])
 
-        def factor(j, between=None, parts=halves):
-            square(j, parts)
+        def factor(j, between=None):
+            parts = cuts[j // PACK]
+            square(j, whole if between and j == 0 else parts)
             if between:
                 between()
             scale_up(j, parts)
@@ -215,46 +246,53 @@ def tile_list_claim_charting_kernel(
             empty(j, first_product(j, half), half * BANK, (half + 1) * BANK)
 
         rounded = {}
-        pieces = [(g, c) for c in range(N // PIECE) for g in range(G_PASSES)]
+
+        def make_room(some, tag):
+            room = tile([P, len(some), PIECE, PACK], BF16, f"w2_woven_{tag}", tag)
+            for i, piece in enumerate(some):
+                rounded[piece] = room[:, i]
+            return room
 
         def round_w2(g, c):
-            rounded[g, c] = tile([P, PIECE, PACK], BF16, f"w2_woven{g}_{c}")
-            nc.scalar.copy(woven(rounded[g, c][:]), planar(w2_raw[g, c]))
+            nc.scalar.copy(woven(rounded[g, c]), planar(w2_raw[g, c]))
 
         w2_mx = {}
 
-        def quantise_w2(g, c, tag=None):
-            codes = tile([P, PIECE], U32, f"w2_codes{g}_{c}", tag)
-            plane = tile([P, PIECE], U8, f"w2_plane{g}_{c}")
-            nc.vector.quantize_mx(out=codes[:].bitcast(FP8X4), scales=plane[:], in_=rounded[g, c][:].rearrange("p c t -> p (c t)"))
-            for n in range(PIECE // P):
-                cols = slice(n * P, (n + 1) * P)
-                w2_mx[g, c * PIECE // P + n] = (codes[:, cols], plane[:, cols])
+        def quantise_w2(some, room, tag=None):
+            codes = tile([P, len(some) * PIECE], U32, f"w2_codes{some[0]}", tag)
+            plane = tile([P, len(some) * PIECE], U8, f"w2_plane{some[0]}")
+            nc.vector.quantize_mx(out=codes[:].bitcast(FP8X4), scales=plane[:], in_=room.rearrange("p i c t -> p (i c t)"))
+            for i, (g, c) in enumerate(some):
+                for n in range(PIECE // P):
+                    cols = slice(i * PIECE + n * P, i * PIECE + (n + 1) * P)
+                    w2_mx[g, c * PIECE // P + n] = (codes[:, cols], plane[:, cols])
 
-        z = [tile([P, P1, PACK], BF16, f"z{g}") for g in range(G_PASSES)]
+        z = {}
         z_codes = [tile([P, P1], U32, f"z_codes{g}") for g in range(G_PASSES)]
         z_plane = [tile([P, P1], U8, f"z_plane{g}") for g in range(G_PASSES)]
 
-        def multiply_beside(g, m):
-            nc.gpsimd.tensor_tensor(woven(z[g][:, m, :]), planar(u[g][:, :, m]), planar(x[g][:, :, m]), ALU.mult)
+        def multiply(engine, g, m):
+            engine.tensor_tensor(woven(z[g, m.start]), planar(u[g, m.start]), planar(x[g][:, :, m]), ALU.mult)
 
-        def multiply(g, m):
-            nc.vector.tensor_tensor(woven(z[g][:, m, :]), planar(u[g][:, :, m]), planar(x[g][:, :, m]), ALU.mult)
+        def quantise_z(g, c0, c1, woven_z):
+            nc.vector.quantize_mx(
+                out=z_codes[g][:, c0:c1].bitcast(FP8X4), scales=z_plane[g][:, c0:c1], in_=woven_z.rearrange("p c t -> p (c t)")
+            )
 
-        def quantise_z(g, parts):
-            for m in parts:
-                nc.vector.quantize_mx(
-                    out=z_codes[g][:, m].bitcast(FP8X4), scales=z_plane[g][:, m], in_=z[g][:, m, :].rearrange("p c t -> p (c t)")
-                )
-
-        empty_tile(0)
-        order_w4(1, 0, PACK, "w4_codes0_0", "w4_plane0_0")
+        empty_half(0, 0)
+        for c0 in range(BANK, S, BANK // 2):
+            narrow_product(0, c0, c0 + BANK // 2)
+        order_w4(nc.vector, 1, 0, PACK)
+        order_w4(nc.vector, 2, 0, PACK, "w4_first")
+        beside_room = make_room([(0, 0), (0, 1)], "early")
+        for c in range(2):
+            nc.gpsimd.tensor_scalar(rounded[0, c], w2_raw[0, c].rearrange("p t c -> p c t"), 1.0, 0.0, ALU.mult, ALU.add)
         for j in range(1, 6):
             empty_tile(j)
         empty_half(6, 0)
         late_bank = first_product(6, 1)
         next_banks = [first_product(7, half) for half in range(HALVES)]
-        sums = tile([P, PACK + 1, P1], F32, "sums", "w4_codes0_0")
+        sums = tile([P, PACK + 1, P1], F32, "sums", "w4_codes1_0")
         x[0] = sums[:, 1:, :]
         x[1] = sums[:, :PACK, :]
         x[2] = tile([P, PACK, P1], F32, "last_sums")[:]
@@ -265,12 +303,10 @@ def tile_list_claim_charting_kernel(
         pick(4)
         pair(2)
         pair(3)
-        order_w4(2, 0, PACK, "h0", "picked0")
         pair(4)
-        load_w2(0, 0, 3, "stage1")
-        load_w2(1, 0, 3, "early")
-        load_w2(2, 0, 3, "w4_plane_raw")
-        factor(0, lambda: empty(6, late_bank, BANK, S), whole)
+        load_w2(0, 2, 3, "picked0")
+        load_w2(1, 0, 3, "h0")
+        factor(0, lambda: empty(6, late_bank, BANK, S))
         factor(1)
         factor(2)
         factor(3, lambda: empty(7, next_banks[0], 0, SHORT))
@@ -278,38 +314,58 @@ def tile_list_claim_charting_kernel(
         empty(7, next_banks[1], BANK, S)
         empty_tile(8)
         factor(4)
-        for j in range(9, ROW_TILES):
-            empty_tile(j)
-        round_w2(*pieces[0])
-        multiply_beside(0, slice(0, P1))
+        empty_tile(9)
+        empty_tile(10)
+        empty_half(11, 0)
+        last_bank = first_product(11, 1)
+        empty(11, last_bank, BANK, S - SHORT)
+        load_w2(2, 0, 3, "v_w1_0")
+        beside, rest = cuts[0]
+        z[0, 0] = tile([P, beside.stop, PACK], BF16, "z0_beside")[:]
+        multiply(nc.gpsimd, 0, beside)
         for j in range(5, 9):
             pick(j)
+        z[0, rest.start] = tile([P, P1 - rest.start, PACK], BF16, "z0_rest", "u0_0")[:]
+        multiply(nc.vector, 0, rest)
+        quantise_z(0, beside.start, beside.stop, z[0, 0])
         for j in range(5, 8):
             pair(j)
-        quantise_z(0, whole)
+        quantise_z(0, rest.start, rest.stop, z[0, rest.start])
         pair(8)
-        for j in range(5, 9):
-            factor(j)
-        multiply_beside(1, slice(0, SHARE))
+        whole_z = {g: tile([P, P1, PACK], BF16, f"z{g}") for g in range(1, G_PASSES)}
+        for g in whole_z:
+            for m in cuts[g]:
+                z[g, m.start] = whole_z[g][:, m, :]
+        factor(5)
+        factor(6)
+        factor(7, lambda: empty(11, last_bank, S - SHORT, S))
+        early = [(1, 0), (2, 0), (1, 1)]
+        early_room = make_room(early, "sq7")
+        factor(8, lambda: round_w2(*early[0]))
+        multiply(nc.gpsimd, 1, cuts[1][0])
         for j in range(9, ROW_TILES):
             pick(j, f"h{j - 4}")
-        for g, c in pieces[1:5]:
+        for g, c in early[1:]:
             round_w2(g, c)
         for j in range(9, ROW_TILES):
             pair(j)
         for j in range(9, ROW_TILES):
             factor(j)
-        for g, c in pieces[5:-1]:
+        late = [(2, 1), (0, 2), (1, 2), (2, 2)]
+        late_room = make_room(late, "sq11")
+        for g, c in late:
             round_w2(g, c)
-        multiply(1, slice(SHARE, P1))
-        for (g, c), tag in zip(pieces[:G_PASSES], ("h9", "h10", "h11")):
-            quantise_w2(g, c, tag)
-        quantise_z(1, whole)
+        multiply(nc.vector, 1, cuts[1][1])
+        quantise_w2([(0, 0), (0, 1)], beside_room[:], "h10")
+        quantise_w2(early[0:2], early_room[:, 0:2], "h11")
+        quantise_z(1, 0, P1, whole_z[1][:])
         for m in halves:
-            multiply(2, m)
-        quantise_z(2, halves)
-        for (g, c), tag in zip(pieces[G_PASSES:-1], ("v_w0_0", "last_sums", None, None, None)):
-            quantise_w2(g, c, tag)
+            multiply(nc.vector, 2, m)
+        for m in halves:
+            quantise_z(2, m.start, m.stop, z[2, m.start])
+        quantise_w2(early[2:3], early_room[:, 2:3], "last_sums")
+        quantise_w2(late[0:2], late_room[:, 0:2])
+        quantise_w2(late[2:4], late_room[:, 2:4])
 
         acc = [psum.tile([P, P1], F32, name=f"acc{n}", tag=f"bank{n}") for n in range(N_TILES)]
 
@@ -330,11 +386,11 @@ def tile_list_claim_charting_kernel(
 
         def empty_second(n):
             second_product(n)
-            y[n] = tile([P, P1], F32, f"y{n}", f"y{n}")
+            y[n] = tile([P, P1], F32, f"y{n}", f"h{1 + n}")
             nc.scalar.activation(y[n][:], acc[n][:], ACT.Copy)
 
         def finish(n):
-            least = tile([P, P2], F32, f"least{n}")
+            least = tile([P, P2], F32, f"least{n}", f"picked{1 + n}")
             nc.vector.tensor_tensor(least[:], rivals[n][:, 0, :], rivals[n][:, 1, :], ALU.min)
             nc.sync.dma_start(out[n * P : (n + 1) * P, :], least[:])
 
@@ -345,16 +401,7 @@ def tile_list_claim_charting_kernel(
                 finish(n - 1)
             nc.vector.tensor_copy(rivals[n][:, 1, :], y[n][:].indirect(pos4_t[:]))
 
-        empty_second(0)
-        empty_second(1)
-        round_w2(*pieces[-1])
-        empty_second(2)
-        empty_second(3)
-        pick_rivals(0)
-        pick_rivals(1)
-        quantise_w2(*pieces[-1], "y0")
-        empty_second(4)
-        empty_second(5)
-        for n in range(2, N_TILES):
+        for n in range(N_TILES):
+            empty_second(n)
             pick_rivals(n)
         finish(N_TILES - 1)

@@ -127,7 +127,6 @@ def tile_list_claim_charting_kernel(
                 w4_codes[g * PACK + t] = codes[:, :, t - t0, :]
 
         gather_words(0, 0, HALVES, S)
-        load_w2(0, 0, 1, "stage0")
         order_w4(nc.gpsimd, 0, 0, 1)
         w4_planes = []
         for g in range(G_PASSES):
@@ -136,11 +135,10 @@ def tile_list_claim_charting_kernel(
                 w4_planes[g][:].rearrange("p a t c -> p (a t c)").bitcast(I32).rearrange("p (a t q w) -> p a t q w", a=A_PASSES, t=PACK, w=2),
                 w4_plane_raw[:].bitcast(I32).rearrange("p (a g q t w) -> p g a t q w", a=A_PASSES, g=G_PASSES, t=PACK, w=2)[:, g],
             )
-        load_w2(0, 1, 2, "w4_plane_raw")
         gather_words(1, 0, 1, BANK)
         gather_words(1, 1, 2, BANK // 2)
         order_w4(nc.vector, 0, 1, PACK, "rows_then_identity")
-        coef_t = tile([P, ROW_TILES, 8], F32, "coef_t", "stage1")
+        coef_t = tile([P, ROW_TILES, 8], F32, "coef_t", "stage0")
         coef_rows = coef.rearrange("(g q t i o) -> g t q i o", g=G_PASSES, t=PACK, i=8, o=1)
         with nc.allow_non_contiguous_dma(reason="one coefficient for each partition and row tile"):
             for j in range(ROW_TILES):
@@ -188,6 +186,14 @@ def tile_list_claim_charting_kernel(
 
         def empty(j, bank, c0, c1):
             nc.scalar.activation(h[j][:, c0:c1], bank[:, c0 % BANK : (c1 - 1) % BANK + 1], ACT.Copy)
+
+        def empty_pair(j):
+            for k in (j, j + 1):
+                empty(k, first_product(k, 0), 0, BANK)
+            second = [first_product(k, 1) for k in (j, j + 1)]
+            for c0, c1 in ((BANK, S - SHORT), (S - SHORT, S)):
+                for k in (j, j + 1):
+                    empty(k, second[k - j], c0, c1)
 
         def empty_tile(j):
             for half in range(HALVES):
@@ -283,35 +289,32 @@ def tile_list_claim_charting_kernel(
         for c0 in range(BANK, S, BANK // 2):
             narrow_product(0, c0, c0 + BANK // 2)
         order_w4(nc.vector, 1, 0, PACK)
-        order_w4(nc.vector, 2, 0, PACK, "w4_first")
-        beside_room = make_room([(0, 0), (0, 1)], "early")
-        for c in range(2):
-            nc.gpsimd.tensor_scalar(rounded[0, c], w2_raw[0, c].rearrange("p t c -> p c t"), 1.0, 0.0, ALU.mult, ALU.add)
-        for j in range(1, 6):
-            empty_tile(j)
-        empty_half(6, 0)
-        late_bank = first_product(6, 1)
-        next_banks = [first_product(7, half) for half in range(HALVES)]
-        sums = tile([P, PACK + 1, P1], F32, "sums", "w4_codes1_0")
+        order_w4(nc.vector, 2, 0, PACK)
+        empty_pair(1)
+        empty_pair(3)
+        sums = tile([P, PACK + 1, P1], F32, "sums")
         x[0] = sums[:, 1:, :]
         x[1] = sums[:, :PACK, :]
         x[2] = tile([P, PACK, P1], F32, "last_sums")[:]
-        for j in range(PACK):
-            pick(j)
+        pick(0)
         pair(0)
-        pair(1)
-        pick(4)
-        pair(2)
-        pair(3)
-        pair(4)
-        load_w2(0, 2, 3, "picked0")
-        load_w2(1, 0, 3, "h0")
-        factor(0, lambda: empty(6, late_bank, BANK, S))
+        for j in (1, 3):
+            pick(j)
+            pick(j + 1)
+            pair(j)
+            pair(j + 1)
+        load_w2(0, 0, 3, "stage1")
+        load_w2(1, 0, 3, "early")
+        load_w2(2, 0, 3, "h0")
+        factor(0, lambda: empty_half(5, 0))
+        empty_half(5, 1)
         factor(1)
         factor(2)
-        factor(3, lambda: empty(7, next_banks[0], 0, SHORT))
-        empty(7, next_banks[0], SHORT, BANK)
-        empty(7, next_banks[1], BANK, S)
+        empty_half(6, 0)
+        late_bank = first_product(6, 1)
+        factor(3, lambda: empty(6, late_bank, BANK, BANK + SHORT))
+        empty(6, late_bank, BANK + SHORT, S)
+        empty_tile(7)
         empty_tile(8)
         factor(4)
         empty_tile(9)
@@ -319,7 +322,8 @@ def tile_list_claim_charting_kernel(
         empty_half(11, 0)
         last_bank = first_product(11, 1)
         empty(11, last_bank, BANK, S - SHORT)
-        load_w2(2, 0, 3, "v_w1_0")
+        first_room = make_room([(0, 0)], "first_room")
+        round_w2(0, 0)
         beside, rest = cuts[0]
         z[0, 0] = tile([P, beside.stop, PACK], BF16, "z0_beside")[:]
         multiply(nc.gpsimd, 0, beside)
@@ -339,7 +343,7 @@ def tile_list_claim_charting_kernel(
         factor(5)
         factor(6)
         factor(7, lambda: empty(11, last_bank, S - SHORT, S))
-        early = [(1, 0), (2, 0), (1, 1)]
+        early = [(1, 0), (2, 0), (0, 1), (1, 1)]
         early_room = make_room(early, "sq7")
         factor(8, lambda: round_w2(*early[0]))
         multiply(nc.gpsimd, 1, cuts[1][0])
@@ -356,14 +360,14 @@ def tile_list_claim_charting_kernel(
         for g, c in late:
             round_w2(g, c)
         multiply(nc.vector, 1, cuts[1][1])
-        quantise_w2([(0, 0), (0, 1)], beside_room[:], "h10")
+        quantise_w2([(0, 0)], first_room[:], "h10")
         quantise_w2(early[0:2], early_room[:, 0:2], "h11")
         quantise_z(1, 0, P1, whole_z[1][:])
         for m in halves:
             multiply(nc.vector, 2, m)
         for m in halves:
             quantise_z(2, m.start, m.stop, z[2, m.start])
-        quantise_w2(early[2:3], early_room[:, 2:3], "last_sums")
+        quantise_w2(early[2:4], early_room[:, 2:4], "last_sums")
         quantise_w2(late[0:2], late_room[:, 0:2])
         quantise_w2(late[2:4], late_room[:, 2:4])
 

@@ -48,9 +48,9 @@ def tile_list_claim_charting_kernel(
             nc.sync.dma_start(held[:], src)
             return held
 
-        rows0 = P - A_PASSES * 16
         tab_plane = tile([P, T], U8, "tab_plane", "early")
-        nc.vector.memset(tab_plane[0:rows0, :].bitcast(I32), 0)
+        nc.vector.memset(tab_plane[32:64, :].bitcast(I32), 0)
+        nc.vector.memset(tab_plane[64:P, :].bitcast(I32), 0)
         v_planes = [tile([P, S], U8, f"v_plane{a}") for a in range(A_PASSES)]
         for plane in v_planes:
             nc.vector.memset(plane[:].bitcast(I32), 0)
@@ -58,7 +58,7 @@ def tile_list_claim_charting_kernel(
         nc.gpsimd.memset(w4_plane_raw[:].bitcast(I32), 0)
 
         offs_t = load_list(offs, "offs_t")
-        nc.scalar.dma_start(tab_plane[rows0:P, :].bitcast(I32), tab_scales.rearrange("a q t -> (a q) t").bitcast(I32))
+        nc.scalar.dma_start(tab_plane[0:32, :].bitcast(I32), tab_scales.rearrange("a q t -> (a q) t").bitcast(I32))
         tab_w = [tile([P, T], I32, f"tab_w{a}", f"stage{a}") for a in range(A_PASSES)]
 
         def load_tab(a):
@@ -87,11 +87,12 @@ def tile_list_claim_charting_kernel(
         nc.vector.tensor_copy(v_rows[:], tab_plane[:].indirect(offs_t[:]))
         for a in range(A_PASSES):
             for q in range(4):
-                row = rows0 + 16 * a + 4 * q
-                nc.sync.dma_start(
-                    v_planes[a][32 * q : 32 * q + 4, :].bitcast(I32),
-                    v_rows[row : row + 4, :].bitcast(I32),
-                )
+                row = 16 * a + 4 * q
+                if row:
+                    nc.sync.dma_start(
+                        v_planes[a][32 * q : 32 * q + 4, :].bitcast(I32),
+                        v_rows[row : row + 4, :].bitcast(I32),
+                    )
         w4_raw.extend(load_w4(1, G_PASSES, "early"))
 
         w2_raw = {}
@@ -127,6 +128,7 @@ def tile_list_claim_charting_kernel(
                 w4_codes[g * PACK + t] = codes[:, :, t - t0, :]
 
         gather_words(0, 0, HALVES, S)
+        nc.vector.tensor_copy(v_planes[0][0:4, :].bitcast(I32), v_rows[0:4, :].bitcast(I32))
         order_w4(nc.gpsimd, 0, 0, 1)
         w4_planes = []
         for g in range(G_PASSES):

@@ -58,7 +58,7 @@ def tile_list_claim_charting_kernel(
         nc.gpsimd.memset(w4_plane_raw[:].bitcast(I32), 0)
 
         offs_t = load_list(offs, "offs_t")
-        nc.scalar.dma_start(tab_plane[0:32, :].bitcast(I32), tab_scales.rearrange("a q t -> (a q) t").bitcast(I32))
+        nc.sync.dma_start(tab_plane[0:32, :].bitcast(I32), tab_scales.rearrange("a q t -> (a q) t").bitcast(I32))
         tab_w = [tile([P, T], I32, f"tab_w{a}", f"stage{a}") for a in range(A_PASSES)]
 
         def load_tab(a):
@@ -70,18 +70,18 @@ def tile_list_claim_charting_kernel(
             nc.sync.dma_start(raw[:], w4_words[:, :, cols].rearrange("a p c -> p a c").bitcast(I32))
             return [raw[:, :, (g - g0) * K_PASS // 2 : (g - g0 + 1) * K_PASS // 2] for g in range(g0, g1)]
 
-        load_tab(0)
-        w4_raw = load_w4(0, 1, "w4_first")
         pos1_t = load_list(pos1, "pos1_t")
         pos2_t = load_list(pos2, "pos2_t")
         pos3_t = load_list(pos3, "pos3_t")
         pos4_t = load_list(pos4, "pos4_t")
-        load_tab(1)
+        load_tab(0)
+        w4_raw = load_w4(0, 1, "w4_first")
         for q in range(4):
-            nc.gpsimd.dma_start(
+            nc.sync.dma_start(
                 w4_plane_raw[32 * q : 32 * q + 4, :].bitcast(I32).rearrange("r (a c) -> r a c", a=A_PASSES),
                 w4_scales[:, 4 * q : 4 * q + 4, :].bitcast(I32).rearrange("a r c -> r a c"),
             )
+        load_tab(1)
 
         v_rows = tile([P, S], U8, "v_rows", "rows_then_identity")
         nc.vector.tensor_copy(v_rows[:], tab_plane[:].indirect(offs_t[:]))

@@ -27,6 +27,7 @@ HALVES = S // BANK
 N_TILES = N // P
 BANKS = 8
 PIECE = 256
+LEAD = 256
 SHORT = 128
 SHARES = (256, 272)
 
@@ -48,17 +49,18 @@ def tile_list_claim_charting_kernel(
             nc.sync.dma_start(held[:], src)
             return held
 
-        tab_plane = tile([P, T], U8, "tab_plane", "early")
+        tab_plane = tile([P, T], U8, "tab_plane")
         nc.vector.memset(tab_plane[32:64, :].bitcast(I32), 0)
         nc.vector.memset(tab_plane[64:P, :].bitcast(I32), 0)
-        v_planes = [tile([P, S], U8, f"v_plane{a}") for a in range(A_PASSES)]
-        for plane in v_planes:
-            nc.vector.memset(plane[:].bitcast(I32), 0)
-        w4_plane_raw = tile([P, A_PASSES * H], U8, "w4_plane_raw")
-        nc.gpsimd.memset(w4_plane_raw[:].bitcast(I32), 0)
+        planes = [tile([P, S + H], U8, f"plane{a}") for a in range(A_PASSES)]
+        nc.gpsimd.memset(planes[0][:].bitcast(I32), 0)
+        nc.vector.memset(planes[1][:].bitcast(I32), 0)
+        v_planes = [plane[:, :S] for plane in planes]
 
         offs_t = load_list(offs, "offs_t")
         nc.sync.dma_start(tab_plane[0:32, :].bitcast(I32), tab_scales.rearrange("a q t -> (a q) t").bitcast(I32))
+        w4_rows = tile([P, H], U8, "w4_rows")
+        nc.sync.dma_start(w4_rows[0:32, :].bitcast(I32), w4_scales.rearrange("a q c -> (a q) c").bitcast(I32))
         tab_w = [tile([P, T], I32, f"tab_w{a}", f"stage{a}") for a in range(A_PASSES)]
 
         def load_tab(a):
@@ -70,30 +72,30 @@ def tile_list_claim_charting_kernel(
             nc.sync.dma_start(raw[:], w4_words[:, :, cols].rearrange("a p c -> p a c").bitcast(I32))
             return [raw[:, :, (g - g0) * K_PASS // 2 : (g - g0 + 1) * K_PASS // 2] for g in range(g0, g1)]
 
+        load_tab(0)
+        w4_raw = load_w4(0, 1, "w4_first")
         pos1_t = load_list(pos1, "pos1_t")
         pos2_t = load_list(pos2, "pos2_t")
         pos3_t = load_list(pos3, "pos3_t")
         pos4_t = load_list(pos4, "pos4_t")
-        load_tab(0)
-        w4_raw = load_w4(0, 1, "w4_first")
-        for q in range(4):
-            nc.sync.dma_start(
-                w4_plane_raw[32 * q : 32 * q + 4, :].bitcast(I32).rearrange("r (a c) -> r a c", a=A_PASSES),
-                w4_scales[:, 4 * q : 4 * q + 4, :].bitcast(I32).rearrange("a r c -> r a c"),
-            )
         load_tab(1)
+        rows_together = tile([P, S + H], U8, "rows_together", "together")
+        for dst, rows in ((rows_together, slice(0, 32)), (planes[0], slice(0, 4))):
+            nc.gpsimd.tensor_copy(
+                dst[rows, S:].bitcast(I32).rearrange("p (g t q w) -> p g t q w", g=G_PASSES, t=PACK, w=2),
+                w4_rows[rows, :].bitcast(I32).rearrange("p (g q t w) -> p g t q w", g=G_PASSES, t=PACK, w=2),
+            )
 
-        v_rows = tile([P, S], U8, "v_rows", "rows_then_identity")
+        v_rows = tile([P, S], U8, "v_rows", "early")
         nc.vector.tensor_copy(v_rows[:], tab_plane[:].indirect(offs_t[:]))
+        v_first = tile([P, S], U32, "v_w0_0")
+        nc.vector.tensor_copy(v_first[:, :LEAD], tab_w[0][:].bitcast(U32).indirect(offs_t[:, : LEAD // 16]))
+        nc.vector.tensor_copy(rows_together[0:32, :S].bitcast(I32), v_rows[0:32, :].bitcast(I32))
         for a in range(A_PASSES):
             for q in range(4):
                 row = 16 * a + 4 * q
                 if row:
-                    nc.sync.dma_start(
-                        v_planes[a][32 * q : 32 * q + 4, :].bitcast(I32),
-                        v_rows[row : row + 4, :].bitcast(I32),
-                    )
-        w4_raw.extend(load_w4(1, G_PASSES, "early"))
+                    nc.sync.dma_start(planes[a][32 * q : 32 * q + 4, :].bitcast(I32), rows_together[row : row + 4, :].bitcast(I32))
 
         w2_raw = {}
 
@@ -127,19 +129,15 @@ def tile_list_claim_charting_kernel(
             for t in range(t0, t1):
                 w4_codes[g * PACK + t] = codes[:, :, t - t0, :]
 
-        gather_words(0, 0, HALVES, S)
-        nc.vector.tensor_copy(v_planes[0][0:4, :].bitcast(I32), v_rows[0:4, :].bitcast(I32))
+        nc.vector.tensor_copy(v_first[:, LEAD:], tab_w[0][:].bitcast(U32).indirect(offs_t[:, LEAD // 16 :]))
+        for half in range(HALVES):
+            v_w[0, half] = v_first[:, half * BANK : (half + 1) * BANK]
+        nc.vector.tensor_copy(planes[0][0:4, :S].bitcast(I32), v_rows[0:4, :].bitcast(I32))
+        w4_raw.extend(load_w4(1, G_PASSES, "early"))
         order_w4(nc.gpsimd, 0, 0, 1)
-        w4_planes = []
-        for g in range(G_PASSES):
-            w4_planes.append(tile([P, A_PASSES, PACK, P], U8, f"w4_plane{g}"))
-            nc.gpsimd.tensor_copy(
-                w4_planes[g][:].rearrange("p a t c -> p (a t c)").bitcast(I32).rearrange("p (a t q w) -> p a t q w", a=A_PASSES, t=PACK, w=2),
-                w4_plane_raw[:].bitcast(I32).rearrange("p (a g q t w) -> p g a t q w", a=A_PASSES, g=G_PASSES, t=PACK, w=2)[:, g],
-            )
         gather_words(1, 0, 1, BANK)
         gather_words(1, 1, 2, BANK // 2)
-        order_w4(nc.vector, 0, 1, PACK, "rows_then_identity")
+        order_w4(nc.vector, 0, 1, PACK, "together")
         coef_t = tile([P, ROW_TILES, 8], F32, "coef_t", "stage0")
         coef_rows = coef.rearrange("(g q t i o) -> g t q i o", g=G_PASSES, t=PACK, i=8, o=1)
         with nc.allow_non_contiguous_dma(reason="one coefficient for each partition and row tile"):
@@ -155,14 +153,14 @@ def tile_list_claim_charting_kernel(
         h = [tile([P, S], F32, f"h{j}") for j in range(ROW_TILES)]
 
         def first_product(j, half):
-            codes, plane = w4_codes[j], w4_planes[j // PACK][:, :, j % PACK, :]
+            codes, rows = w4_codes[j], slice(S + j * P, S + (j + 1) * P)
             cols = slice(half * BANK, (half + 1) * BANK)
             bank = next_bank([P, BANK], f"hb{j}_{half}")
             for a in range(A_PASSES):
                 nc.tensor.matmul_mx(
                     out=bank[:],
                     lhsT=codes[:, a, :].bitcast(FP4X4),
-                    lhsT_scale=plane[:, a, :],
+                    lhsT_scale=planes[a][:, rows],
                     rhs=v_w[a, half].bitcast(FP8X4),
                     rhs_scale=v_planes[a][:, cols],
                     start=(a == 0),
@@ -171,14 +169,14 @@ def tile_list_claim_charting_kernel(
             return bank
 
         def narrow_product(j, c0, c1):
-            codes, plane = w4_codes[j], w4_planes[j // PACK][:, :, j % PACK, :]
+            codes, rows = w4_codes[j], slice(S + j * P, S + (j + 1) * P)
             bank = next_bank([P, c1 - c0], f"hb{j}_{c0}")
             for a in range(A_PASSES):
                 for c in range(c0, c1, P):
                     nc.tensor.matmul_mx(
                         out=bank[:, c - c0 : c - c0 + P],
                         lhsT=codes[:, a, :].bitcast(FP4X4),
-                        lhsT_scale=plane[:, a, :],
+                        lhsT_scale=planes[a][:, rows],
                         rhs=v_w[a, c // BANK][:, c % BANK : c % BANK + P].bitcast(FP8X4),
                         rhs_scale=v_planes[a][:, c : c + P],
                         start=(a == 0 and c == c0),

@@ -29,7 +29,7 @@ BANKS = 8
 PIECE = 256
 LEAD = 256
 SHORT = 128
-SHARES = (256, 272)
+SHARES = (352, 256)
 
 
 def tile_list_claim_charting_kernel(
@@ -39,9 +39,14 @@ def tile_list_claim_charting_kernel(
     with ExitStack() as ctx:
         keep = ctx.enter_context(tc.tile_pool(name="keep", bufs=1))
         ring = ctx.enter_context(tc.tile_pool(name="ring", bufs=2))
+        reuse = ctx.enter_context(tc.tile_pool(name="reuse", bufs=1))
         psum = ctx.enter_context(tc.psum_pool(name="psum", bufs=1))
 
+        places = {"picked0": 20480, "room0": 20480, "picked2": 22528, "room2": 22528, "early_room": 0, "chain": 7680, "sq8": 9472, "sq9": 11264, "late_room": 12800}
+
         def tile(shape, dtype, name, tag=None):
+            if tag in places:
+                return reuse.tile(shape, dtype, name=name, align_bytes=64, offset=places[tag])
             return keep.tile(shape, dtype, name=name, tag=tag or name, align_bytes=64)
 
         def load_list(src, name):
@@ -129,20 +134,17 @@ def tile_list_claim_charting_kernel(
             for t in range(t0, t1):
                 w4_codes[g * PACK + t] = codes[:, :, t - t0, :]
 
+        nc.vector.tensor_copy(planes[0][0:4, :S].bitcast(I32), v_rows[0:4, :].bitcast(I32))
+        w4_raw.extend(load_w4(1, G_PASSES, "early"))
         nc.vector.tensor_copy(v_first[:, LEAD:], tab_w[0][:].bitcast(U32).indirect(offs_t[:, LEAD // 16 :]))
         for half in range(HALVES):
             v_w[0, half] = v_first[:, half * BANK : (half + 1) * BANK]
-        nc.vector.tensor_copy(planes[0][0:4, :S].bitcast(I32), v_rows[0:4, :].bitcast(I32))
-        w4_raw.extend(load_w4(1, G_PASSES, "early"))
         order_w4(nc.gpsimd, 0, 0, 1)
         gather_words(1, 0, 1, BANK)
         gather_words(1, 1, 2, BANK // 2)
         order_w4(nc.vector, 0, 1, PACK, "together")
-        coef_t = tile([P, ROW_TILES, 8], F32, "coef_t", "stage0")
+        coef_t = tile([P, ROW_TILES, 8], F32, "coef_t", "w4_first")
         coef_rows = coef.rearrange("(g q t i o) -> g t q i o", g=G_PASSES, t=PACK, i=8, o=1)
-        with nc.allow_non_contiguous_dma(reason="one coefficient for each partition and row tile"):
-            for j in range(ROW_TILES):
-                nc.sync.dma_start(coef_t[:, j, 0:1], coef_rows[j // PACK, j % PACK])
 
         banks = []
 
@@ -207,8 +209,8 @@ def tile_list_claim_charting_kernel(
 
         picked, x, u = {}, {}, {}
 
-        def pick(j, tag=None):
-            picked[j] = x[2][:, 0, :] if j == 2 * PACK - 1 else tile([P, P1], F32, f"picked{j}", tag)[:]
+        def pick(j, into=None):
+            picked[j] = tile([P, P1], F32, f"picked{j}")[:] if into is None else into
             nc.vector.tensor_copy(picked[j], h[j][:].indirect(pos1_t[:]))
 
         def pair(j):
@@ -217,36 +219,37 @@ def tile_list_claim_charting_kernel(
 
         squares = {}
         halves = [slice(0, P1 // 2), slice(P1 // 2, P1)]
-        whole = [slice(0, P1)]
-        cuts = [[slice(0, share), slice(share, P1)] for share in SHARES] + [halves]
+        whole = slice(0, P1)
+        cuts = [[slice(share, P1), slice(0, share)] for share in SHARES] + [halves]
 
-        def square(j, parts):
+        def square(j, tag=None, cut=False):
             g, t = divmod(j, PACK)
-            if j in (2 * PACK - 1, ROW_TILES - 1):
-                squares[j] = tile([P, P1], F32, f"sq{j}")
+            if tag == "same":
+                squares[j] = squares[j - 1]
+            elif tag:
+                squares[j] = tile([P, P1], F32, f"sq{j}", tag)
             else:
                 squares[j] = ring.tile([P, P1], F32, name=f"sq{j}", tag="sq")
-            for m in parts:
+            for m in cuts[g] if cut else [whole]:
                 nc.scalar.activation(squares[j][:, m], x[g][:, t, m], ACT.Square)
 
-        def scale_up(j, parts):
-            g, t = divmod(j, PACK)
-            if t == 0 and g == 0:
-                for m in parts:
-                    u[g, m.start] = tile([P, PACK, m.stop - m.start], F32, f"u{g}_{m.start}")[:]
-            elif t == 0:
-                whole_u = tile([P, PACK, P1], F32, f"u{g}", ("u1", "v_w0_0")[g - 1])
-                for m in parts:
-                    u[g, m.start] = whole_u[:, :, m]
-            for m in parts:
-                nc.scalar.activation(u[g, m.start][:, t, :], squares[j][:, m], ACT.Identity, bias=1.0, scale=coef_t[:, j, 0:1])
+        shared = [tile([P, (PACK + g) * P1], F32, f"shared{g}") for g in range(2)]
+        slots = [held[:].rearrange("p (s c) -> p s c", c=P1) for held in shared]
+        for g in range(2):
+            first, beside = cuts[g]
+            u[g, first.start] = slots[g][:, :PACK, : P1 - first.start]
+            u[g, 0] = tile([P, PACK, beside.stop], F32, f"u{g}")[:]
+        u[2, None] = tile([P, PACK, P1], F32, "u2", "v_w0_0")[:]
+        for m in halves:
+            u[2, m.start] = u[2, None][:, :, m]
 
-        def factor(j, between=None):
-            parts = cuts[j // PACK]
-            square(j, whole if between and j == 0 else parts)
-            if between:
-                between()
-            scale_up(j, parts)
+        def scale_up(j, cut=False):
+            g, t = divmod(j, PACK)
+            if cut or g < 2:
+                for m in cuts[g]:
+                    nc.scalar.activation(u[g, m.start][:, t, :], squares[j][:, m], ACT.Identity, bias=1.0, scale=coef_t[:, j, 0:1])
+            else:
+                nc.scalar.activation(u[g, None][:, t, :], squares[j][:], ACT.Identity, bias=1.0, scale=coef_t[:, j, 0:1])
 
         def empty_half(j, half):
             empty(j, first_product(j, half), half * BANK, (half + 1) * BANK)
@@ -261,6 +264,9 @@ def tile_list_claim_charting_kernel(
 
         def round_w2(g, c):
             nc.scalar.copy(woven(rounded[g, c]), planar(w2_raw[g, c]))
+
+        def round_beside(g, c):
+            nc.gpsimd.tensor_scalar(rounded[g, c], w2_raw[g, c].rearrange("p t c -> p c t"), 1.0, 0.0, ALU.mult, ALU.add)
 
         w2_mx = {}
 
@@ -303,73 +309,87 @@ def tile_list_claim_charting_kernel(
             pick(j + 1)
             pair(j)
             pair(j + 1)
-        load_w2(0, 0, 3, "stage1")
+        load_w2(0, 0, 2, "stage0")
+        with nc.allow_non_contiguous_dma(reason="one coefficient for each partition and row tile"):
+            for j in range(ROW_TILES):
+                nc.sync.dma_start(coef_t[:, j, 0:1], coef_rows[j // PACK, j % PACK])
+        load_w2(0, 2, 3, "stage1")
         load_w2(1, 0, 3, "early")
         load_w2(2, 0, 3, "h0")
-        factor(0, lambda: empty_half(5, 0))
+        rooms = {}
+        for j, piece in ((0, (0, 0)), (2, (0, 1))):
+            rooms[piece] = make_room([piece], f"room{j}")
+            round_beside(*piece)
+        square(0)
+        empty_half(5, 0)
+        scale_up(0)
         empty_half(5, 1)
-        factor(1)
-        factor(2)
-        empty_half(6, 0)
-        late_bank = first_product(6, 1)
-        factor(3, lambda: empty(6, late_bank, BANK, BANK + SHORT))
-        empty(6, late_bank, BANK + SHORT, S)
-        empty_tile(7)
-        empty_tile(8)
-        factor(4)
-        empty_tile(9)
-        empty_tile(10)
-        empty_half(11, 0)
-        last_bank = first_product(11, 1)
-        empty(11, last_bank, BANK, S - SHORT)
-        first_room = make_room([(0, 0)], "first_room")
-        round_w2(0, 0)
-        beside, rest = cuts[0]
-        z[0, 0] = tile([P, beside.stop, PACK], BF16, "z0_beside")[:]
-        multiply(nc.gpsimd, 0, beside)
-        for j in range(5, 9):
-            pick(j)
-        z[0, rest.start] = tile([P, P1 - rest.start, PACK], BF16, "z0_rest", "u0_0")[:]
-        multiply(nc.vector, 0, rest)
-        quantise_z(0, beside.start, beside.stop, z[0, 0])
-        for j in range(5, 8):
-            pair(j)
-        quantise_z(0, rest.start, rest.stop, z[0, rest.start])
-        pair(8)
-        whole_z = {g: tile([P, P1, PACK], BF16, f"z{g}") for g in range(1, G_PASSES)}
+        square(1)
+        square(2)
+        scale_up(1)
+        scale_up(2)
+        empty_tile(6)
+        square(3, cut=True)
+        scale_up(3)
+        whole_z = {g: shared[g][:, (2 + g) * P1 :].bitcast(BF16).rearrange("p (c t) -> p c t", t=PACK) for g in range(2)}
+        whole_z[2] = tile([P, P1, PACK], BF16, "z2")[:]
         for g in whole_z:
             for m in cuts[g]:
                 z[g, m.start] = whole_z[g][:, m, :]
-        factor(5)
-        factor(6)
-        factor(7, lambda: empty(11, last_bank, S - SHORT, S))
-        early = [(1, 0), (2, 0), (0, 1), (1, 1)]
-        early_room = make_room(early, "sq7")
-        factor(8, lambda: round_w2(*early[0]))
-        multiply(nc.gpsimd, 1, cuts[1][0])
+        multiply(nc.vector, 0, cuts[0][0])
+        multiply(nc.gpsimd, 0, cuts[0][1])
+        empty_tile(7)
+        empty_tile(8)
+        square(4)
+        empty_half(9, 0)
+        scale_up(4)
+        empty_half(9, 1)
+        empty_tile(10)
+        pick(5, slots[0][:, 0, :])
+        pick(6, slots[0][:, 1, :])
+        pick(7, x[2][:, 0, :])
+        pick(8)
+        for j in range(5, 8):
+            pair(j)
+        quantise_z(0, 0, P1, whole_z[0])
+        pair(8)
+        empty_half(11, 0)
+        last_bank = first_product(11, 1)
+        for j in range(5, 8):
+            square(j, "chain" if j == 5 else "same", True)
+            scale_up(j, True)
+        empty(11, last_bank, BANK, S)
+        multiply(nc.vector, 1, cuts[1][0])
+        multiply(nc.gpsimd, 1, cuts[1][1])
+        early = [(1, 0), (2, 0), (1, 1), (2, 1)]
+        early_room = make_room(early, "early_room")
+        square(8, "sq8")
+        round_w2(*early[0])
+        scale_up(8)
         for j in range(9, ROW_TILES):
-            pick(j, f"h{j - 4}")
+            pick(j, slots[1][:, j - 9, :])
         for g, c in early[1:]:
             round_w2(g, c)
         for j in range(9, ROW_TILES):
             pair(j)
         for j in range(9, ROW_TILES):
-            factor(j)
-        late = [(2, 1), (0, 2), (1, 2), (2, 2)]
-        late_room = make_room(late, "sq11")
+            square(j, "sq9" if j == 9 else "same", True)
+            scale_up(j, True)
+        late = [(0, 2), (1, 2), (2, 2)]
+        late_room = make_room(late, "late_room")
         for g, c in late:
             round_w2(g, c)
-        multiply(nc.vector, 1, cuts[1][1])
-        quantise_w2([(0, 0)], first_room[:], "h10")
+        quantise_z(1, 0, P1, whole_z[1])
         quantise_w2(early[0:2], early_room[:, 0:2], "h11")
-        quantise_z(1, 0, P1, whole_z[1][:])
+        quantise_w2([(0, 0)], rooms[0, 0][:], "h10")
         for m in halves:
             multiply(nc.vector, 2, m)
         for m in halves:
             quantise_z(2, m.start, m.stop, z[2, m.start])
-        quantise_w2(early[2:4], early_room[:, 2:4], "last_sums")
+        quantise_w2([(0, 1)], rooms[0, 1][:], "last_sums")
+        quantise_w2(early[2:4], early_room[:, 2:4], "z2")
         quantise_w2(late[0:2], late_room[:, 0:2])
-        quantise_w2(late[2:4], late_room[:, 2:4])
+        quantise_w2(late[2:3], late_room[:, 2:3])
 
         acc = [psum.tile([P, P1], F32, name=f"acc{n}", tag=f"bank{n}") for n in range(N_TILES)]
 
@@ -394,7 +414,7 @@ def tile_list_claim_charting_kernel(
             nc.scalar.activation(y[n][:], acc[n][:], ACT.Copy)
 
         def finish(n):
-            least = tile([P, P2], F32, f"least{n}", f"picked{1 + n}")
+            least = tile([P, P2], F32, f"least{n}", ("picked1", "picked3", "picked4", "picked8", "u0", "u1")[n])
             nc.vector.tensor_tensor(least[:], rivals[n][:, 0, :], rivals[n][:, 1, :], ALU.min)
             nc.sync.dma_start(out[n * P : (n + 1) * P, :], least[:])
 

@@ -28,7 +28,6 @@ N_TILES = N // P
 BANKS = 8
 PIECE = 256
 LEAD = 256
-SHORT = 128
 SHARES = (352, 256)
 
 
@@ -45,8 +44,8 @@ def tile_list_claim_charting_kernel(
         places = {"picked0": 20480, "room0": 20480, "picked2": 22528, "room2": 22528, "early_room": 0, "chain": 7680, "sq8": 9472, "sq9": 11264, "late_room": 12800}
 
         def tile(shape, dtype, name, tag=None):
-            if tag in places:
-                return reuse.tile(shape, dtype, name=name, align_bytes=64, offset=places[tag])
+            if (tag or name) in places:
+                return reuse.tile(shape, dtype, name=name, align_bytes=64, offset=places[tag or name])
             return keep.tile(shape, dtype, name=name, tag=tag or name, align_bytes=64)
 
         def load_list(src, name):
@@ -86,9 +85,9 @@ def tile_list_claim_charting_kernel(
         load_tab(1)
         rows_together = tile([P, S + H], U8, "rows_together", "together")
         for dst, rows in ((rows_together, slice(0, 32)), (planes[0], slice(0, 4))):
-            nc.gpsimd.tensor_copy(
-                dst[rows, S:].bitcast(I32).rearrange("p (g t q w) -> p g t q w", g=G_PASSES, t=PACK, w=2),
-                w4_rows[rows, :].bitcast(I32).rearrange("p (g q t w) -> p g t q w", g=G_PASSES, t=PACK, w=2),
+            nc.scalar.copy(
+                dst[rows, S:].bitcast(U32).rearrange("p (g t q w) -> p g t q w", g=G_PASSES, t=PACK, w=2),
+                w4_rows[rows, :].bitcast(U32).rearrange("p (g q t w) -> p g t q w", g=G_PASSES, t=PACK, w=2),
             )
 
         v_rows = tile([P, S], U8, "v_rows", "early")
@@ -117,8 +116,9 @@ def tile_list_claim_charting_kernel(
         def gather_words(a, half0, half1, step):
             words = tile([P, (half1 - half0) * BANK], U32, f"v_w{a}_{half0}")
             for c in range(0, (half1 - half0) * BANK, step):
-                cols = slice((half0 * BANK + c) // 16, (half0 * BANK + c + step) // 16)
-                nc.vector.tensor_copy(words[:, c : c + step], tab_w[a][:].bitcast(U32).indirect(offs_t[:, cols]))
+                end = min(c + step, (half1 - half0) * BANK)
+                cols = slice((half0 * BANK + c) // 16, (half0 * BANK + end) // 16)
+                nc.vector.tensor_copy(words[:, c:end], tab_w[a][:].bitcast(U32).indirect(offs_t[:, cols]))
             for half in range(half0, half1):
                 v_w[a, half] = words[:, (half - half0) * BANK : (half - half0 + 1) * BANK]
 
@@ -127,9 +127,9 @@ def tile_list_claim_charting_kernel(
         def order_w4(engine, g, t0, t1, tag=None):
             n = t1 - t0
             codes = tile([P, A_PASSES, n, 2 * P], U8, f"w4_codes{g}_{t0}", tag)
-            engine.tensor_copy(
-                codes[:].rearrange("p a t c -> p (a t c)").bitcast(I32).rearrange("p (a t q w) -> p a t q w", a=A_PASSES, t=n, w=4),
-                w4_raw[g].rearrange("p a (q t w) -> p a t q w", t=PACK, w=4)[:, :, t0:t1],
+            engine(
+                codes[:].rearrange("p a t c -> p (a t c)").bitcast(U32 if g == 0 else I32).rearrange("p (a t q w) -> p a t q w", a=A_PASSES, t=n, w=4),
+                (w4_raw[g].bitcast(U32) if g == 0 else w4_raw[g]).rearrange("p a (q t w) -> p a t q w", t=PACK, w=4)[:, :, t0:t1],
             )
             for t in range(t0, t1):
                 w4_codes[g * PACK + t] = codes[:, :, t - t0, :]
@@ -139,10 +139,10 @@ def tile_list_claim_charting_kernel(
         nc.vector.tensor_copy(v_first[:, LEAD:], tab_w[0][:].bitcast(U32).indirect(offs_t[:, LEAD // 16 :]))
         for half in range(HALVES):
             v_w[0, half] = v_first[:, half * BANK : (half + 1) * BANK]
-        order_w4(nc.gpsimd, 0, 0, 1)
+        order_w4(nc.scalar.copy, 0, 0, 1)
         gather_words(1, 0, 1, BANK)
-        gather_words(1, 1, 2, BANK // 2)
-        order_w4(nc.vector, 0, 1, PACK, "together")
+        gather_words(1, 1, 2, BANK - P)
+        order_w4(nc.scalar.copy, 0, 1, PACK, "together")
         coef_t = tile([P, ROW_TILES, 8], F32, "coef_t", "w4_first")
         coef_rows = coef.rearrange("(g q t i o) -> g t q i o", g=G_PASSES, t=PACK, i=8, o=1)
 
@@ -188,14 +188,6 @@ def tile_list_claim_charting_kernel(
 
         def empty(j, bank, c0, c1):
             nc.scalar.activation(h[j][:, c0:c1], bank[:, c0 % BANK : (c1 - 1) % BANK + 1], ACT.Copy)
-
-        def empty_pair(j):
-            for k in (j, j + 1):
-                empty(k, first_product(k, 0), 0, BANK)
-            second = [first_product(k, 1) for k in (j, j + 1)]
-            for c0, c1 in ((BANK, S - SHORT), (S - SHORT, S)):
-                for k in (j, j + 1):
-                    empty(k, second[k - j], c0, c1)
 
         def empty_tile(j):
             for half in range(HALVES):
@@ -266,7 +258,7 @@ def tile_list_claim_charting_kernel(
             nc.scalar.copy(woven(rounded[g, c]), planar(w2_raw[g, c]))
 
         def round_beside(g, c):
-            nc.gpsimd.tensor_scalar(rounded[g, c], w2_raw[g, c].rearrange("p t c -> p c t"), 1.0, 0.0, ALU.mult, ALU.add)
+            nc.gpsimd.tensor_scalar(rounded[g, c].rearrange("p c (s l) -> p c s l", l=2), w2_raw[g, c].rearrange("p s l c -> p c s l"), 1.0, 0.0, ALU.mult, ALU.add)
 
         w2_mx = {}
 
@@ -292,34 +284,38 @@ def tile_list_claim_charting_kernel(
             )
 
         empty_half(0, 0)
-        for c0 in range(BANK, S, BANK // 2):
-            narrow_product(0, c0, c0 + BANK // 2)
-        order_w4(nc.vector, 1, 0, PACK)
-        order_w4(nc.vector, 2, 0, PACK)
-        empty_pair(1)
-        empty_pair(3)
-        sums = tile([P, PACK + 1, P1], F32, "sums")
+        narrow_product(0, BANK, S - P)
+        narrow_product(0, S - P, S)
+        order_w4(nc.vector.tensor_copy, 1, 0, PACK)
+        order_w4(nc.vector.tensor_copy, 2, 0, PACK)
+        for j in range(1, 5):
+            empty_tile(j)
+        sums = tile([P, (PACK + 1) * P1], F32, "sums", "stage0")[:].rearrange("p (s c) -> p s c", c=P1)
+        quarters = sums.rearrange("p s (l c) -> p s l c", l=2)
+        for c, rows_at in enumerate((quarters[:, 2:4], quarters[:, 0::4])):
+            rows = w2[:K_PASS, c * PIECE : (c + 1) * PIECE].rearrange("(q t i) n -> t q i n", t=PACK, i=8)
+            for t in range(PACK):
+                nc.sync.dma_start(rows_at[:, t // 2, t % 2, :], rows[t])
+            w2_raw[0, c] = rows_at
         x[0] = sums[:, 1:, :]
         x[1] = sums[:, :PACK, :]
         x[2] = tile([P, PACK, P1], F32, "last_sums")[:]
         pick(0)
         pair(0)
-        for j in (1, 3):
+        rooms = {}
+        for c, j in enumerate((1, 3)):
+            rooms[0, c] = make_room([(0, c)], f"room{j - 1}")
+            round_beside(0, c)
             pick(j)
             pick(j + 1)
             pair(j)
             pair(j + 1)
-        load_w2(0, 0, 2, "stage0")
         with nc.allow_non_contiguous_dma(reason="one coefficient for each partition and row tile"):
             for j in range(ROW_TILES):
                 nc.sync.dma_start(coef_t[:, j, 0:1], coef_rows[j // PACK, j % PACK])
         load_w2(0, 2, 3, "stage1")
         load_w2(1, 0, 3, "early")
         load_w2(2, 0, 3, "h0")
-        rooms = {}
-        for j, piece in ((0, (0, 0)), (2, (0, 1))):
-            rooms[piece] = make_room([piece], f"room{j}")
-            round_beside(*piece)
         square(0)
         empty_half(5, 0)
         scale_up(0)

@@ -41,7 +41,7 @@ def tile_list_claim_charting_kernel(
         reuse = ctx.enter_context(tc.tile_pool(name="reuse", bufs=1))
         psum = ctx.enter_context(tc.psum_pool(name="psum", bufs=1))
 
-        places = {"picked0": 20480, "room0": 20480, "picked2": 22528, "room2": 22528, "early_room": 0, "chain": 7680, "sq8": 9472, "sq9": 11264, "late_room": 12800}
+        places = {"early_room": 0, "chain": 7680, "sq8": 9472, "sq9": 11264, "late_room": 12800, "room1": 17408, "picked1": 20480, "picked_next": 21504, "early": 27648, "room0": 27648, "w2_pass1": 29696}
 
         def tile(shape, dtype, name, tag=None):
             if (tag or name) in places:
@@ -57,8 +57,6 @@ def tile_list_claim_charting_kernel(
         nc.vector.memset(tab_plane[32:64, :].bitcast(I32), 0)
         nc.vector.memset(tab_plane[64:P, :].bitcast(I32), 0)
         planes = [tile([P, S + H], U8, f"plane{a}") for a in range(A_PASSES)]
-        nc.gpsimd.memset(planes[0][:].bitcast(I32), 0)
-        nc.vector.memset(planes[1][:].bitcast(I32), 0)
         v_planes = [plane[:, :S] for plane in planes]
 
         offs_t = load_list(offs, "offs_t")
@@ -225,7 +223,7 @@ def tile_list_claim_charting_kernel(
             for m in cuts[g] if cut else [whole]:
                 nc.scalar.activation(squares[j][:, m], x[g][:, t, m], ACT.Square)
 
-        shared = [tile([P, (PACK + g) * P1], F32, f"shared{g}") for g in range(2)]
+        shared = [tile([P, (PACK + 1) * P1], F32, f"shared{g}") for g in range(2)]
         slots = [held[:].rearrange("p (s c) -> p s c", c=P1) for held in shared]
         for g in range(2):
             first, beside = cuts[g]
@@ -235,11 +233,15 @@ def tile_list_claim_charting_kernel(
         for m in halves:
             u[2, m.start] = u[2, None][:, :, m]
 
+        def scale_part(j, m):
+            g, t = divmod(j, PACK)
+            nc.scalar.activation(u[g, m.start][:, t, :], squares[j][:, m], ACT.Identity, bias=1.0, scale=coef_t[:, j, 0:1])
+
         def scale_up(j, cut=False):
             g, t = divmod(j, PACK)
             if cut or g < 2:
                 for m in cuts[g]:
-                    nc.scalar.activation(u[g, m.start][:, t, :], squares[j][:, m], ACT.Identity, bias=1.0, scale=coef_t[:, j, 0:1])
+                    scale_part(j, m)
             else:
                 nc.scalar.activation(u[g, None][:, t, :], squares[j][:], ACT.Identity, bias=1.0, scale=coef_t[:, j, 0:1])
 
@@ -257,8 +259,10 @@ def tile_list_claim_charting_kernel(
         def round_w2(g, c):
             nc.scalar.copy(woven(rounded[g, c]), planar(w2_raw[g, c]))
 
-        def round_beside(g, c):
-            nc.gpsimd.tensor_scalar(rounded[g, c].rearrange("p c (s l) -> p c s l", l=2), w2_raw[g, c].rearrange("p s l c -> p c s l"), 1.0, 0.0, ALU.mult, ALU.add)
+        def round_beside(room, raw):
+            nc.gpsimd.tensor_scalar(
+                room[:].rearrange("p i c (s l) -> p (i c) s l", l=2), raw.rearrange("p s l c -> p c s l"), 1.0, 0.0, ALU.mult, ALU.add
+            )
 
         w2_mx = {}
 
@@ -290,71 +294,79 @@ def tile_list_claim_charting_kernel(
         order_w4(nc.vector.tensor_copy, 2, 0, PACK)
         for j in range(1, 5):
             empty_tile(j)
-        sums = tile([P, (PACK + 1) * P1], F32, "sums", "stage0")[:].rearrange("p (s c) -> p s c", c=P1)
-        quarters = sums.rearrange("p s (l c) -> p s l c", l=2)
-        for c, rows_at in enumerate((quarters[:, 2:4], quarters[:, 0::4])):
-            rows = w2[:K_PASS, c * PIECE : (c + 1) * PIECE].rearrange("(q t i) n -> t q i n", t=PACK, i=8)
+        sums = tile([P, (PACK + 2) * P1], F32, "sums", "stage0")[:].rearrange("p (s c) -> p s c", c=P1)
+        first_raw = sums[:, 2:4, :].rearrange("p s (l c) -> p s l c", l=2)
+        next_raw = sums.rearrange("p (s l) c -> p s l c", l=2)[:, 0::2]
+        for raw, cols in ((first_raw, slice(0, PIECE)), (next_raw, slice(PIECE, N))):
+            rows = w2[:K_PASS, cols].rearrange("(q t i) n -> t q i n", t=PACK, i=8)
             for t in range(PACK):
-                nc.sync.dma_start(rows_at[:, t // 2, t % 2, :], rows[t])
-            w2_raw[0, c] = rows_at
-        x[0] = sums[:, 1:, :]
-        x[1] = sums[:, :PACK, :]
-        x[2] = tile([P, PACK, P1], F32, "last_sums")[:]
-        pick(0)
-        pair(0)
-        rooms = {}
-        for c, j in enumerate((1, 3)):
-            rooms[0, c] = make_room([(0, c)], f"room{j - 1}")
-            round_beside(0, c)
+                nc.sync.dma_start(raw[:, t // 2, t % 2, :], rows[t])
+        x[0] = sums[:, 2:, :]
+        x[1] = sums[:, 1 : PACK + 1, :]
+        first_room = make_room([(0, 0)], "room0")
+        round_beside(first_room, first_raw)
+        for j in (0, 1):
             pick(j)
-            pick(j + 1)
+        for j in (0, 1):
             pair(j)
-            pair(j + 1)
+        next_room = make_room([(0, 1), (0, 2)], "room1")
+        round_beside(next_room, next_raw)
+        picked_next = tile([P, 3, P1], F32, "picked_next")
+        for j in (2, 3, 4):
+            pick(j, picked_next[:, j - 2, :])
+        for j in (2, 3, 4):
+            pair(j)
         with nc.allow_non_contiguous_dma(reason="one coefficient for each partition and row tile"):
             for j in range(ROW_TILES):
                 nc.sync.dma_start(coef_t[:, j, 0:1], coef_rows[j // PACK, j % PACK])
-        load_w2(0, 2, 3, "stage1")
-        load_w2(1, 0, 3, "early")
-        load_w2(2, 0, 3, "h0")
-        square(0)
-        empty_half(5, 0)
-        scale_up(0)
-        empty_half(5, 1)
-        square(1)
-        square(2)
-        scale_up(1)
-        scale_up(2)
+        load_w2(1, 0, 3, "w2_pass1")
+        load_w2(2, 0, 3, "stage1")
+        for j in (0, 1):
+            square(j)
+            empty_half(5, j)
+            scale_up(j)
         empty_tile(6)
-        square(3, cut=True)
-        scale_up(3)
-        whole_z = {g: shared[g][:, (2 + g) * P1 :].bitcast(BF16).rearrange("p (c t) -> p c t", t=PACK) for g in range(2)}
+        empty_half(7, 0)
+        first, beside = cuts[0]
+        square(2, cut=True)
+        scale_part(2, first)
+        square(3, "chain0", True)
+        scale_part(3, first)
+        for j in (2, 3):
+            scale_part(j, beside)
+        empty_half(7, 1)
+        whole_z = {g: shared[g][:, 3 * P1 :].bitcast(BF16).rearrange("p (c t) -> p c t", t=PACK) for g in range(2)}
         whole_z[2] = tile([P, P1, PACK], BF16, "z2")[:]
         for g in whole_z:
             for m in cuts[g]:
                 z[g, m.start] = whole_z[g][:, m, :]
         multiply(nc.vector, 0, cuts[0][0])
         multiply(nc.gpsimd, 0, cuts[0][1])
-        empty_tile(7)
         empty_tile(8)
-        square(4)
+        square(4, "chain0")
         empty_half(9, 0)
         scale_up(4)
         empty_half(9, 1)
         empty_tile(10)
-        pick(5, slots[0][:, 0, :])
-        pick(6, slots[0][:, 1, :])
-        pick(7, x[2][:, 0, :])
+        for j in range(5, 8):
+            pick(j, slots[0][:, j - 5, :])
         pick(8)
         for j in range(5, 8):
             pair(j)
         quantise_z(0, 0, P1, whole_z[0])
+        x[2] = tile([P, PACK, P1], F32, "last_sums", "u0")[:]
         pair(8)
+        first, beside = cuts[1]
+        square(5)
         empty_half(11, 0)
-        last_bank = first_product(11, 1)
-        for j in range(5, 8):
-            square(j, "chain" if j == 5 else "same", True)
-            scale_up(j, True)
-        empty(11, last_bank, BANK, S)
+        square(6)
+        for j in (5, 6):
+            scale_part(j, first)
+        square(7, "chain", True)
+        scale_part(7, first)
+        for j in (5, 6, 7):
+            scale_part(j, beside)
+        empty_half(11, 1)
         multiply(nc.vector, 1, cuts[1][0])
         multiply(nc.gpsimd, 1, cuts[1][1])
         early = [(1, 0), (2, 0), (1, 1), (2, 1)]
@@ -371,21 +383,20 @@ def tile_list_claim_charting_kernel(
         for j in range(9, ROW_TILES):
             square(j, "sq9" if j == 9 else "same", True)
             scale_up(j, True)
-        late = [(0, 2), (1, 2), (2, 2)]
+        late = [(1, 2), (2, 2)]
         late_room = make_room(late, "late_room")
         for g, c in late:
             round_w2(g, c)
         quantise_z(1, 0, P1, whole_z[1])
         quantise_w2(early[0:2], early_room[:, 0:2], "h11")
-        quantise_w2([(0, 0)], rooms[0, 0][:], "h10")
+        quantise_w2([(0, 0)], first_room[:], "h10")
         for m in halves:
             multiply(nc.vector, 2, m)
         for m in halves:
             quantise_z(2, m.start, m.stop, z[2, m.start])
-        quantise_w2([(0, 1)], rooms[0, 1][:], "last_sums")
+        quantise_w2([(0, 1), (0, 2)], next_room[:], "u0")
         quantise_w2(early[2:4], early_room[:, 2:4], "z2")
         quantise_w2(late[0:2], late_room[:, 0:2])
-        quantise_w2(late[2:3], late_room[:, 2:3])
 
         acc = [psum.tile([P, P1], F32, name=f"acc{n}", tag=f"bank{n}") for n in range(N_TILES)]
 
@@ -410,7 +421,7 @@ def tile_list_claim_charting_kernel(
             nc.scalar.activation(y[n][:], acc[n][:], ACT.Copy)
 
         def finish(n):
-            least = tile([P, P2], F32, f"least{n}", ("picked1", "picked3", "picked4", "picked8", "u0", "u1")[n])
+            least = tile([P, P2], F32, f"least{n}", ("picked0", "chain0", "h7", "picked8", "h8", "u1")[n])
             nc.vector.tensor_tensor(least[:], rivals[n][:, 0, :], rivals[n][:, 1, :], ALU.min)
             nc.sync.dma_start(out[n * P : (n + 1) * P, :], least[:])
 

@@ -41,7 +41,7 @@ def tile_list_claim_charting_kernel(
         reuse = ctx.enter_context(tc.tile_pool(name="reuse", bufs=1))
         psum = ctx.enter_context(tc.psum_pool(name="psum", bufs=1))
 
-        places = {"early_room": 0, "chain": 7680, "sq8": 9472, "sq9": 11264, "late_room": 12800, "room1": 17408, "picked1": 20480, "picked_next": 21504, "early": 27648, "room0": 27648, "w2_pass1": 29696}
+        places = {"early_room": 0, "chain": 7680, "sq8": 9472, "sq9": 11264, "late_room": 12800, "room1": 17408, "picked1": 19456, "picked0": 21504, "picked_next": 21504, "early": 27648, "room0": 27648, "w2_pass1": 29696}
 
         def tile(shape, dtype, name, tag=None):
             if (tag or name) in places:
@@ -223,11 +223,15 @@ def tile_list_claim_charting_kernel(
             for m in cuts[g] if cut else [whole]:
                 nc.scalar.activation(squares[j][:, m], x[g][:, t, m], ACT.Square)
 
-        shared = [tile([P, (PACK + 1) * P1], F32, f"shared{g}") for g in range(2)]
-        slots = [held[:].rearrange("p (s c) -> p s c", c=P1) for held in shared]
+        shared, slots, z_at = [], [], []
         for g in range(2):
             first, beside = cuts[g]
-            u[g, first.start] = slots[g][:, :PACK, : P1 - first.start]
+            width = P1 - first.start
+            rows_at = P1 - width // 2
+            z_at.append(max(3 * P1, rows_at + 3 * P1 + width - 2 * beside.stop))
+            shared.append(tile([P, z_at[g] + 2 * P1], F32, f"shared{g}"))
+            slots.append(shared[g][:, : 3 * P1].rearrange("p (s c) -> p s c", c=P1))
+            u[g, first.start] = shared[g][:, rows_at : rows_at + PACK * P1].rearrange("p (t c) -> p t c", c=P1)[:, :, :width]
             u[g, 0] = tile([P, PACK, beside.stop], F32, f"u{g}")[:]
         u[2, None] = tile([P, PACK, P1], F32, "u2", "v_w0_0")[:]
         for m in halves:
@@ -282,6 +286,15 @@ def tile_list_claim_charting_kernel(
         def multiply(engine, g, m):
             engine.tensor_tensor(woven(z[g, m.start]), planar(u[g, m.start]), planar(x[g][:, :, m]), ALU.mult)
 
+        def multiply_first(g):
+            m = cuts[g][0]
+            width = (m.stop - m.start) // 2
+            for c in (0, width):
+                part = slice(c, c + width)
+                nc.vector.tensor_tensor(
+                    woven(z[g, m.start][:, part, :]), planar(u[g, m.start][:, :, part]), planar(x[g][:, :, m][:, :, part]), ALU.mult
+                )
+
         def quantise_z(g, c0, c1, woven_z):
             nc.vector.quantize_mx(
                 out=z_codes[g][:, c0:c1].bitcast(FP8X4), scales=z_plane[g][:, c0:c1], in_=woven_z.rearrange("p c t -> p (c t)")
@@ -335,12 +348,12 @@ def tile_list_claim_charting_kernel(
         for j in (2, 3):
             scale_part(j, beside)
         empty_half(7, 1)
-        whole_z = {g: shared[g][:, 3 * P1 :].bitcast(BF16).rearrange("p (c t) -> p c t", t=PACK) for g in range(2)}
+        whole_z = {g: shared[g][:, z_at[g] :].bitcast(BF16).rearrange("p (c t) -> p c t", t=PACK) for g in range(2)}
         whole_z[2] = tile([P, P1, PACK], BF16, "z2")[:]
         for g in whole_z:
             for m in cuts[g]:
                 z[g, m.start] = whole_z[g][:, m, :]
-        multiply(nc.vector, 0, cuts[0][0])
+        multiply_first(0)
         multiply(nc.gpsimd, 0, cuts[0][1])
         empty_tile(8)
         square(4, "chain0")
@@ -367,7 +380,7 @@ def tile_list_claim_charting_kernel(
         for j in (5, 6, 7):
             scale_part(j, beside)
         empty_half(11, 1)
-        multiply(nc.vector, 1, cuts[1][0])
+        multiply_first(1)
         multiply(nc.gpsimd, 1, cuts[1][1])
         early = [(1, 0), (2, 0), (1, 1), (2, 1)]
         early_room = make_room(early, "early_room")
@@ -413,26 +426,26 @@ def tile_list_claim_charting_kernel(
                     stop=(g == G_PASSES - 1),
                 )
 
-        y, rivals = {}, {}
+        rivals = [tile([P, N_TILES * P2], F32, f"rivals{i}", tag) for i, tag in enumerate(("picked_next", "stage0"))]
+        least = tile([P, N_TILES * P2], F32, "least", "shared0")
+        lag = P2 // 2
 
-        def empty_second(n):
-            second_product(n)
-            y[n] = tile([P, P1], F32, f"y{n}", f"h{1 + n}")
-            nc.scalar.activation(y[n][:], acc[n][:], ACT.Copy)
+        def finish(c0, c1):
+            nc.vector.tensor_tensor(least[:, c0:c1], rivals[0][:, c0:c1], rivals[1][:, c0:c1], ALU.min)
 
-        def finish(n):
-            least = tile([P, P2], F32, f"least{n}", ("picked0", "chain0", "h7", "picked8", "h8", "u1")[n])
-            nc.vector.tensor_tensor(least[:], rivals[n][:, 0, :], rivals[n][:, 1, :], ALU.min)
-            nc.sync.dma_start(out[n * P : (n + 1) * P, :], least[:])
-
-        def pick_rivals(n):
-            rivals[n] = ring.tile([P, 2, P2], F32, name=f"rivals{n}", tag="rivals", bufs=3, align_bytes=64)
-            nc.vector.tensor_copy(rivals[n][:, 0, :], y[n][:].indirect(pos3_t[:]))
-            if n:
-                finish(n - 1)
-            nc.vector.tensor_copy(rivals[n][:, 1, :], y[n][:].indirect(pos4_t[:]))
+        def store(n):
+            nc.sync.dma_start(out[n * P : (n + 1) * P, :], least[:, n * P2 : (n + 1) * P2])
 
         for n in range(N_TILES):
-            empty_second(n)
-            pick_rivals(n)
-        finish(N_TILES - 1)
+            second_product(n)
+            y = tile([P, P1], F32, f"y{n}", f"h{1 + n}")
+            nc.scalar.activation(y[:], acc[n][:], ACT.Copy)
+            c = n * P2
+            nc.vector.tensor_copy(rivals[0][:, c : c + P2], y[:].indirect(pos3_t[:]))
+            for part in (0, lag):
+                nc.vector.tensor_copy(rivals[1][:, c + part : c + part + lag], y[:].indirect(pos4_t[:, part // 16 : (part + lag) // 16]))
+            finish(max(c - lag, 0), c + lag)
+            if n:
+                store(n - 1)
+        finish(N_TILES * P2 - lag, N_TILES * P2)
+        store(N_TILES - 1)

@@ -29,6 +29,7 @@ BANKS = 8
 PIECE = 256
 LEAD = 256
 SHARES = (352, 256)
+BESIDE = 3
 
 
 def tile_list_claim_charting_kernel(
@@ -426,26 +427,35 @@ def tile_list_claim_charting_kernel(
                     stop=(g == G_PASSES - 1),
                 )
 
-        rivals = [tile([P, N_TILES * P2], F32, f"rivals{i}", tag) for i, tag in enumerate(("picked_next", "stage0"))]
-        least = tile([P, N_TILES * P2], F32, "least", "shared0")
-        lag = P2 // 2
+        first_of = tile([P, N_TILES, P2], F32, "first_of", "picked_next")
+        second_of = tile([P, N_TILES, P2], F32, "second_of", "stage0")
+        least = tile([P, N_TILES, P2], F32, "least", "shared0")
 
-        def finish(c0, c1):
-            nc.vector.tensor_tensor(least[:, c0:c1], rivals[0][:, c0:c1], rivals[1][:, c0:c1], ALU.min)
+        def store(n, src):
+            nc.sync.dma_start(out[n * P : (n + 1) * P, :], src)
 
-        def store(n):
-            nc.sync.dma_start(out[n * P : (n + 1) * P, :], least[:, n * P2 : (n + 1) * P2])
+        y = []
+
+        def second_look(n):
+            window = y[n][:].indirect(pos4_t[:])
+            if n < BESIDE:
+                nc.vector.tensor_tensor(second_of[:, n, :], window, first_of[:, n, :], ALU.subtract)
+                nc.scalar.activation(least[:, BESIDE + n, :], second_of[:, n, :], ACT.Relu, scale=-1.0)
+            else:
+                nc.vector.tensor_copy(second_of[:, n, :], window)
 
         for n in range(N_TILES):
             second_product(n)
-            y = tile([P, P1], F32, f"y{n}", f"h{1 + n}")
-            nc.scalar.activation(y[:], acc[n][:], ACT.Copy)
-            c = n * P2
-            nc.vector.tensor_copy(rivals[0][:, c : c + P2], y[:].indirect(pos3_t[:]))
-            for part in (0, lag):
-                nc.vector.tensor_copy(rivals[1][:, c + part : c + part + lag], y[:].indirect(pos4_t[:, part // 16 : (part + lag) // 16]))
-            finish(max(c - lag, 0), c + lag)
+            y.append(tile([P, P1], F32, f"y{n}", f"h{1 + n}"))
+            nc.scalar.activation(y[n][:], acc[n][:], ACT.Copy)
+            nc.vector.tensor_copy(first_of[:, n, :], y[n][:].indirect(pos3_t[:]))
             if n:
-                store(n - 1)
-        finish(N_TILES * P2 - lag, N_TILES * P2)
-        store(N_TILES - 1)
+                second_look(n - 1)
+        second_look(N_TILES - 1)
+        nc.gpsimd.tensor_tensor(least[:, :BESIDE, :], first_of[:, :BESIDE, :], least[:, BESIDE:, :], ALU.subtract)
+        for n in range(BESIDE):
+            store(n, least[:, n, :])
+        for n0, n1 in ((BESIDE, N_TILES - 1), (N_TILES - 1, N_TILES)):
+            nc.vector.tensor_tensor(least[:, n0:n1, :], first_of[:, n0:n1, :], second_of[:, n0:n1, :], ALU.min)
+            for n in range(n0, n1):
+                store(n, least[:, n, :])

@@ -30,6 +30,7 @@ PIECE = 256
 LEAD = 256
 SHARES = (352, 256)
 BESIDE = 3
+TAIL = 64
 
 
 def tile_list_claim_charting_kernel(
@@ -42,7 +43,7 @@ def tile_list_claim_charting_kernel(
         reuse = ctx.enter_context(tc.tile_pool(name="reuse", bufs=1))
         psum = ctx.enter_context(tc.psum_pool(name="psum", bufs=1))
 
-        places = {"early_room": 0, "chain": 7680, "sq8": 9472, "sq9": 11264, "late_room": 12800, "room1": 17408, "picked1": 19456, "picked0": 21504, "picked_next": 21504, "early": 27648, "room0": 27648, "w2_pass1": 29696}
+        places = {"early_room": 0, "chain": 7680, "sq8": 9472, "sq9": 11264, "late_room": 12800, "room1": 17408, "picked0": 20480, "picked_next": 21504, "early": 27648, "room0": 27648, "w2_pass1": 29696}
 
         def tile(shape, dtype, name, tag=None):
             if (tag or name) in places:
@@ -102,8 +103,9 @@ def tile_list_claim_charting_kernel(
 
         w2_raw = {}
 
-        def load_w2(g, c0, c1, tag):
-            raw = tile([P, PACK, (c1 - c0) * PIECE], F32, f"w2_raw{g}_{c0}", tag)
+        def load_w2(g, c0, c1, tag, raw=None):
+            if raw is None:
+                raw = tile([P, PACK, (c1 - c0) * PIECE], F32, f"w2_raw{g}_{c0}", tag)
             rows = w2[K_PASS * g : K_PASS * (g + 1), c0 * PIECE : c1 * PIECE].rearrange("(q t i) n -> t q i n", t=PACK, i=8)
             for t in range(PACK):
                 nc.sync.dma_start(raw[:, t, :], rows[t])
@@ -266,7 +268,7 @@ def tile_list_claim_charting_kernel(
 
         def round_beside(room, raw):
             nc.gpsimd.tensor_scalar(
-                room[:].rearrange("p i c (s l) -> p (i c) s l", l=2), raw.rearrange("p s l c -> p c s l"), 1.0, 0.0, ALU.mult, ALU.add
+                room[:].rearrange("p i c (s l) -> p (i c) s l", l=2)[:, : raw.shape[-1]], raw.rearrange("p s l c -> p c s l"), 1.0, 0.0, ALU.mult, ALU.add
             )
 
         w2_mx = {}
@@ -310,8 +312,8 @@ def tile_list_claim_charting_kernel(
             empty_tile(j)
         sums = tile([P, (PACK + 2) * P1], F32, "sums", "stage0")[:].rearrange("p (s c) -> p s c", c=P1)
         first_raw = sums[:, 2:4, :].rearrange("p s (l c) -> p s l c", l=2)
-        next_raw = sums.rearrange("p (s l) c -> p s l c", l=2)[:, 0::2]
-        for raw, cols in ((first_raw, slice(0, PIECE)), (next_raw, slice(PIECE, N))):
+        next_raw = sums.rearrange("p (s l) c -> p s l c", l=2)[:, 0::2, :, : N - PIECE - P]
+        for raw, cols in ((first_raw, slice(0, PIECE)), (next_raw, slice(PIECE, N - P))):
             rows = w2[:K_PASS, cols].rearrange("(q t i) n -> t q i n", t=PACK, i=8)
             for t in range(PACK):
                 nc.sync.dma_start(raw[:, t // 2, t % 2, :], rows[t])
@@ -333,7 +335,12 @@ def tile_list_claim_charting_kernel(
         with nc.allow_non_contiguous_dma(reason="one coefficient for each partition and row tile"):
             for j in range(ROW_TILES):
                 nc.sync.dma_start(coef_t[:, j, 0:1], coef_rows[j // PACK, j % PACK])
-        load_w2(1, 0, 3, "w2_pass1")
+        both = tile([P, PACK * (N + P)], F32, "w2_pass1")
+        single_raw = both[:, PACK * N :].rearrange("p (t c) -> p t c", t=PACK)
+        rows = w2[:K_PASS, N - P :].rearrange("(q t i) n -> t q i n", t=PACK, i=8)
+        for t in range(PACK):
+            nc.sync.dma_start(single_raw[:, t, :], rows[t])
+        load_w2(1, 0, 3, None, both[:, : PACK * N].rearrange("p (t c) -> p t c", t=PACK))
         load_w2(2, 0, 3, "stage1")
         for j in (0, 1):
             square(j)
@@ -362,6 +369,7 @@ def tile_list_claim_charting_kernel(
         scale_up(4)
         empty_half(9, 1)
         empty_tile(10)
+        nc.scalar.copy(woven(next_room[:, 1, P:, :]), planar(single_raw))
         for j in range(5, 8):
             pick(j, slots[0][:, j - 5, :])
         pick(8)
@@ -451,11 +459,16 @@ def tile_list_claim_charting_kernel(
             nc.vector.tensor_copy(first_of[:, n, :], y[n][:].indirect(pos3_t[:]))
             if n:
                 second_look(n - 1)
-        second_look(N_TILES - 1)
+        last, cut = N_TILES - 1, P2 - TAIL
+        nc.vector.tensor_copy(second_of[:, last, :cut], y[last][:].indirect(pos4_t[:, : cut // 16]))
         nc.gpsimd.tensor_tensor(least[:, :BESIDE, :], first_of[:, :BESIDE, :], least[:, BESIDE:, :], ALU.subtract)
         for n in range(BESIDE):
             store(n, least[:, n, :])
-        for n0, n1 in ((BESIDE, N_TILES - 1), (N_TILES - 1, N_TILES)):
-            nc.vector.tensor_tensor(least[:, n0:n1, :], first_of[:, n0:n1, :], second_of[:, n0:n1, :], ALU.min)
-            for n in range(n0, n1):
-                store(n, least[:, n, :])
+        for n in range(BESIDE, last):
+            nc.vector.tensor_tensor(least[:, n, :], first_of[:, n, :], second_of[:, n, :], ALU.min)
+            store(n, least[:, n, :])
+        end = second_of[:, BESIDE, :TAIL]
+        nc.vector.tensor_copy(end, y[last][:].indirect(pos4_t[:, cut // 16 :]))
+        for cols, second in ((slice(0, cut), second_of[:, last, :cut]), (slice(cut, P2), end)):
+            nc.vector.tensor_tensor(least[:, last, cols], first_of[:, last, cols], second, ALU.min)
+            nc.sync.dma_start(out[last * P :, cols], least[:, last, cols])

@@ -77,12 +77,12 @@ def tile_list_claim_charting_kernel(
             return [raw[:, :, (g - g0) * K_PASS // 2 : (g - g0 + 1) * K_PASS // 2] for g in range(g0, g1)]
 
         load_tab(0)
-        w4_raw = load_w4(0, 1, "w4_first")
         pos1_t = load_list(pos1, "pos1_t")
         pos2_t = load_list(pos2, "pos2_t")
         pos3_t = load_list(pos3, "pos3_t")
         pos4_t = load_list(pos4, "pos4_t")
         load_tab(1)
+        w4_raw = load_w4(0, 1, "w4_first")
         rows_together = tile([P, S + H], U8, "rows_together", "together")
         for dst, rows in ((rows_together, slice(0, 32)), (planes[0], slice(0, 4))):
             nc.scalar.copy(

from contextlib import ExitStack

import concourse.mybir as mybir

T, S, P1, P2, K, H, N = 2048, 1024, 512, 256, 1024, 1536, 768
FLOPS = 2 * K * H * S + 2 * H * N * P1

F32 = mybir.dt.float32
BF16 = mybir.dt.bfloat16
I32 = mybir.dt.int32
U32 = mybir.dt.uint32
U16 = mybir.dt.uint16
U8 = mybir.dt.uint8
FP8X4 = mybir.dt.float8_e4m3fn_x4
FP4X4 = mybir.dt.float4_e2m1fn_x4
ACT = mybir.ActivationFunctionType
ALU = mybir.AluOpType

P = 128
PACK = 4
K_PASS = P * PACK
A_PASSES = K // K_PASS
G_PASSES = H // K_PASS
ROW_TILES = G_PASSES * PACK
BANK = 512
HALVES = S // BANK
N_TILES = N // P
BANKS = 8
PIECE = 256
LEAD = 256
SHARES = (352, 256)
BESIDE = 3
TAIL = 64


def tile_list_claim_charting_kernel(
    tc, tab_words, tab_scales, offs, pos1, pos2, pos3, pos4, w4_words, w4_scales, coef, w2, out
):
    nc = tc.nc
    with ExitStack() as ctx:
        keep = ctx.enter_context(tc.tile_pool(name="keep", bufs=1))
        ring = ctx.enter_context(tc.tile_pool(name="ring", bufs=2))
        reuse = ctx.enter_context(tc.tile_pool(name="reuse", bufs=1))
        psum = ctx.enter_context(tc.psum_pool(name="psum", bufs=1))

        places = {"early_room": 0, "chain": 7680, "sq8": 9472, "sq9": 11264, "late_room": 12800, "room1": 17408, "picked0": 20480, "picked_next": 21504, "early": 27648, "room0": 27648, "w2_pass1": 29696}

        def tile(shape, dtype, name, tag=None):
            if (tag or name) in places:
                return reuse.tile(shape, dtype, name=name, align_bytes=64, offset=places[tag or name])
            return keep.tile(shape, dtype, name=name, tag=tag or name, align_bytes=64)

        def load_list(src, name):
            held = keep.tile(list(src.shape), U16, name=name)
            nc.sync.dma_start(held[:], src)
            return held

        tab_plane = tile([P, T], U8, "tab_plane")
        nc.vector.memset(tab_plane[32:64, :].bitcast(I32), 0)
        nc.vector.memset(tab_plane[64:P, :].bitcast(I32), 0)
        planes = [tile([P, S + H], U8, f"plane{a}") for a in range(A_PASSES)]
        v_planes = [plane[:, :S] for plane in planes]

        offs_t = load_list(offs, "offs_t")
        nc.sync.dma_start(tab_plane[0:32, :].bitcast(I32), tab_scales.rearrange("a q t -> (a q) t").bitcast(I32))
        w4_rows = tile([P, H], U8, "w4_rows")
        nc.sync.dma_start(w4_rows[0:32, :].bitcast(I32), w4_scales.rearrange("a q c -> (a q) c").bitcast(I32))
        tab_w = [tile([P, T], I32, f"tab_w{a}", f"stage{a}") for a in range(A_PASSES)]

        def load_tab(a):
            nc.sync.dma_start(tab_w[a][:], tab_words[a].rearrange("p t i -> p (t i)").bitcast(I32))

        def load_w4(g0, g1, tag):
            raw = tile([P, A_PASSES, (g1 - g0) * K_PASS // 2], I32, f"w4_raw{g0}", tag)
            cols = slice(2 * K_PASS * g0, 2 * K_PASS * g1)
            nc.sync.dma_start(raw[:], w4_words[:, :, cols].rearrange("a p c -> p a c").bitcast(I32))
            return [raw[:, :, (g - g0) * K_PASS // 2 : (g - g0 + 1) * K_PASS // 2] for g in range(g0, g1)]

        load_tab(0)
        pos1_t = load_list(pos1, "pos1_t")
        pos2_t = load_list(pos2, "pos2_t")
        pos3_t = load_list(pos3, "pos3_t")
        pos4_t = load_list(pos4, "pos4_t")
        load_tab(1)
        w4_raw = load_w4(0, 1, "w4_first")
        rows_together = tile([P, S + H], U8, "rows_together", "together")
        for dst, rows in ((rows_together, slice(0, 32)), (planes[0], slice(0, 4))):
            nc.scalar.copy(
                dst[rows, S:].bitcast(U32).rearrange("p (g t q w) -> p g t q w", g=G_PASSES, t=PACK, w=2),
                w4_rows[rows, :].bitcast(U32).rearrange("p (g q t w) -> p g t q w", g=G_PASSES, t=PACK, w=2),
            )

        v_rows = tile([P, S], U8, "v_rows", "early")
        nc.vector.tensor_copy(v_rows[:], tab_plane[:].indirect(offs_t[:]))
        v_first = tile([P, S], U32, "v_w0_0")
        nc.vector.tensor_copy(v_first[:, :LEAD], tab_w[0][:].bitcast(U32).indirect(offs_t[:, : LEAD // 16]))
        nc.vector.tensor_copy(rows_together[0:32, :S].bitcast(I32), v_rows[0:32, :].bitcast(I32))
        for a in range(A_PASSES):
            for q in range(4):
                row = 16 * a + 4 * q
                if row:
                    nc.sync.dma_start(planes[a][32 * q : 32 * q + 4, :].bitcast(I32), rows_together[row : row + 4, :].bitcast(I32))

        w2_raw = {}

        def load_w2(g, c0, c1, tag, raw=None):
            if raw is None:
                raw = tile([P, PACK, (c1 - c0) * PIECE], F32, f"w2_raw{g}_{c0}", tag)
            rows = w2[K_PASS * g : K_PASS * (g + 1), c0 * PIECE : c1 * PIECE].rearrange("(q t i) n -> t q i n", t=PACK, i=8)
            for t in range(PACK):
                nc.sync.dma_start(raw[:, t, :], rows[t])
            for c in range(c0, c1):
                w2_raw[g, c] = raw[:, :, (c - c0) * PIECE : (c - c0 + 1) * PIECE]

        v_w = {}

        def gather_words(a, half0, half1, step):
            words = tile([P, (half1 - half0) * BANK], U32, f"v_w{a}_{half0}")
            for c in range(0, (half1 - half0) * BANK, step):
                end = min(c + step, (half1 - half0) * BANK)
                cols = slice((half0 * BANK + c) // 16, (half0 * BANK + end) // 16)
                nc.vector.tensor_copy(words[:, c:end], tab_w[a][:].bitcast(U32).indirect(offs_t[:, cols]))
            for half in range(half0, half1):
                v_w[a, half] = words[:, (half - half0) * BANK : (half - half0 + 1) * BANK]

        w4_codes = {}

        def order_w4(engine, g, t0, t1, tag=None):
            n = t1 - t0
            codes = tile([P, A_PASSES, n, 2 * P], U8, f"w4_codes{g}_{t0}", tag)
            engine(
                codes[:].rearrange("p a t c -> p (a t c)").bitcast(U32 if g == 0 else I32).rearrange("p (a t q w) -> p a t q w", a=A_PASSES, t=n, w=4),
                (w4_raw[g].bitcast(U32) if g == 0 else w4_raw[g]).rearrange("p a (q t w) -> p a t q w", t=PACK, w=4)[:, :, t0:t1],
            )
            for t in range(t0, t1):
                w4_codes[g * PACK + t] = codes[:, :, t - t0, :]

        nc.vector.tensor_copy(planes[0][0:4, :S].bitcast(I32), v_rows[0:4, :].bitcast(I32))
        w4_raw.extend(load_w4(1, G_PASSES, "early"))
        nc.vector.tensor_copy(v_first[:, LEAD:], tab_w[0][:].bitcast(U32).indirect(offs_t[:, LEAD // 16 :]))
        for half in range(HALVES):
            v_w[0, half] = v_first[:, half * BANK : (half + 1) * BANK]
        order_w4(nc.scalar.copy, 0, 0, 1)
        gather_words(1, 0, 1, BANK)
        gather_words(1, 1, 2, BANK - P)
        order_w4(nc.scalar.copy, 0, 1, PACK, "together")
        coef_t = tile([P, ROW_TILES, 8], F32, "coef_t", "w4_first")
        coef_rows = coef.rearrange("(g q t i o) -> g t q i o", g=G_PASSES, t=PACK, i=8, o=1)

        banks = []

        def next_bank(shape, name):
            banks.append(psum.tile(shape, F32, name=name, tag=f"bank{len(banks) % BANKS}"))
            return banks[-1]

        h = [tile([P, S], F32, f"h{j}") for j in range(ROW_TILES)]

        def first_product(j, half):
            codes, rows = w4_codes[j], slice(S + j * P, S + (j + 1) * P)
            cols = slice(half * BANK, (half + 1) * BANK)
            bank = next_bank([P, BANK], f"hb{j}_{half}")
            for a in range(A_PASSES):
                nc.tensor.matmul_mx(
                    out=bank[:],
                    lhsT=codes[:, a, :].bitcast(FP4X4),
                    lhsT_scale=planes[a][:, rows],
                    rhs=v_w[a, half].bitcast(FP8X4),
                    rhs_scale=v_planes[a][:, cols],
                    start=(a == 0),
                    stop=(a == A_PASSES - 1),
                )
            return bank

        def narrow_product(j, c0, c1):
            codes, rows = w4_codes[j], slice(S + j * P, S + (j + 1) * P)
            bank = next_bank([P, c1 - c0], f"hb{j}_{c0}")
            for a in range(A_PASSES):
                for c in range(c0, c1, P):
                    nc.tensor.matmul_mx(
                        out=bank[:, c - c0 : c - c0 + P],
                        lhsT=codes[:, a, :].bitcast(FP4X4),
                        lhsT_scale=planes[a][:, rows],
                        rhs=v_w[a, c // BANK][:, c % BANK : c % BANK + P].bitcast(FP8X4),
                        rhs_scale=v_planes[a][:, c : c + P],
                        start=(a == 0 and c == c0),
                        stop=(a == A_PASSES - 1 and c + P == c1),
                    )
            nc.scalar.activation(h[j][:, c0:c1], bank[:], ACT.Copy)

        def empty(j, bank, c0, c1):
            nc.scalar.activation(h[j][:, c0:c1], bank[:, c0 % BANK : (c1 - 1) % BANK + 1], ACT.Copy)

        def empty_tile(j):
            for half in range(HALVES):
                empty(j, first_product(j, half), half * BANK, (half + 1) * BANK)

        def woven(view):
            return view.rearrange("p (c i) t -> p c t i", i=4)

        def planar(view):
            return view.rearrange("p t (c i) -> p c t i", i=4)

        picked, x, u = {}, {}, {}

        def pick(j, into=None):
            picked[j] = tile([P, P1], F32, f"picked{j}")[:] if into is None else into
            nc.vector.tensor_copy(picked[j], h[j][:].indirect(pos1_t[:]))

        def pair(j):
            g, t = divmod(j, PACK)
            nc.vector.tensor_tensor(x[g][:, t, :], h[j][:].indirect(pos2_t[:]), picked[j], ALU.add)

        squares = {}
        halves = [slice(0, P1 // 2), slice(P1 // 2, P1)]
        whole = slice(0, P1)
        cuts = [[slice(share, P1), slice(0, share)] for share in SHARES] + [halves]

        def square(j, tag=None, cut=False):
            g, t = divmod(j, PACK)
            if tag == "same":
                squares[j] = squares[j - 1]
            elif tag:
                squares[j] = tile([P, P1], F32, f"sq{j}", tag)
            else:
                squares[j] = ring.tile([P, P1], F32, name=f"sq{j}", tag="sq")
            for m in cuts[g] if cut else [whole]:
                nc.scalar.activation(squares[j][:, m], x[g][:, t, m], ACT.Square)

        shared, slots, z_at = [], [], []
        for g in range(2):
            first, beside = cuts[g]
            width = P1 - first.start
            rows_at = P1 - width // 2
            z_at.append(max(3 * P1, rows_at + 3 * P1 + width - 2 * beside.stop))
            shared.append(tile([P, z_at[g] + 2 * P1], F32, f"shared{g}"))
            slots.append(shared[g][:, : 3 * P1].rearrange("p (s c) -> p s c", c=P1))
            u[g, first.start] = shared[g][:, rows_at : rows_at + PACK * P1].rearrange("p (t c) -> p t c", c=P1)[:, :, :width]
            u[g, 0] = tile([P, PACK, beside.stop], F32, f"u{g}")[:]
        u[2, None] = tile([P, PACK, P1], F32, "u2", "v_w0_0")[:]
        for m in halves:
            u[2, m.start] = u[2, None][:, :, m]

        def scale_part(j, m):
            g, t = divmod(j, PACK)
            nc.scalar.activation(u[g, m.start][:, t, :], squares[j][:, m], ACT.Identity, bias=1.0, scale=coef_t[:, j, 0:1])

        def scale_up(j, cut=False):
            g, t = divmod(j, PACK)
            if cut or g < 2:
                for m in cuts[g]:
                    scale_part(j, m)
            else:
                nc.scalar.activation(u[g, None][:, t, :], squares[j][:], ACT.Identity, bias=1.0, scale=coef_t[:, j, 0:1])

        def empty_half(j, half):
            empty(j, first_product(j, half), half * BANK, (half + 1) * BANK)

        rounded = {}

        def make_room(some, tag):
            room = tile([P, len(some), PIECE, PACK], BF16, f"w2_woven_{tag}", tag)
            for i, piece in enumerate(some):
                rounded[piece] = room[:, i]
            return room

        def round_w2(g, c):
            nc.scalar.copy(woven(rounded[g, c]), planar(w2_raw[g, c]))

        def round_beside(room, raw):
            nc.gpsimd.tensor_scalar(
                room[:].rearrange("p i c (s l) -> p (i c) s l", l=2)[:, : raw.shape[-1]], raw.rearrange("p s l c -> p c s l"), 1.0, 0.0, ALU.mult, ALU.add
            )

        w2_mx = {}

        def quantise_w2(some, room, tag=None):
            codes = tile([P, len(some) * PIECE], U32, f"w2_codes{some[0]}", tag)
            plane = tile([P, len(some) * PIECE], U8, f"w2_plane{some[0]}")
            nc.vector.quantize_mx(out=codes[:].bitcast(FP8X4), scales=plane[:], in_=room.rearrange("p i c t -> p (i c t)"))
            for i, (g, c) in enumerate(some):
                for n in range(PIECE // P):
                    cols = slice(i * PIECE + n * P, i * PIECE + (n + 1) * P)
                    w2_mx[g, c * PIECE // P + n] = (codes[:, cols], plane[:, cols])

        z = {}
        z_codes = [tile([P, P1], U32, f"z_codes{g}") for g in range(G_PASSES)]
        z_plane = [tile([P, P1], U8, f"z_plane{g}") for g in range(G_PASSES)]

        def multiply(engine, g, m):
            engine.tensor_tensor(woven(z[g, m.start]), planar(u[g, m.start]), planar(x[g][:, :, m]), ALU.mult)

        def multiply_first(g):
            m = cuts[g][0]
            width = (m.stop - m.start) // 2
            for c in (0, width):
                part = slice(c, c + width)
                nc.vector.tensor_tensor(
                    woven(z[g, m.start][:, part, :]), planar(u[g, m.start][:, :, part]), planar(x[g][:, :, m][:, :, part]), ALU.mult
                )

        def quantise_z(g, c0, c1, woven_z):
            nc.vector.quantize_mx(
                out=z_codes[g][:, c0:c1].bitcast(FP8X4), scales=z_plane[g][:, c0:c1], in_=woven_z.rearrange("p c t -> p (c t)")
            )

        empty_half(0, 0)
        narrow_product(0, BANK, S - P)
        narrow_product(0, S - P, S)
        order_w4(nc.vector.tensor_copy, 1, 0, PACK)
        order_w4(nc.vector.tensor_copy, 2, 0, PACK)
        for j in range(1, 5):
            empty_tile(j)
        sums = tile([P, (PACK + 2) * P1], F32, "sums", "stage0")[:].rearrange("p (s c) -> p s c", c=P1)
        first_raw = sums[:, 2:4, :].rearrange("p s (l c) -> p s l c", l=2)
        next_raw = sums.rearrange("p (s l) c -> p s l c", l=2)[:, 0::2, :, : N - PIECE - P]
        for raw, cols in ((first_raw, slice(0, PIECE)), (next_raw, slice(PIECE, N - P))):
            rows = w2[:K_PASS, cols].rearrange("(q t i) n -> t q i n", t=PACK, i=8)
            for t in range(PACK):
                nc.sync.dma_start(raw[:, t // 2, t % 2, :], rows[t])
        x[0] = sums[:, 2:, :]
        x[1] = sums[:, 1 : PACK + 1, :]
        first_room = make_room([(0, 0)], "room0")
        round_beside(first_room, first_raw)
        for j in (0, 1):
            pick(j)
        for j in (0, 1):
            pair(j)
        next_room = make_room([(0, 1), (0, 2)], "room1")
        round_beside(next_room, next_raw)
        picked_next = tile([P, 3, P1], F32, "picked_next")
        for j in (2, 3, 4):
            pick(j, picked_next[:, j - 2, :])
        for j in (2, 3, 4):
            pair(j)
        with nc.allow_non_contiguous_dma(reason="one coefficient for each partition and row tile"):
            for j in range(ROW_TILES):
                nc.sync.dma_start(coef_t[:, j, 0:1], coef_rows[j // PACK, j % PACK])
        both = tile([P, PACK * (N + P)], F32, "w2_pass1")
        single_raw = both[:, PACK * N :].rearrange("p (t c) -> p t c", t=PACK)
        rows = w2[:K_PASS, N - P :].rearrange("(q t i) n -> t q i n", t=PACK, i=8)
        for t in range(PACK):
            nc.sync.dma_start(single_raw[:, t, :], rows[t])
        load_w2(1, 0, 3, None, both[:, : PACK * N].rearrange("p (t c) -> p t c", t=PACK))
        load_w2(2, 0, 3, "stage1")
        for j in (0, 1):
            square(j)
            empty_half(5, j)
            scale_up(j)
        empty_tile(6)
        empty_half(7, 0)
        first, beside = cuts[0]
        square(2, cut=True)
        scale_part(2, first)
        square(3, "chain0", True)
        scale_part(3, first)
        for j in (2, 3):
            scale_part(j, beside)
        empty_half(7, 1)
        whole_z = {g: shared[g][:, z_at[g] :].bitcast(BF16).rearrange("p (c t) -> p c t", t=PACK) for g in range(2)}
        whole_z[2] = tile([P, P1, PACK], BF16, "z2")[:]
        for g in whole_z:
            for m in cuts[g]:
                z[g, m.start] = whole_z[g][:, m, :]
        multiply_first(0)
        multiply(nc.gpsimd, 0, cuts[0][1])
        empty_tile(8)
        square(4, "chain0")
        empty_half(9, 0)
        scale_up(4)
        empty_half(9, 1)
        empty_tile(10)
        nc.scalar.copy(woven(next_room[:, 1, P:, :]), planar(single_raw))
        for j in range(5, 8):
            pick(j, slots[0][:, j - 5, :])
        pick(8)
        for j in range(5, 8):
            pair(j)
        quantise_z(0, 0, P1, whole_z[0])
        x[2] = tile([P, PACK, P1], F32, "last_sums", "u0")[:]
        pair(8)
        first, beside = cuts[1]
        square(5)
        empty_half(11, 0)
        square(6)
        for j in (5, 6):
            scale_part(j, first)
        square(7, "chain", True)
        scale_part(7, first)
        for j in (5, 6, 7):
            scale_part(j, beside)
        empty_half(11, 1)
        multiply_first(1)
        multiply(nc.gpsimd, 1, cuts[1][1])
        early = [(1, 0), (2, 0), (1, 1), (2, 1)]
        early_room = make_room(early, "early_room")
        square(8, "sq8")
        round_w2(*early[0])
        scale_up(8)
        for j in range(9, ROW_TILES):
            pick(j, slots[1][:, j - 9, :])
        for g, c in early[1:]:
            round_w2(g, c)
        for j in range(9, ROW_TILES):
            pair(j)
        for j in range(9, ROW_TILES):
            square(j, "sq9" if j == 9 else "same", True)
            scale_up(j, True)
        late = [(1, 2), (2, 2)]
        late_room = make_room(late, "late_room")
        for g, c in late:
            round_w2(g, c)
        quantise_z(1, 0, P1, whole_z[1])
        quantise_w2(early[0:2], early_room[:, 0:2], "h11")
        quantise_w2([(0, 0)], first_room[:], "h10")
        for m in halves:
            multiply(nc.vector, 2, m)
        for m in halves:
            quantise_z(2, m.start, m.stop, z[2, m.start])
        quantise_w2([(0, 1), (0, 2)], next_room[:], "u0")
        quantise_w2(early[2:4], early_room[:, 2:4], "z2")
        quantise_w2(late[0:2], late_room[:, 0:2])

        acc = [psum.tile([P, P1], F32, name=f"acc{n}", tag=f"bank{n}") for n in range(N_TILES)]

        def second_product(n):
            for g in range(G_PASSES):
                codes, plane = w2_mx[g, n]
                nc.tensor.matmul_mx(
                    out=acc[n][:],
                    lhsT=codes.bitcast(FP8X4),
                    lhsT_scale=plane,
                    rhs=z_codes[g][:].bitcast(FP8X4),
                    rhs_scale=z_plane[g][:],
                    start=(g == 0),
                    stop=(g == G_PASSES - 1),
                )

        first_of = tile([P, N_TILES, P2], F32, "first_of", "picked_next")
        second_of = tile([P, N_TILES, P2], F32, "second_of", "stage0")
        least = tile([P, N_TILES, P2], F32, "least", "shared0")

        def store(n, src):
            nc.sync.dma_start(out[n * P : (n + 1) * P, :], src)

        y = []

        def second_look(n):
            window = y[n][:].indirect(pos4_t[:])
            if n < BESIDE:
                nc.vector.tensor_tensor(second_of[:, n, :], window, first_of[:, n, :], ALU.subtract)
                nc.scalar.activation(least[:, BESIDE + n, :], second_of[:, n, :], ACT.Relu, scale=-1.0)
            else:
                nc.vector.tensor_copy(second_of[:, n, :], window)

        for n in range(N_TILES):
            second_product(n)
            y.append(tile([P, P1], F32, f"y{n}", f"h{1 + n}"))
            nc.scalar.activation(y[n][:], acc[n][:], ACT.Copy)
            nc.vector.tensor_copy(first_of[:, n, :], y[n][:].indirect(pos3_t[:]))
            if n:
                second_look(n - 1)
        last, cut = N_TILES - 1, P2 - TAIL
        nc.vector.tensor_copy(second_of[:, last, :cut], y[last][:].indirect(pos4_t[:, : cut // 16]))
        nc.gpsimd.tensor_tensor(least[:, :BESIDE, :], first_of[:, :BESIDE, :], least[:, BESIDE:, :], ALU.subtract)
        for n in range(BESIDE):
            store(n, least[:, n, :])
        for n in range(BESIDE, last):
            nc.vector.tensor_tensor(least[:, n, :], first_of[:, n, :], second_of[:, n, :], ALU.min)
            store(n, least[:, n, :])
        end = second_of[:, BESIDE, :TAIL]
        nc.vector.tensor_copy(end, y[last][:].indirect(pos4_t[:, cut // 16 :]))
        for cols, second in ((slice(0, cut), second_of[:, last, :cut]), (slice(cut, P2), end)):
            nc.vector.tensor_tensor(least[:, last, cols], first_of[:, last, cols], second, ALU.min)
            nc.sync.dma_start(out[last * P :, cols], least[:, last, cols])
